import numpy as np
import ml_dtypes


def mxq(x, axis, fmt="e4m3"):
    dtype, down = {"e4m3": (ml_dtypes.float8_e4m3fn, 7), "e5m2": (ml_dtypes.float8_e5m2, 14)}[fmt]
    v = np.moveaxis(np.asarray(x, np.float32).astype(ml_dtypes.bfloat16).astype(np.float64), axis, -1)
    blocks = v.reshape(v.shape[:-1] + (-1, 32))
    amax = np.abs(blocks).max(-1, keepdims=True)
    byte = np.maximum(np.where(amax > 0, np.frexp(amax)[1] - 1 + 127, 0) - down, 1)
    scale = np.exp2(byte - 127.0)
    codes = (blocks / scale).astype(np.float32).astype(dtype).astype(np.float64)
    return np.moveaxis((codes * scale).reshape(v.shape), -1, axis)


WIDE = False


def mx_kscale(k):
    if not WIDE:
        return np.ones(k)
    levels = np.array([10, -10, 5, -5, 0])
    if k % 512:
        return np.exp2(np.random.permutation(np.resize(levels, k // 32))).repeat(32)
    a = np.empty((k // 512, 16))
    for p in range(k // 512):
        a[p, :8] = np.random.permutation(np.resize(levels, 8))
        for g in range(8):
            far = levels[np.abs(levels - a[p, g]) >= 10]
            a[p, g + 8] = far[np.random.randint(len(far))]
    return np.exp2(a.ravel()).repeat(32)


def f64(x):
    return np.asarray(x).astype(np.float64)


def striped(idx):
    return np.tile(idx.reshape(-1, 16).T, (8, 1)).astype(np.uint16)


def unstriped(offs):
    return offs[:16].T.reshape(-1).astype(np.int64)


E2M1 = np.array([0.0, 0.5, 1.0, 1.5, 2.0, 3.0, 4.0, 6.0, -0.0, -0.5, -1.0, -1.5, -2.0, -3.0, -4.0, -6.0])


def pack_weight(w, fmt):
    k, n = w.shape
    w = f64(np.asarray(w, np.float32).astype(ml_dtypes.bfloat16)).reshape(k // 32, 32, n)
    amax = np.abs(w).max(1)
    if fmt == "e4m3":
        byte = np.frexp(amax)[1] - 1 + 127 - 7
    else:
        mant, ex = np.frexp(amax / 6.0)
        byte = np.where(mant > 0.5, ex, ex - 1) + 127
    byte = np.clip(np.where(amax > 0, byte, 1), 1, 254)
    scaled = (w * np.exp2(127.0 - byte)[:, None, :]).reshape(k, n).astype(np.float32)
    by_word = np.ascontiguousarray(scaled.reshape(k // 512, 128, 4, n).transpose(0, 1, 3, 2))
    if fmt == "e4m3":
        words = by_word.astype(ml_dtypes.float8_e4m3fn).view(np.uint8)
    else:
        c = by_word.astype(ml_dtypes.float4_e2m1fn).view(np.uint8) & 0xF
        words = (c[..., 0::2] | (c[..., 1::2] << 4)).reshape(k // 512, 128, 2 * n)
    return np.ascontiguousarray(words), np.ascontiguousarray(byte.astype(np.uint8).reshape(k // 512, 16, n))


def unpack_weight(words, scales, fmt):
    g, _, n = scales.shape
    words = np.ascontiguousarray(words).reshape(g, 128, n, -1)
    if fmt == "e4m3":
        vals = words.view(ml_dtypes.float8_e4m3fn).astype(np.float64)
    else:
        nib = np.empty((g, 128, n, 4), np.uint8)
        nib[..., 0::2] = words & 0xF
        nib[..., 1::2] = words >> 4
        vals = E2M1[nib]
    vals = vals * np.repeat(np.exp2(scales.astype(np.float64) - 127.0), 8, axis=1)[..., None]
    return vals.transpose(0, 1, 3, 2).reshape(g * 512, n)


def gelu(v):
    return 0.5 * v * (1.0 + np.tanh(np.sqrt(2.0 / np.pi) * (v + 0.044715 * v**3)))


def bf(x):
    return np.asarray(x, np.float32).astype(ml_dtypes.bfloat16)


def planes(Y):
    n, m = Y.shape
    b = f64(bf(Y)).reshape(n // 32, 32, m)
    amax = np.abs(b).max(1)
    byte = np.clip(np.where(amax > 0, np.frexp(amax)[1] - 1 + 127 - 7, 1), 1, 254)
    codes = (b * np.exp2(127.0 - byte)[:, None, :]).reshape(n, m).astype(np.float32).astype(ml_dtypes.float8_e4m3fn).view(np.uint8)
    words = codes.reshape(n // 512, 128, 4, m).transpose(0, 1, 3, 2)
    return np.ascontiguousarray(words), np.ascontiguousarray(byte.astype(np.uint8).reshape(n // 512, 16, m))


K, K2, H, H2, N, T, S, T2 = 1024, 512, 512, 1024, 1024, 2048, 1024, 2048

def setup_inputs():
    n = np.random.standard_normal
    s, s2, u = mx_kscale(K)[:, None], mx_kscale(K2)[:, None], mx_kscale(H)[:, None]
    tab_words, tab_scales = pack_weight(n((K, T)) * s, "e4m3")
    tab2_words, tab2_scales = pack_weight(n((K2, T)) * s2, "e4m3")
    w2_words, w2_scales = pack_weight(n((K, H)) * 0.3 / np.sqrt(K) / s, "e2m1")
    w3_words, w3_scales = pack_weight(n((K2, H2)) * 0.5 / np.sqrt(K2) / s2, "e4m3")
    w1 = n((K, H)) * 0.5 / np.sqrt(K) / s
    w4 = n((H, N)) * np.exp(0.8 * n((1, N))) / np.sqrt(H) / u
    gain = np.exp(0.3 * n(H)) * u[:, 0]
    perm = np.random.permutation(T2)
    return {"tab_words": tab_words, "tab_scales": tab_scales,
            "tab2_words": tab2_words, "tab2_scales": tab2_scales,
            "w1": w1.astype(np.float32),
            "w2_words": w2_words, "w2_scales": w2_scales,
            "w3_words": w3_words, "w3_scales": w3_scales,
            "w4": w4.astype(np.float32),
            "gain": gain.astype(np.float32),
            "wg1": np.exp(0.3 * n((128, S))).astype(np.float32),
            "wg2": np.exp(0.3 * n((128, S))).astype(np.float32),
            "offs": striped(np.random.permutation(T)[:S]),
            "offs2": striped(np.random.permutation(T)[:S]),
            "offs3": striped(perm[:S]), "offs4": striped(perm[S:])}

def reference(tab_words, tab_scales, tab2_words, tab2_scales, w1, w2_words, w2_scales,
              w3_words, w3_scales, w4, gain, wg1, wg2, offs, offs2, offs3, offs4):
    v = unpack_weight(tab_words, tab_scales, "e4m3")[:, unstriped(offs)]
    v2 = unpack_weight(tab2_words, tab2_scales, "e4m3")[:, unstriped(offs2)]
    phase = mxq(f64(w1), 0, "e4m3").T @ v
    level = unpack_weight(w2_words, w2_scales, "e2m1").T @ v
    h1 = np.sin(phase) * np.exp(level)
    cs = np.cos(unpack_weight(w3_words, w3_scales, "e4m3").T @ v2)
    h2 = cs[:H] + cs[H:]
    page = np.zeros((H, T2))
    page[:, unstriped(offs3)] = np.tile(f64(wg1), (H // 128, 1)) * h1
    page[:, unstriped(offs4)] = np.tile(f64(wg2), (H // 128, 1)) * h2
    z = page * f64(gain)[:, None]
    y = mxq(f64(w4), 0, "e4m3").T @ mxq(z, 0, "e4m3")
    words, scales = planes(y)
    return y, words, scales

@@ -1,0 +1,317 @@
+from contextlib import ExitStack
+
+import concourse.mybir as mybir
+from concourse.masks import make_identity
+
+K, K2, H, N, T, S, T2 = 1024, 512, 512, 1024, 2048, 1024, 2048
+FLOPS = 2 * (2 * K * H * S + K2 * 2 * H * S + H * N * T2)
+
+F32 = mybir.dt.float32
+BF16 = mybir.dt.bfloat16
+I32 = mybir.dt.int32
+U32 = mybir.dt.uint32
+U16 = mybir.dt.uint16
+U8 = mybir.dt.uint8
+FP8X4 = mybir.dt.float8_e4m3fn_x4
+FP4X4 = mybir.dt.float4_e2m1fn_x4
+ACT = mybir.ActivationFunctionType
+MULT = mybir.AluOpType.mult
+
+P = 128
+PACK = 4
+K_PASS = P * PACK
+BANK = 512
+QUADS = 4
+H2_SLICE = 256
+H1_SLICE = 512
+OUT_CHUNKS = (128, 128, 256, 512, 512, 512)
+
+
+def tile_list_ocean_band_weave_kernel(
+    tc, tab_words, tab_scales, tab2_words, tab2_scales, w1, w2_words, w2_scales, w3_words, w3_scales,
+    w4, gain, wg1, wg2, offs, offs2, offs3, offs4, out_0, out_1, out_2,
+):
+    nc = tc.nc
+    with ExitStack() as ctx:
+        keep = ctx.enter_context(tc.tile_pool(name="keep", bufs=1))
+        ring = ctx.enter_context(tc.tile_pool(name="ring", bufs=1))
+        psum = ctx.enter_context(tc.psum_pool(name="psum", bufs=1))
+
+        def held(shape, dtype, name):
+            return keep.tile(shape, dtype, name=name, align_bytes=64)
+
+        def rotating(shape, dtype, tag, bufs):
+            return ring.tile(shape, dtype, name=tag, tag=tag, bufs=bufs, align_bytes=64)
+
+        def bank(tag):
+            return psum.tile([P, BANK], F32, name=tag, tag=tag, bufs=4)
+
+        def load_list(src, name):
+            tile = keep.tile([P, S // 16], U16, name=name)
+            nc.sync.dma_start(tile[:], src)
+            return tile
+
+        def load_words(queue, src, name):
+            tile = held([P, src.shape[1]], U32, name)
+            queue.dma_start(tile[:].bitcast(I32), src.rearrange("p c i -> p (c i)").bitcast(I32))
+            return tile
+
+        def load_plane(queue, rows, name):
+            width = rows.shape[1]
+            tile = held([P, width], U8, name)
+            words = rows.bitcast(I32)
+            for q in range(QUADS):
+                queue.dma_start(
+                    tile[32 * q : 32 * q + 32, :].bitcast(I32),
+                    words[4 * q : 4 * q + 4, :].unsqueeze(0).to_broadcast([8, 4, width // 4]),
+                )
+            return tile
+
+        def load_spread(tile, wg, j0):
+            width = tile.shape[2]
+            rows = wg.rearrange("(q t) j -> q t j", t=PACK)[:, :, j0 : j0 + width]
+            for u in (0, 2, 1, 3):
+                nc.sync.dma_start(tile[32 * u : 32 * u + 32, :, :], rows)
+
+        def load_block(rows):
+            raw = rotating([P, PACK, BANK], F32, "wide", 4)
+            nc.sync.dma_start(raw[:], rows.rearrange("(p j) c -> p j c", j=PACK))
+            return raw
+
+        def quantize_block(raw, codes, scales):
+            dealt = rotating([P, BANK * PACK], BF16, "rounded", 4)
+            src = raw[:].rearrange("p j (m t) -> p m t j", t=PACK)
+            dst = dealt[:].rearrange("p (t m j) -> p m t j", t=PACK, j=PACK)
+            for m0 in (0, P // 2):
+                nc.scalar.copy(out=dst[:, m0 : m0 + P // 2], in_=src[:, m0 : m0 + P // 2])
+            nc.vector.quantize_mx(out=codes.bitcast(FP8X4), scales=scales, in_=dealt[:])
+
+        def interleave(planes, width):
+            woven = rotating([P, width * PACK], BF16, "rounded", 4)
+            nc.vector.tensor_copy(
+                out=woven[:].rearrange("p (c i t) -> p c t i", i=4, t=PACK),
+                in_=planes.rearrange("p t (c i) -> p c t i", i=4),
+            )
+            return woven
+
+        list2 = load_list(offs2, "list2")
+        tab2_s = load_plane(nc.sync, tab2_scales[0], "tab2_s")
+        tab2_w = load_words(nc.sync, tab2_words[0], "tab2_w")
+        w3_w = load_words(nc.sync, w3_words[0], "w3_w")
+        w3_s = load_plane(nc.gpsimd, w3_scales[0], "w3_s")
+        list1 = load_list(offs, "list1")
+
+        tab_s = held([P, T], U8, "tab_s")
+        nc.gpsimd.memset(tab_s[:].bitcast(I32), 0)
+        for q in range(QUADS):
+            nc.sync.dma_start(
+                tab_s[32 * q : 32 * q + 8, :].bitcast(I32), tab_scales.bitcast(I32)[:, 4 * q : 4 * q + 4, :]
+            )
+        gain_sb = held([P, PACK], F32, "gain_sb")
+        nc.sync.dma_start(gain_sb[:], gain.rearrange("(p t) -> p t", t=PACK))
+        list4 = load_list(offs4, "list4")
+        tab_w = [load_words(nc.sync, tab_words[0], "tab_w0")]
+        wg2_sb = [rotating([P, PACK, H2_SLICE], F32, "quarter", 4) for s in range(S // H2_SLICE)]
+        load_spread(wg2_sb[0], wg2, 0)
+        tab_w.append(load_words(nc.sync, tab_words[1], "tab_w1"))
+        load_spread(wg2_sb[1], wg2, H2_SLICE)
+        w1_raw = [load_block(w1[a * K_PASS : (a + 1) * K_PASS, :]) for a in range(K // K_PASS)]
+        for s in range(2, S // H2_SLICE):
+            load_spread(wg2_sb[s], wg2, s * H2_SLICE)
+        w2_w = held([P, K // K_PASS, 2 * H], U8, "w2_w")
+        nc.sync.dma_start(w2_w[:].bitcast(I32), w2_words.bitcast(I32).rearrange("a p c -> p a c"))
+        w2_s = held([P, K // K_PASS, H], U8, "w2_s")
+        nc.gpsimd.memset(w2_s[:].bitcast(I32), 0)
+        for q in range(QUADS):
+            nc.sync.dma_start(
+                w2_s[32 * q : 32 * q + 4, :, :].bitcast(I32),
+                w2_scales.bitcast(I32)[:, 4 * q : 4 * q + 4, :].rearrange("a r c -> r a c"),
+            )
+        list3 = load_list(offs3, "list3")
+        wg1_sb = [rotating([P, PACK, H1_SLICE], F32, "wide", 4) for s in range(S // H1_SLICE)]
+        for s in range(S // H1_SLICE):
+            load_spread(wg1_sb[s], wg1, s * H1_SLICE)
+        w4_raw = [load_block(w4[:, g * BANK : (g + 1) * BANK]) for g in range(N // BANK)]
+
+        ident = held([P, P], F32, "ident")
+        make_identity(nc, ident[:])
+        gain_m2 = held([P, PACK], F32, "gain_m2")
+        gain_p2 = held([P, PACK], F32, "gain_p2")
+        nc.gpsimd.tensor_scalar(out=gain_m2[:], in0=gain_sb[:], scalar1=-2.0, scalar2=None, op0=MULT)
+        nc.gpsimd.tensor_scalar(out=gain_p2[:], in0=gain_sb[:], scalar1=2.0, scalar2=None, op0=MULT)
+
+        v2_s = held([P, S], U8, "v2_s")
+        v2_w = held([P, S], U32, "v2_w")
+        nc.vector.tensor_copy(v2_s[:], tab2_s[:].indirect(list2[:]))
+        for h in range(2):
+            nc.vector.tensor_copy(
+                v2_w[:, h * 512 : (h + 1) * 512], tab2_w[:].indirect(list2[:, h * 32 : (h + 1) * 32])
+            )
+        v_s0 = held([P, S], U8, "v_s0")
+        nc.vector.tensor_copy(v_s0[:], tab_s[:].indirect(list1[:]))
+        v_s1 = held([P, S], U8, "v_s1")
+        nc.gpsimd.memset(v_s1[:].bitcast(I32), 0)
+        nc.gpsimd.dma_start(v_s1[0 : P - 4, :].bitcast(I32), v_s0[4:P, :].bitcast(I32))
+        v_s = [v_s0, v_s1]
+        v_w = []
+        for a in range(K // K_PASS):
+            v_w.append(held([P, S], U32, "v_w%d" % a))
+            nc.vector.tensor_copy(v_w[a][:], tab_w[a][:].indirect(list1[:]))
+
+        pages = [held([P, T2], F32, "page%d" % t) for t in range(PACK)]
+
+        w1_w = held([P, K // K_PASS, H], U32, "w1_w")
+        w1_s = held([P, K // K_PASS, H], U8, "w1_s")
+        per_bank = BANK // H2_SLICE
+        for s in range(S // H2_SLICE):
+            sums = [bank("turn") for b in range(PACK // per_bank)]
+            for jj in range(H2_SLICE // P):
+                cols = slice(s * H2_SLICE + jj * P, s * H2_SLICE + (jj + 1) * P)
+                half_sin = rotating([P, 2 * H], F32, "turned", 3)
+                for c in range(2):
+                    arg = bank("prod")
+                    nc.tensor.matmul_mx(
+                        out=arg[:], lhsT=v2_w[:, cols].bitcast(FP8X4), lhsT_scale=v2_s[:, cols],
+                        rhs=w3_w[:, c * H : (c + 1) * H].bitcast(FP8X4), rhs_scale=w3_s[:, c * H : (c + 1) * H],
+                        start=True, stop=True,
+                    )
+                    nc.scalar.activation(
+                        out=half_sin[:, c * H : (c + 1) * H].rearrange("p (t m) -> p t m", t=PACK),
+                        in_=arg[:].rearrange("p (m t) -> p t m", t=PACK), func=ACT.Sin, scale=0.5,
+                    )
+                nc.scalar.activation(out=half_sin[:], in_=half_sin[:], func=ACT.Square)
+                for t in range(PACK):
+                    at = (t % per_bank) * H2_SLICE + jj * P
+                    for c in range(2):
+                        nc.tensor.matmul(
+                            sums[t // per_bank][:, at : at + P],
+                            half_sin[:, c * H + t * P : c * H + (t + 1) * P], ident[:],
+                            is_transpose=True, start=(c == 0), stop=(c == 1),
+                        )
+            h2 = rotating([P, PACK, H2_SLICE], F32, "placed", 3)
+            for t in range(PACK):
+                at = (t % per_bank) * H2_SLICE
+                nc.scalar.activation(
+                    out=h2[:, t, :], in_=sums[t // per_bank][:, at : at + H2_SLICE], func=ACT.Identity,
+                    scale=gain_m2[:, t : t + 1], bias=gain_p2[:, t : t + 1],
+                )
+            picks = list4[:, s * H2_SLICE // 16 : (s + 1) * H2_SLICE // 16]
+            for t in range(PACK):
+                nc.vector.tensor_tensor(pages[t][:].indirect(picks), h2[:, t, :], wg2_sb[s][:, t, :], MULT)
+            if 1 <= s <= K // K_PASS:
+                quantize_block(w1_raw[s - 1], w1_w[:, s - 1, :], w1_s[:, s - 1, :])
+
+        sines = {}
+        for s in range(S // H1_SLICE):
+            cols = slice(s * H1_SLICE, (s + 1) * H1_SLICE)
+            for t in range(PACK):
+                phase = bank("prod")
+                for a in range(K // K_PASS):
+                    nc.tensor.matmul_mx(
+                        out=phase[:], lhsT=w1_w[:, a, t * P : (t + 1) * P].bitcast(FP8X4),
+                        lhsT_scale=w1_s[:, a, t * P : (t + 1) * P],
+                        rhs=v_w[a][:, cols].bitcast(FP8X4), rhs_scale=v_s[a][:, cols],
+                        start=(a == 0), stop=(a == K // K_PASS - 1),
+                    )
+                sines[s, t] = held([P, H1_SLICE], F32, "sine%d_%d" % (s, t))
+                nc.scalar.activation(out=sines[s, t][:], in_=phase[:], func=ACT.Sin)
+
+        w4_w = held([P, N], U32, "w4_w")
+        w4_s = held([P, N], U8, "w4_s")
+        groups = [rotating([P, PACK, BANK], BF16, "quarter", 4) for c in range(T2 // BANK)]
+        for s in range(S // H1_SLICE):
+            exps = [bank("turn") for t in range(PACK)]
+            for jp in range(H1_SLICE // (2 * P)):
+                turned = rotating([P, 2 * H], F32, "turned", 3)
+                for e in range(2):
+                    jj = 2 * jp + e
+                    cols = slice(s * H1_SLICE + jj * P, s * H1_SLICE + (jj + 1) * P)
+                    level = bank("prod")
+                    for a in range(K // K_PASS):
+                        nc.tensor.matmul_mx(
+                            out=level[:], lhsT=v_w[a][:, cols].bitcast(FP8X4), lhsT_scale=v_s[a][:, cols],
+                            rhs=w2_w[:, a, :].bitcast(FP4X4), rhs_scale=w2_s[:, a, :],
+                            start=(a == 0), stop=(a == K // K_PASS - 1),
+                        )
+                    nc.scalar.activation(
+                        out=turned[:, e * H : (e + 1) * H].rearrange("p (t m) -> p t m", t=PACK),
+                        in_=level[:].rearrange("p (m t) -> p t m", t=PACK), func=ACT.Exp,
+                    )
+                    for t in range(PACK):
+                        nc.tensor.transpose(
+                            exps[t][:, jj * P : (jj + 1) * P], turned[:, e * H + t * P : e * H + (t + 1) * P], ident[:]
+                        )
+            picks = list3[:, s * H1_SLICE // 16 : (s + 1) * H1_SLICE // 16]
+            h1 = []
+            for t in range(PACK + 1):
+                if t < PACK:
+                    h1.append(rotating([P, H1_SLICE], F32, "placed", 3))
+                    nc.vector.scalar_tensor_tensor(
+                        out=h1[t][:], in0=exps[t][:], scalar=gain_sb[:, t : t + 1], in1=sines[s, t][:],
+                        op0=MULT, op1=MULT,
+                    )
+                if t > 0:
+                    nc.vector.tensor_tensor(pages[t - 1][:].indirect(picks), h1[t - 1][:], wg1_sb[s][:, t - 1, :], MULT)
+        for g in range(N // BANK):
+            quantize_block(w4_raw[g], w4_w[:, g * BANK : (g + 1) * BANK], w4_s[:, g * BANK : (g + 1) * BANK])
+
+        for t in range(PACK - 1):
+            for c in range(T2 // BANK):
+                nc.scalar.copy(out=groups[c][:, t, :], in_=pages[t][:, c * BANK : (c + 1) * BANK])
+
+        z_w = held([P, T2], U32, "z_w")
+        z_s = held([P, T2], U8, "z_s")
+        y_s = held([P, T2], U8, "y_s")
+        starts = [sum(OUT_CHUNKS[:c]) for c in range(len(OUT_CHUNKS))]
+
+        def make_z(c):
+            c0, width = starts[c], OUT_CHUNKS[c]
+            planes = groups[c0 // BANK][:, :, c0 % BANK : c0 % BANK + width]
+            nc.scalar.copy(out=planes[:, PACK - 1, :], in_=pages[PACK - 1][:, c0 : c0 + width])
+            woven = interleave(planes, width)
+            nc.vector.quantize_mx(
+                out=z_w[:, c0 : c0 + width].bitcast(FP8X4), scales=z_s[:, c0 : c0 + width], in_=woven[:]
+            )
+
+        def make_y(c, g):
+            c0, width = starts[c], OUT_CHUNKS[c]
+            cols = slice(c0, c0 + width)
+            y = rotating([P, PACK, width], F32, "wide", 4)
+            flat = y[:].rearrange("p t c -> p (t c)")
+            share = BANK // width
+            for b in range(PACK // share):
+                acc = bank(("prod", "turn")[(g + b) % 2])
+                for i in range(share):
+                    at = g * BANK + (b * share + i) * P
+                    nc.tensor.matmul_mx(
+                        out=acc[:, i * width : (i + 1) * width],
+                        lhsT=w4_w[:, at : at + P].bitcast(FP8X4), lhsT_scale=w4_s[:, at : at + P],
+                        rhs=z_w[:, cols].bitcast(FP8X4), rhs_scale=z_s[:, cols], start=True, stop=True,
+                    )
+                nc.scalar.copy(out=flat[:, b * BANK : (b + 1) * BANK], in_=acc[:])
+            nc.sync.dma_start(
+                out_0[g * K_PASS : (g + 1) * K_PASS, cols].rearrange("(p t) c -> p t c", t=PACK), y[:]
+            )
+            return y
+
+        def make_planes(c, g, y):
+            c0, width = starts[c], OUT_CHUNKS[c]
+            cols = slice(c0, c0 + width)
+            woven = interleave(y[:], width)
+            words = rotating([P, width], U32, "words", 4)
+            nc.vector.quantize_mx(out=words[:].bitcast(FP8X4), scales=y_s[4 * g : P, cols], in_=woven[:])
+            nc.sync.dma_start(
+                out_1[g, :, cols, :].rearrange("p m t -> p (m t)").bitcast(I32), words[:].bitcast(I32)
+            )
+
+        make_z(0)
+        for c in range(len(OUT_CHUNKS)):
+            if c + 1 < len(OUT_CHUNKS):
+                make_z(c + 1)
+            ys = [make_y(c, g) for g in range(N // K_PASS)]
+            for g in range(N // K_PASS):
+                make_planes(c, g, ys[g])
+        for q in range(QUADS):
+            (nc.scalar, nc.sync)[q % 2].dma_start(
+                out_2.bitcast(I32)[:, 4 * q : 4 * q + 4, :], y_s[32 * q : 32 * q + 8, :].bitcast(I32)
+            )

@@ -23,8 +23,9 @@ K_PASS = P * PACK
 BANK = 512
 QUADS = 4
 H2_SLICE = 256
-H1_SLICE = 512
-OUT_CHUNKS = (128, 128, 256, 512, 512, 512)
+OUT_CHUNKS = (128, 128, 256, 512, 512, 256, 256)
+PAGES = H // P
+Z_ON_SCALAR = ()
 
 
 def tile_list_ocean_band_weave_kernel(
@@ -51,8 +52,11 @@ def tile_list_ocean_band_weave_kernel(
             nc.sync.dma_start(tile[:], src)
             return tile
 
-        def load_words(queue, src, name):
-            tile = held([P, src.shape[1]], U32, name)
+        def tenant(shape, dtype, tag):
+            return ring.tile(shape, dtype, name=tag, tag=tag, bufs=1, align_bytes=64)
+
+        def load_words(queue, src, tag):
+            tile = tenant([P, src.shape[1]], U32, tag)
             queue.dma_start(tile[:].bitcast(I32), src.rearrange("p c i -> p (c i)").bitcast(I32))
             return tile
 
@@ -67,76 +71,57 @@ def tile_list_ocean_band_weave_kernel(
                 )
             return tile
 
-        def load_spread(tile, wg, j0):
-            width = tile.shape[2]
-            rows = wg.rearrange("(q t) j -> q t j", t=PACK)[:, :, j0 : j0 + width]
-            for u in (0, 2, 1, 3):
-                nc.sync.dma_start(tile[32 * u : 32 * u + 32, :, :], rows)
-
-        def load_block(rows):
-            raw = rotating([P, PACK, BANK], F32, "wide", 4)
+        def load_block(rows, tag):
+            raw = tenant([P, PACK, BANK], F32, tag)
             nc.sync.dma_start(raw[:], rows.rearrange("(p j) c -> p j c", j=PACK))
             return raw
 
-        def quantize_block(raw, codes, scales):
-            dealt = rotating([P, BANK * PACK], BF16, "rounded", 4)
-            src = raw[:].rearrange("p j (m t) -> p m t j", t=PACK)
-            dst = dealt[:].rearrange("p (t m j) -> p m t j", t=PACK, j=PACK)
-            for m0 in (0, P // 2):
-                nc.scalar.copy(out=dst[:, m0 : m0 + P // 2], in_=src[:, m0 : m0 + P // 2])
-            nc.vector.quantize_mx(out=codes.bitcast(FP8X4), scales=scales, in_=dealt[:])
-
-        def interleave(planes, width):
-            woven = rotating([P, width * PACK], BF16, "rounded", 4)
-            nc.vector.tensor_copy(
-                out=woven[:].rearrange("p (c i t) -> p c t i", i=4, t=PACK),
-                in_=planes.rearrange("p t (c i) -> p c t i", i=4),
-            )
-            return woven
+        def round_block(src, order):
+            rounded = rotating([P, BANK * PACK], BF16, "rounded", 4)
+            dst = order(rounded[:])
+            half = src.shape[1] // 2
+            for m0 in (0, half):
+                nc.scalar.copy(out=dst[:, m0 : m0 + half], in_=src[:, m0 : m0 + half])
+            return rounded
 
         list2 = load_list(offs2, "list2")
         tab2_s = load_plane(nc.sync, tab2_scales[0], "tab2_s")
-        tab2_w = load_words(nc.sync, tab2_words[0], "tab2_w")
-        w3_w = load_words(nc.sync, w3_words[0], "w3_w")
-        w3_s = load_plane(nc.gpsimd, w3_scales[0], "w3_s")
+        tab2_w = load_words(nc.sync, tab2_words[0], "big2")
         list1 = load_list(offs, "list1")
-
         tab_s = held([P, T], U8, "tab_s")
-        nc.gpsimd.memset(tab_s[:].bitcast(I32), 0)
-        for q in range(QUADS):
-            nc.sync.dma_start(
-                tab_s[32 * q : 32 * q + 8, :].bitcast(I32), tab_scales.bitcast(I32)[:, 4 * q : 4 * q + 4, :]
-            )
-        gain_sb = held([P, PACK], F32, "gain_sb")
-        nc.sync.dma_start(gain_sb[:], gain.rearrange("(p t) -> p t", t=PACK))
+        nc.sync.dma_start(tab_s[0:32, :].bitcast(I32), tab_scales.bitcast(I32).rearrange("a q c -> (a q) c"))
+        nc.vector.memset(tab_s[32:64, :].bitcast(I32), 0)
+        nc.vector.memset(tab_s[64:P, :].bitcast(I32), 0)
+        w3_s = load_plane(nc.sync, w3_scales[0], "w3_s")
+        w3_w = load_words(nc.sync, w3_words[0], "w3_w")
+        tab_w = [load_words(nc.sync, tab_words[a], "big%d" % a) for a in range(K // K_PASS)]
+        gain_sb = held([P, PAGES], F32, "gain_sb")
+        with nc.allow_non_contiguous_dma(reason="one gain value for each partition and page"):
+            nc.scalar.dma_start(gain_sb[:], gain.rearrange("(b p) -> p b", p=P))
         list4 = load_list(offs4, "list4")
-        tab_w = [load_words(nc.sync, tab_words[0], "tab_w0")]
-        wg2_sb = [rotating([P, PACK, H2_SLICE], F32, "quarter", 4) for s in range(S // H2_SLICE)]
-        load_spread(wg2_sb[0], wg2, 0)
-        tab_w.append(load_words(nc.sync, tab_words[1], "tab_w1"))
-        load_spread(wg2_sb[1], wg2, H2_SLICE)
-        w1_raw = [load_block(w1[a * K_PASS : (a + 1) * K_PASS, :]) for a in range(K // K_PASS)]
-        for s in range(2, S // H2_SLICE):
-            load_spread(wg2_sb[s], wg2, s * H2_SLICE)
+        wg2_sb = held([P, S], F32, "wg2_sb")
+        nc.sync.dma_start(wg2_sb[:], wg2)
+        w1_raw = [load_block(w1[a * K_PASS : (a + 1) * K_PASS, :], "raw%d" % a) for a in range(K // K_PASS)]
         w2_w = held([P, K // K_PASS, 2 * H], U8, "w2_w")
         nc.sync.dma_start(w2_w[:].bitcast(I32), w2_words.bitcast(I32).rearrange("a p c -> p a c"))
+        list3 = load_list(offs3, "list3")
+        wg1_sb = held([P, S], F32, "wg1_sb")
+        nc.sync.dma_start(wg1_sb[:], wg1)
+        w4_raw = [load_block(w4[:, g * BANK : (g + 1) * BANK], "raw%d" % (2 + g)) for g in range(N // BANK)]
         w2_s = held([P, K // K_PASS, H], U8, "w2_s")
-        nc.gpsimd.memset(w2_s[:].bitcast(I32), 0)
+        nc.vector.memset(w2_s[:].bitcast(I32), 0)
         for q in range(QUADS):
             nc.sync.dma_start(
                 w2_s[32 * q : 32 * q + 4, :, :].bitcast(I32),
                 w2_scales.bitcast(I32)[:, 4 * q : 4 * q + 4, :].rearrange("a r c -> r a c"),
             )
-        list3 = load_list(offs3, "list3")
-        wg1_sb = [rotating([P, PACK, H1_SLICE], F32, "wide", 4) for s in range(S // H1_SLICE)]
-        for s in range(S // H1_SLICE):
-            load_spread(wg1_sb[s], wg1, s * H1_SLICE)
-        w4_raw = [load_block(w4[:, g * BANK : (g + 1) * BANK]) for g in range(N // BANK)]
+        v_s = held([P, K // K_PASS, S], U8, "v_s")
+        nc.vector.memset(v_s[:].bitcast(I32), 0)
 
         ident = held([P, P], F32, "ident")
         make_identity(nc, ident[:])
-        gain_m2 = held([P, PACK], F32, "gain_m2")
-        gain_p2 = held([P, PACK], F32, "gain_p2")
+        gain_m2 = held([P, PAGES], F32, "gain_m2")
+        gain_p2 = held([P, PAGES], F32, "gain_p2")
         nc.gpsimd.tensor_scalar(out=gain_m2[:], in0=gain_sb[:], scalar1=-2.0, scalar2=None, op0=MULT)
         nc.gpsimd.tensor_scalar(out=gain_p2[:], in0=gain_sb[:], scalar1=2.0, scalar2=None, op0=MULT)
 
@@ -147,140 +132,195 @@ def tile_list_ocean_band_weave_kernel(
             nc.vector.tensor_copy(
                 v2_w[:, h * 512 : (h + 1) * 512], tab2_w[:].indirect(list2[:, h * 32 : (h + 1) * 32])
             )
-        v_s0 = held([P, S], U8, "v_s0")
-        nc.vector.tensor_copy(v_s0[:], tab_s[:].indirect(list1[:]))
-        v_s1 = held([P, S], U8, "v_s1")
-        nc.gpsimd.memset(v_s1[:].bitcast(I32), 0)
-        nc.gpsimd.dma_start(v_s1[0 : P - 4, :].bitcast(I32), v_s0[4:P, :].bitcast(I32))
-        v_s = [v_s0, v_s1]
+        v_rows = held([P, S], U8, "v_rows")
+        nc.vector.tensor_copy(v_rows[:], tab_s[:].indirect(list1[:]))
+        for a in range(K // K_PASS):
+            for q in range(QUADS):
+                nc.sync.dma_start(
+                    v_s[32 * q : 32 * q + 4, a, :].bitcast(I32),
+                    v_rows[16 * a + 4 * q : 16 * a + 4 * q + 4, :].bitcast(I32),
+                )
         v_w = []
         for a in range(K // K_PASS):
             v_w.append(held([P, S], U32, "v_w%d" % a))
             nc.vector.tensor_copy(v_w[a][:], tab_w[a][:].indirect(list1[:]))
 
-        pages = [held([P, T2], F32, "page%d" % t) for t in range(PACK)]
+        pages = [held([P, T2], F32, "page%d" % b) for b in range(PAGES)]
 
         w1_w = held([P, K // K_PASS, H], U32, "w1_w")
         w1_s = held([P, K // K_PASS, H], U8, "w1_s")
         per_bank = BANK // H2_SLICE
-        for s in range(S // H2_SLICE):
-            sums = [bank("turn") for b in range(PACK // per_bank)]
-            for jj in range(H2_SLICE // P):
-                cols = slice(s * H2_SLICE + jj * P, s * H2_SLICE + (jj + 1) * P)
-                half_sin = rotating([P, 2 * H], F32, "turned", 3)
+        tiles_per_slice = H2_SLICE // P
+        sums = {}
+
+        def sines_of_tile(s, jj):
+            cols = slice(s * H2_SLICE + jj * P, s * H2_SLICE + (jj + 1) * P)
+            if s == 2:
+                half_sin = tenant([P, 2 * H], F32, "raw%d" % jj)
+            else:
+                half_sin = rotating([P, 2 * H], F32, "turned", 4)
+            for c in range(2):
+                arg = bank("prod")
+                nc.tensor.matmul_mx(
+                    out=arg[:], lhsT=v2_w[:, cols].bitcast(FP8X4), lhsT_scale=v2_s[:, cols],
+                    rhs=w3_w[:, c * H : (c + 1) * H].bitcast(FP8X4), rhs_scale=w3_s[:, c * H : (c + 1) * H],
+                    start=True, stop=True,
+                )
+                nc.scalar.activation(out=half_sin[:, c * H : (c + 1) * H], in_=arg[:], func=ACT.Sin, scale=0.5)
+            nc.scalar.activation(out=half_sin[:], in_=half_sin[:], func=ACT.Square)
+            if jj == 0:
+                sums[s] = [bank("turn") for b in range(PAGES // per_bank)]
+            for b in range(PAGES):
+                at = (b % per_bank) * H2_SLICE + jj * P
                 for c in range(2):
-                    arg = bank("prod")
-                    nc.tensor.matmul_mx(
-                        out=arg[:], lhsT=v2_w[:, cols].bitcast(FP8X4), lhsT_scale=v2_s[:, cols],
-                        rhs=w3_w[:, c * H : (c + 1) * H].bitcast(FP8X4), rhs_scale=w3_s[:, c * H : (c + 1) * H],
-                        start=True, stop=True,
+                    nc.tensor.matmul(
+                        sums[s][b // per_bank][:, at : at + P],
+                        half_sin[:, c * H + b * P : c * H + (b + 1) * P], ident[:],
+                        is_transpose=True, start=(c == 0), stop=(c == 1),
                     )
-                    nc.scalar.activation(
-                        out=half_sin[:, c * H : (c + 1) * H].rearrange("p (t m) -> p t m", t=PACK),
-                        in_=arg[:].rearrange("p (m t) -> p t m", t=PACK), func=ACT.Sin, scale=0.5,
-                    )
-                nc.scalar.activation(out=half_sin[:], in_=half_sin[:], func=ACT.Square)
-                for t in range(PACK):
-                    at = (t % per_bank) * H2_SLICE + jj * P
-                    for c in range(2):
-                        nc.tensor.matmul(
-                            sums[t // per_bank][:, at : at + P],
-                            half_sin[:, c * H + t * P : c * H + (t + 1) * P], ident[:],
-                            is_transpose=True, start=(c == 0), stop=(c == 1),
-                        )
-            h2 = rotating([P, PACK, H2_SLICE], F32, "placed", 3)
-            for t in range(PACK):
-                at = (t % per_bank) * H2_SLICE
+
+        def place_slice(s):
+            h2 = rotating([P, PAGES, H2_SLICE], F32, "placed", 4)
+            for b in range(PAGES):
+                at = (b % per_bank) * H2_SLICE
                 nc.scalar.activation(
-                    out=h2[:, t, :], in_=sums[t // per_bank][:, at : at + H2_SLICE], func=ACT.Identity,
-                    scale=gain_m2[:, t : t + 1], bias=gain_p2[:, t : t + 1],
+                    out=h2[:, b, :], in_=sums[s][b // per_bank][:, at : at + H2_SLICE], func=ACT.Identity,
+                    scale=gain_m2[:, b : b + 1], bias=gain_p2[:, b : b + 1],
                 )
             picks = list4[:, s * H2_SLICE // 16 : (s + 1) * H2_SLICE // 16]
-            for t in range(PACK):
-                nc.vector.tensor_tensor(pages[t][:].indirect(picks), h2[:, t, :], wg2_sb[s][:, t, :], MULT)
-            if 1 <= s <= K // K_PASS:
-                quantize_block(w1_raw[s - 1], w1_w[:, s - 1, :], w1_s[:, s - 1, :])
+            for b in range(PAGES):
+                nc.vector.tensor_tensor(
+                    pages[b][:].indirect(picks), h2[:, b, :], wg2_sb[:, s * H2_SLICE : (s + 1) * H2_SLICE], MULT
+                )
 
-        sines = {}
-        for s in range(S // H1_SLICE):
-            cols = slice(s * H1_SLICE, (s + 1) * H1_SLICE)
-            for t in range(PACK):
-                phase = bank("prod")
-                for a in range(K // K_PASS):
-                    nc.tensor.matmul_mx(
-                        out=phase[:], lhsT=w1_w[:, a, t * P : (t + 1) * P].bitcast(FP8X4),
-                        lhsT_scale=w1_s[:, a, t * P : (t + 1) * P],
-                        rhs=v_w[a][:, cols].bitcast(FP8X4), rhs_scale=v_s[a][:, cols],
-                        start=(a == 0), stop=(a == K // K_PASS - 1),
+        def quantize_w1(a):
+            rounded = round_block(
+                w1_raw[a][:].rearrange("p j (c i) -> p c j i", i=4),
+                lambda ap: ap.rearrange("p (c i j) -> p c j i", i=4, j=PACK),
+            )
+            nc.vector.quantize_mx(out=w1_w[:, a, :].bitcast(FP8X4), scales=w1_s[:, a, :], in_=rounded[:])
+
+        for s in range(S // H2_SLICE):
+            for jj in range(tiles_per_slice):
+                sines_of_tile(s, jj)
+                if s == 3 and jj == 0:
+                    place_slice(2)
+            if s == 1:
+                quantize_w1(0)
+                place_slice(1)
+                quantize_w1(1)
+            if s == 0:
+                place_slice(0)
+
+        def first_product(words, scales, b, cols):
+            acc = bank("prod")
+            for a in range(K // K_PASS):
+                nc.tensor.matmul_mx(
+                    out=acc[:], lhsT=words(a, b), lhsT_scale=scales[:, a, b * P : (b + 1) * P],
+                    rhs=v_w[a][:, cols].bitcast(FP8X4), rhs_scale=v_s[:, a, cols],
+                    start=(a == 0), stop=(a == K // K_PASS - 1),
+                )
+            return acc
+
+        halves = [slice(h * BANK, (h + 1) * BANK) for h in range(S // BANK)]
+        sines = [tenant([P, 2, S], F32, "sine%d" % i) for i in range(PAGES // 2)]
+        for b in range(PAGES):
+            for cols in halves:
+                phase = first_product(lambda a, b: w1_w[:, a, b * P : (b + 1) * P].bitcast(FP8X4), w1_s, b, cols)
+                nc.scalar.activation(out=sines[b // 2][:, b % 2, cols], in_=phase[:], func=ACT.Sin)
+            if b == 0:
+                place_slice(3)
+
+        exps = []
+        h1 = []
+        for b in range(PAGES):
+            exps.append(tenant([P, S], F32, ("big0", "big1", "raw2", "raw3")[b]))
+            for cols in halves:
+                level = first_product(
+                    lambda a, b: w2_w[:, a, 2 * b * P : 2 * (b + 1) * P].bitcast(FP4X4), w2_s, b, cols
+                )
+                nc.scalar.activation(out=exps[b][:, cols], in_=level[:], func=ACT.Exp)
+            if b < PAGES - 1:
+                h1.append(rotating([P, S], F32, "placed", 4))
+            else:
+                h1.append(tenant([P, S], F32, "last"))
+            nc.vector.scalar_tensor_tensor(
+                out=h1[b][:], in0=exps[b][:], scalar=gain_sb[:, b : b + 1],
+                in1=sines[b // 2][:, b % 2, :], op0=MULT, op1=MULT,
+            )
+            if b > 0:
+                nc.vector.tensor_tensor(pages[b - 1][:].indirect(list3[:]), h1[b - 1][:], wg1_sb[:], MULT)
+            if b == 1:
+                w4_rounded = [
+                    round_block(
+                        w4_raw[g][:].rearrange("p j (m t) -> p m j t", t=PACK),
+                        lambda ap: ap.rearrange("p (t m j) -> p m j t", t=PACK, j=PACK),
                     )
-                sines[s, t] = held([P, H1_SLICE], F32, "sine%d_%d" % (s, t))
-                nc.scalar.activation(out=sines[s, t][:], in_=phase[:], func=ACT.Sin)
+                    for g in range(N // BANK)
+                ]
+        nc.vector.tensor_tensor(pages[PAGES - 1][:].indirect(list3[:]), h1[PAGES - 1][:], wg1_sb[:], MULT)
 
-        w4_w = held([P, N], U32, "w4_w")
+        w4_w = tenant([P, N], U32, "last")
         w4_s = held([P, N], U8, "w4_s")
-        groups = [rotating([P, PACK, BANK], BF16, "quarter", 4) for c in range(T2 // BANK)]
-        for s in range(S // H1_SLICE):
-            exps = [bank("turn") for t in range(PACK)]
-            for jp in range(H1_SLICE // (2 * P)):
-                turned = rotating([P, 2 * H], F32, "turned", 3)
-                for e in range(2):
-                    jj = 2 * jp + e
-                    cols = slice(s * H1_SLICE + jj * P, s * H1_SLICE + (jj + 1) * P)
-                    level = bank("prod")
-                    for a in range(K // K_PASS):
-                        nc.tensor.matmul_mx(
-                            out=level[:], lhsT=v_w[a][:, cols].bitcast(FP8X4), lhsT_scale=v_s[a][:, cols],
-                            rhs=w2_w[:, a, :].bitcast(FP4X4), rhs_scale=w2_s[:, a, :],
-                            start=(a == 0), stop=(a == K // K_PASS - 1),
-                        )
-                    nc.scalar.activation(
-                        out=turned[:, e * H : (e + 1) * H].rearrange("p (t m) -> p t m", t=PACK),
-                        in_=level[:].rearrange("p (m t) -> p t m", t=PACK), func=ACT.Exp,
-                    )
-                    for t in range(PACK):
-                        nc.tensor.transpose(
-                            exps[t][:, jj * P : (jj + 1) * P], turned[:, e * H + t * P : e * H + (t + 1) * P], ident[:]
-                        )
-            picks = list3[:, s * H1_SLICE // 16 : (s + 1) * H1_SLICE // 16]
-            h1 = []
-            for t in range(PACK + 1):
-                if t < PACK:
-                    h1.append(rotating([P, H1_SLICE], F32, "placed", 3))
-                    nc.vector.scalar_tensor_tensor(
-                        out=h1[t][:], in0=exps[t][:], scalar=gain_sb[:, t : t + 1], in1=sines[s, t][:],
-                        op0=MULT, op1=MULT,
-                    )
-                if t > 0:
-                    nc.vector.tensor_tensor(pages[t - 1][:].indirect(picks), h1[t - 1][:], wg1_sb[s][:, t - 1, :], MULT)
         for g in range(N // BANK):
-            quantize_block(w4_raw[g], w4_w[:, g * BANK : (g + 1) * BANK], w4_s[:, g * BANK : (g + 1) * BANK])
+            cols = slice(g * BANK, (g + 1) * BANK)
+            nc.vector.quantize_mx(out=w4_w[:, cols].bitcast(FP8X4), scales=w4_s[:, cols], in_=w4_rounded[g][:])
 
-        for t in range(PACK - 1):
-            for c in range(T2 // BANK):
-                nc.scalar.copy(out=groups[c][:, t, :], in_=pages[t][:, c * BANK : (c + 1) * BANK])
+        across = [rotating([P, BANK // P, 2, P, 2], BF16, "turned", 4) for c in range(T2 // BANK)]
+
+        def turn_page(b, c0, width):
+            turned = bank("turn")
+            tiles = width // P
+            first = (c0 % BANK) // P
+            for i in range(tiles):
+                nc.tensor.transpose(turned[:, i * P : (i + 1) * P], pages[b][:, c0 + i * P : c0 + (i + 1) * P], ident[:])
+            nc.scalar.copy(
+                out=across[c0 // BANK][:, first : first + tiles, :, 32 * b : 32 * (b + 1), :],
+                in_=turned[:, 0:width].rearrange("c (i q u e) -> c i u q e", q=32, u=2, e=2),
+            )
+
+        for b in range(PAGES - 1):
+            for c0 in range(0, T2, BANK):
+                turn_page(b, c0, BANK)
 
         z_w = held([P, T2], U32, "z_w")
         z_s = held([P, T2], U8, "z_s")
         y_s = held([P, T2], U8, "y_s")
+        y_w = held([P, N // K_PASS, T2], U32, "y_w")
         starts = [sum(OUT_CHUNKS[:c]) for c in range(len(OUT_CHUNKS))]
+        y_tags = ["raw0", "raw1", "raw2", "raw3", "big2", "big0", "big1", "sine0", "sine1"]
 
-        def make_z(c):
+        def weave_z(c):
             c0, width = starts[c], OUT_CHUNKS[c]
-            planes = groups[c0 // BANK][:, :, c0 % BANK : c0 % BANK + width]
-            nc.scalar.copy(out=planes[:, PACK - 1, :], in_=pages[PACK - 1][:, c0 : c0 + width])
-            woven = interleave(planes, width)
-            nc.vector.quantize_mx(
-                out=z_w[:, c0 : c0 + width].bitcast(FP8X4), scales=z_s[:, c0 : c0 + width], in_=woven[:]
-            )
+            pairs = across[c0 // BANK][:].rearrange("c i u p e -> c (i u p e)").bitcast(F32)
+            woven = rotating([P, width * PACK], BF16, "z_woven", 2)
+            tiles = min(2, width // P)
+            for i0 in range(0, width // P, tiles):
+                back = bank("turn")
+                for iu in range(2 * tiles):
+                    at = (2 * ((c0 % BANK) // P + i0) + iu) * P
+                    nc.tensor.transpose(back[:, iu * P : (iu + 1) * P], pairs[:, at : at + P], ident[:])
+                dst = woven[:].bitcast(F32)[:, 2 * i0 * P : 2 * (i0 + tiles) * P]
+                dst = dst.rearrange("p (i c u) -> p i c u", i=tiles, u=2)
+                src = back[:, 0 : 2 * tiles * P].rearrange("p (i u c) -> p i c u", i=tiles, u=2)
+                if c in Z_ON_SCALAR:
+                    nc.scalar.copy(out=dst, in_=src)
+                else:
+                    nc.vector.tensor_copy(out=dst, in_=src)
+            return woven
+
+        def quantize_z(c, woven):
+            cols = slice(starts[c], starts[c] + OUT_CHUNKS[c])
+            nc.vector.quantize_mx(out=z_w[:, cols].bitcast(FP8X4), scales=z_s[:, cols], in_=woven[:])
 
         def make_y(c, g):
             c0, width = starts[c], OUT_CHUNKS[c]
             cols = slice(c0, c0 + width)
-            y = rotating([P, PACK, width], F32, "wide", 4)
+            y = tenant([P, PACK, width], F32, y_tags[(2 * c + g) % len(y_tags)])
             flat = y[:].rearrange("p t c -> p (t c)")
             share = BANK // width
             for b in range(PACK // share):
-                acc = bank(("prod", "turn")[(g + b) % 2])
+                acc = bank("prod")
                 for i in range(share):
                     at = g * BANK + (b * share + i) * P
                     nc.tensor.matmul_mx(
@@ -294,24 +334,56 @@ def tile_list_ocean_band_weave_kernel(
             )
             return y
 
-        def make_planes(c, g, y):
+        def weave_y(c, g, y):
+            woven = rotating([P, OUT_CHUNKS[c] * PACK], BF16, "rounded", 4)
+            dst = woven[:].rearrange("p (c i t) -> p c t i", i=4, t=PACK)
+            src = y[:].rearrange("p t (c i) -> p c t i", i=4)
+            if c == chunks - 1 and g == 1:
+                nc.scalar.copy(out=dst, in_=src)
+            else:
+                nc.vector.tensor_copy(out=dst, in_=src)
+            return woven
+
+        def make_planes(c, g, woven):
             c0, width = starts[c], OUT_CHUNKS[c]
             cols = slice(c0, c0 + width)
-            woven = interleave(y[:], width)
-            words = rotating([P, width], U32, "words", 4)
-            nc.vector.quantize_mx(out=words[:].bitcast(FP8X4), scales=y_s[4 * g : P, cols], in_=woven[:])
+            nc.vector.quantize_mx(out=y_w[:, g, cols].bitcast(FP8X4), scales=y_s[4 * g : P, cols], in_=woven[:])
+
+        def store_words(cols):
             nc.sync.dma_start(
-                out_1[g, :, cols, :].rearrange("p m t -> p (m t)").bitcast(I32), words[:].bitcast(I32)
+                out_1[:, :, cols, :].rearrange("g p m t -> p g (m t)").bitcast(I32), y_w[:, :, cols].bitcast(I32)
             )
 
-        make_z(0)
-        for c in range(len(OUT_CHUNKS)):
-            if c + 1 < len(OUT_CHUNKS):
-                make_z(c + 1)
-            ys = [make_y(c, g) for g in range(N // K_PASS)]
-            for g in range(N // K_PASS):
-                make_planes(c, g, ys[g])
-        for q in range(QUADS):
-            (nc.scalar, nc.sync)[q % 2].dma_start(
-                out_2.bitcast(I32)[:, 4 * q : 4 * q + 4, :], y_s[32 * q : 32 * q + 8, :].bitcast(I32)
-            )
+        def store_scales(queues, cols):
+            words = slice(cols.start // 4, cols.stop // 4)
+            for q in range(QUADS):
+                queues[q % len(queues)].dma_start(
+                    out_2.bitcast(I32)[:, 4 * q : 4 * q + 4, words],
+                    y_s[32 * q : 32 * q + 8, :].bitcast(I32)[:, words],
+                )
+
+        chunks = len(OUT_CHUNKS)
+        groups = range(N // K_PASS)
+        turn_page(PAGES - 1, starts[0], OUT_CHUNKS[0])
+        turn_page(PAGES - 1, starts[1], OUT_CHUNKS[1])
+        quantize_z(0, weave_z(0))
+        for c in range(2, chunks):
+            turn_page(PAGES - 1, starts[c], OUT_CHUNKS[c])
+        ys = [[make_y(0, g) for g in groups]]
+        ahead = weave_z(1)
+        stored = 0
+        for c in range(1, chunks + 1):
+            if c < chunks:
+                woven_z = ahead
+                if c + 1 < chunks:
+                    ahead = weave_z(c + 1)
+                quantize_z(c, woven_z)
+                ys.append([make_y(c, g) for g in groups])
+            woven_y = [weave_y(c - 1, g, ys[c - 1][g]) for g in groups]
+            for g in groups:
+                make_planes(c - 1, g, woven_y[g])
+            done = starts[c - 1] + OUT_CHUNKS[c - 1]
+            if done >= BANK:
+                store_words(slice(stored, done))
+                stored = done
+        store_scales((nc.scalar, nc.sync), slice(0, T2))

@@ -23,9 +23,8 @@ K_PASS = P * PACK
 BANK = 512
 QUADS = 4
 H2_SLICE = 256
-OUT_CHUNKS = (128, 128, 256, 512, 512, 256, 256)
+OUT_CHUNKS = (256, 256, 512, 1024)
 PAGES = H // P
-Z_ON_SCALAR = ()
 
 
 def tile_list_ocean_band_weave_kernel(
@@ -71,11 +70,6 @@ def tile_list_ocean_band_weave_kernel(
                 )
             return tile
 
-        def load_block(rows, tag):
-            raw = tenant([P, PACK, BANK], F32, tag)
-            nc.sync.dma_start(raw[:], rows.rearrange("(p j) c -> p j c", j=PACK))
-            return raw
-
         def round_block(src, order):
             rounded = rotating([P, BANK * PACK], BF16, "rounded", 4)
             dst = order(rounded[:])
@@ -101,13 +95,15 @@ def tile_list_ocean_band_weave_kernel(
         list4 = load_list(offs4, "list4")
         wg2_sb = held([P, S], F32, "wg2_sb")
         nc.sync.dma_start(wg2_sb[:], wg2)
-        w1_raw = [load_block(w1[a * K_PASS : (a + 1) * K_PASS, :], "raw%d" % a) for a in range(K // K_PASS)]
+        w1_raw = tenant([P, K // K_PASS, PACK, H], F32, "raw1")
+        nc.sync.dma_start(w1_raw[:], w1.rearrange("(a p j) c -> p a j c", p=P, j=PACK))
         w2_w = held([P, K // K_PASS, 2 * H], U8, "w2_w")
         nc.sync.dma_start(w2_w[:].bitcast(I32), w2_words.bitcast(I32).rearrange("a p c -> p a c"))
         list3 = load_list(offs3, "list3")
         wg1_sb = held([P, S], F32, "wg1_sb")
         nc.sync.dma_start(wg1_sb[:], wg1)
-        w4_raw = [load_block(w4[:, g * BANK : (g + 1) * BANK], "raw%d" % (2 + g)) for g in range(N // BANK)]
+        w4_raw = tenant([P, PACK, N], F32, "raw4")
+        nc.sync.dma_start(w4_raw[:], w4.rearrange("(p j) c -> p j c", j=PACK))
         w2_s = held([P, K // K_PASS, H], U8, "w2_s")
         nc.vector.memset(w2_s[:].bitcast(I32), 0)
         for q in range(QUADS):
@@ -155,10 +151,7 @@ def tile_list_ocean_band_weave_kernel(
 
         def sines_of_tile(s, jj):
             cols = slice(s * H2_SLICE + jj * P, s * H2_SLICE + (jj + 1) * P)
-            if s == 2:
-                half_sin = tenant([P, 2 * H], F32, "raw%d" % jj)
-            else:
-                half_sin = rotating([P, 2 * H], F32, "turned", 4)
+            half_sin = rotating([P, 2 * H], F32, "turned", 4)
             for c in range(2):
                 arg = bank("prod")
                 nc.tensor.matmul_mx(
@@ -195,7 +188,7 @@ def tile_list_ocean_band_weave_kernel(
 
         def quantize_w1(a):
             rounded = round_block(
-                w1_raw[a][:].rearrange("p j (c i) -> p c j i", i=4),
+                w1_raw[:, a].rearrange("p j (c i) -> p c j i", i=4),
                 lambda ap: ap.rearrange("p (c i j) -> p c j i", i=4, j=PACK),
             )
             nc.vector.quantize_mx(out=w1_w[:, a, :].bitcast(FP8X4), scales=w1_s[:, a, :], in_=rounded[:])
@@ -231,21 +224,19 @@ def tile_list_ocean_band_weave_kernel(
             if b == 0:
                 place_slice(3)
 
-        exps = []
         h1 = []
         for b in range(PAGES):
-            exps.append(tenant([P, S], F32, ("big0", "big1", "raw2", "raw3")[b]))
-            for cols in halves:
-                level = first_product(
-                    lambda a, b: w2_w[:, a, 2 * b * P : 2 * (b + 1) * P].bitcast(FP4X4), w2_s, b, cols
-                )
-                nc.scalar.activation(out=exps[b][:, cols], in_=level[:], func=ACT.Exp)
             if b < PAGES - 1:
                 h1.append(rotating([P, S], F32, "placed", 4))
             else:
                 h1.append(tenant([P, S], F32, "last"))
+            for cols in halves:
+                level = first_product(
+                    lambda a, b: w2_w[:, a, 2 * b * P : 2 * (b + 1) * P].bitcast(FP4X4), w2_s, b, cols
+                )
+                nc.scalar.activation(out=h1[b][:, cols], in_=level[:], func=ACT.Exp)
             nc.vector.scalar_tensor_tensor(
-                out=h1[b][:], in0=exps[b][:], scalar=gain_sb[:, b : b + 1],
+                out=h1[b][:], in0=h1[b][:], scalar=gain_sb[:, b : b + 1],
                 in1=sines[b // 2][:, b % 2, :], op0=MULT, op1=MULT,
             )
             if b > 0:
@@ -253,7 +244,7 @@ def tile_list_ocean_band_weave_kernel(
             if b == 1:
                 w4_rounded = [
                     round_block(
-                        w4_raw[g][:].rearrange("p j (m t) -> p m j t", t=PACK),
+                        w4_raw[:, :, g * BANK : (g + 1) * BANK].rearrange("p j (m t) -> p m j t", t=PACK),
                         lambda ap: ap.rearrange("p (t m j) -> p m j t", t=PACK, j=PACK),
                     )
                     for g in range(N // BANK)
@@ -287,103 +278,120 @@ def tile_list_ocean_band_weave_kernel(
         z_s = held([P, T2], U8, "z_s")
         y_s = held([P, T2], U8, "y_s")
         y_w = held([P, N // K_PASS, T2], U32, "y_w")
-        starts = [sum(OUT_CHUNKS[:c]) for c in range(len(OUT_CHUNKS))]
-        y_tags = ["raw0", "raw1", "raw2", "raw3", "big2", "big0", "big1", "sine0", "sine1"]
+        chunks = len(OUT_CHUNKS)
+        groups = range(N // K_PASS)
+        starts = [sum(OUT_CHUNKS[:c]) for c in range(chunks)]
+        pieces = [(c0, min(BANK, starts[c] + OUT_CHUNKS[c] - c0)) for c in range(chunks)
+                  for c0 in range(starts[c], starts[c] + OUT_CHUNKS[c], BANK)]
 
-        def weave_z(c):
-            c0, width = starts[c], OUT_CHUNKS[c]
+        def weave_z(c0, width):
             pairs = across[c0 // BANK][:].rearrange("c i u p e -> c (i u p e)").bitcast(F32)
             woven = rotating([P, width * PACK], BF16, "z_woven", 2)
-            tiles = min(2, width // P)
-            for i0 in range(0, width // P, tiles):
+            for i0 in range(0, width // P, 2):
                 back = bank("turn")
-                for iu in range(2 * tiles):
+                for iu in range(4):
                     at = (2 * ((c0 % BANK) // P + i0) + iu) * P
                     nc.tensor.transpose(back[:, iu * P : (iu + 1) * P], pairs[:, at : at + P], ident[:])
-                dst = woven[:].bitcast(F32)[:, 2 * i0 * P : 2 * (i0 + tiles) * P]
-                dst = dst.rearrange("p (i c u) -> p i c u", i=tiles, u=2)
-                src = back[:, 0 : 2 * tiles * P].rearrange("p (i u c) -> p i c u", i=tiles, u=2)
-                if c in Z_ON_SCALAR:
-                    nc.scalar.copy(out=dst, in_=src)
-                else:
-                    nc.vector.tensor_copy(out=dst, in_=src)
+                dst = woven[:].bitcast(F32)[:, 2 * i0 * P : 2 * (i0 + 2) * P]
+                nc.vector.tensor_copy(
+                    out=dst.rearrange("p (i c u) -> p i c u", i=2, u=2),
+                    in_=back[:].rearrange("p (i u c) -> p i c u", i=2, u=2),
+                )
             return woven
 
-        def quantize_z(c, woven):
-            cols = slice(starts[c], starts[c] + OUT_CHUNKS[c])
+        def quantize_z(c0, width, woven):
+            cols = slice(c0, c0 + width)
             nc.vector.quantize_mx(out=z_w[:, cols].bitcast(FP8X4), scales=z_s[:, cols], in_=woven[:])
+
+        def result_tile(c, g):
+            shape = [P, PACK, OUT_CHUNKS[c]]
+            if OUT_CHUNKS[c] < BANK:
+                return rotating(shape, F32, "placed", 4)
+            return tenant(shape, F32, (("big0", "big1"), ("raw1", "raw4"))[OUT_CHUNKS[c] // BANK - 1][g])
+
+        def fill_bank(y, g, slots, c, c0, width):
+            acc = bank("prod")
+            for i, t in enumerate(slots):
+                at = g * BANK + t * P
+                nc.tensor.matmul_mx(
+                    out=acc[:, i * width : (i + 1) * width],
+                    lhsT=w4_w[:, at : at + P].bitcast(FP8X4), lhsT_scale=w4_s[:, at : at + P],
+                    rhs=z_w[:, c0 : c0 + width].bitcast(FP8X4), rhs_scale=z_s[:, c0 : c0 + width],
+                    start=True, stop=True,
+                )
+            at = c0 - starts[c]
+            nc.scalar.copy(
+                out=y[:, slots[0] : slots[-1] + 1, at : at + width],
+                in_=acc[:].rearrange("p (t c) -> p t c", c=width),
+            )
+
+        def store_y(y, g, c, t0, t1):
+            rows = out_0[g * K_PASS : (g + 1) * K_PASS, starts[c] : starts[c] + OUT_CHUNKS[c]]
+            nc.sync.dma_start(rows.rearrange("(p t) c -> p t c", t=PACK)[:, t0:t1, :], y[:, t0:t1, :])
 
         def make_y(c, g):
             c0, width = starts[c], OUT_CHUNKS[c]
-            cols = slice(c0, c0 + width)
-            y = tenant([P, PACK, width], F32, y_tags[(2 * c + g) % len(y_tags)])
-            flat = y[:].rearrange("p t c -> p (t c)")
-            share = BANK // width
-            for b in range(PACK // share):
-                acc = bank("prod")
-                for i in range(share):
-                    at = g * BANK + (b * share + i) * P
-                    nc.tensor.matmul_mx(
-                        out=acc[:, i * width : (i + 1) * width],
-                        lhsT=w4_w[:, at : at + P].bitcast(FP8X4), lhsT_scale=w4_s[:, at : at + P],
-                        rhs=z_w[:, cols].bitcast(FP8X4), rhs_scale=z_s[:, cols], start=True, stop=True,
-                    )
-                nc.scalar.copy(out=flat[:, b * BANK : (b + 1) * BANK], in_=acc[:])
-            nc.sync.dma_start(
-                out_0[g * K_PASS : (g + 1) * K_PASS, cols].rearrange("(p t) c -> p t c", t=PACK), y[:]
-            )
+            y = result_tile(c, g)
+            if width <= BANK:
+                share = BANK // width
+                for t0 in range(0, PACK, share):
+                    fill_bank(y, g, range(t0, t0 + share), c, c0, width)
+                store_y(y, g, c, 0, PACK)
+            else:
+                for at in range(c0, c0 + width, BANK):
+                    for t in range(PACK):
+                        fill_bank(y, g, [t], c, at, BANK)
+                        if at + BANK == c0 + width and t % 2 == 1:
+                            store_y(y, g, c, t - 1, t + 1)
             return y
 
-        def weave_y(c, g, y):
-            woven = rotating([P, OUT_CHUNKS[c] * PACK], BF16, "rounded", 4)
-            dst = woven[:].rearrange("p (c i t) -> p c t i", i=4, t=PACK)
-            src = y[:].rearrange("p t (c i) -> p c t i", i=4)
-            if c == chunks - 1 and g == 1:
-                nc.scalar.copy(out=dst, in_=src)
-            else:
-                nc.vector.tensor_copy(out=dst, in_=src)
+        def weave_y(y, at, width):
+            woven = rotating([P, width * PACK], BF16, "rounded", 4)
+            nc.vector.tensor_copy(
+                out=woven[:].rearrange("p (c i t) -> p c t i", i=4, t=PACK),
+                in_=y[:, :, at : at + width].rearrange("p t (c i) -> p c t i", i=4),
+            )
             return woven
 
-        def make_planes(c, g, woven):
-            c0, width = starts[c], OUT_CHUNKS[c]
-            cols = slice(c0, c0 + width)
-            nc.vector.quantize_mx(out=y_w[:, g, cols].bitcast(FP8X4), scales=y_s[4 * g : P, cols], in_=woven[:])
+        def make_planes(c, ys):
+            width = min(BANK, OUT_CHUNKS[c])
+            parts = [(g, c0) for g in groups for c0 in range(starts[c], starts[c] + OUT_CHUNKS[c], BANK)]
+            for pair in range(0, len(parts), 2):
+                woven = [weave_y(ys[g], c0 - starts[c], width) for g, c0 in parts[pair : pair + 2]]
+                for (g, c0), tile in zip(parts[pair : pair + 2], woven):
+                    cols = slice(c0, c0 + width)
+                    nc.vector.quantize_mx(
+                        out=y_w[:, g, cols].bitcast(FP8X4), scales=y_s[4 * g : P, cols], in_=tile[:]
+                    )
 
-        def store_words(cols):
+        def store_words(g, cols):
             nc.sync.dma_start(
-                out_1[:, :, cols, :].rearrange("g p m t -> p g (m t)").bitcast(I32), y_w[:, :, cols].bitcast(I32)
+                out_1[g, :, cols, :].rearrange("p m t -> p (m t)").bitcast(I32), y_w[:, g, cols].bitcast(I32)
             )
 
-        def store_scales(queues, cols):
-            words = slice(cols.start // 4, cols.stop // 4)
-            for q in range(QUADS):
-                queues[q % len(queues)].dma_start(
-                    out_2.bitcast(I32)[:, 4 * q : 4 * q + 4, words],
-                    y_s[32 * q : 32 * q + 8, :].bitcast(I32)[:, words],
-                )
-
-        chunks = len(OUT_CHUNKS)
-        groups = range(N // K_PASS)
-        turn_page(PAGES - 1, starts[0], OUT_CHUNKS[0])
-        turn_page(PAGES - 1, starts[1], OUT_CHUNKS[1])
-        quantize_z(0, weave_z(0))
-        for c in range(2, chunks):
-            turn_page(PAGES - 1, starts[c], OUT_CHUNKS[c])
+        turn_page(PAGES - 1, *pieces[0])
+        turn_page(PAGES - 1, *pieces[1])
+        quantize_z(*pieces[0], weave_z(*pieces[0]))
+        for piece in pieces[2:]:
+            turn_page(PAGES - 1, *piece)
         ys = [[make_y(0, g) for g in groups]]
-        ahead = weave_z(1)
-        stored = 0
-        for c in range(1, chunks + 1):
-            if c < chunks:
-                woven_z = ahead
-                if c + 1 < chunks:
-                    ahead = weave_z(c + 1)
-                quantize_z(c, woven_z)
-                ys.append([make_y(c, g) for g in groups])
-            woven_y = [weave_y(c - 1, g, ys[c - 1][g]) for g in groups]
-            for g in groups:
-                make_planes(c - 1, g, woven_y[g])
-            done = starts[c - 1] + OUT_CHUNKS[c - 1]
-            if done >= BANK:
-                store_words(slice(stored, done))
-                stored = done
-        store_scales((nc.scalar, nc.sync), slice(0, T2))
+        ahead = weave_z(*pieces[1])
+        for i in range(1, len(pieces)):
+            woven_z = ahead
+            if i + 1 < len(pieces):
+                ahead = weave_z(*pieces[i + 1])
+            quantize_z(*pieces[i], woven_z)
+            if i < chunks - 1:
+                ys.append([make_y(i, g) for g in groups])
+            if i < chunks:
+                make_planes(i - 1, ys[i - 1])
+        ys.append([make_y(chunks - 1, g) for g in groups])
+        for g in groups:
+            store_words(g, slice(0, starts[-1]))
+        make_planes(chunks - 1, ys[-1])
+        for g in groups:
+            store_words(g, slice(starts[-1], T2))
+        for q in range(QUADS):
+            (nc.scalar, nc.sync)[q % 2].dma_start(
+                out_2.bitcast(I32)[:, 4 * q : 4 * q + 4, :], y_s[32 * q : 32 * q + 8, :].bitcast(I32)
+            )

@@ -23,7 +23,7 @@ K_PASS = P * PACK
 BANK = 512
 QUADS = 4
 H2_SLICE = 256
-OUT_CHUNKS = (256, 256, 512, 1024)
+OUT_CHUNKS = (256, 256, 512, 512, 512)
 PAGES = H // P
 
 
@@ -188,8 +188,8 @@ def tile_list_ocean_band_weave_kernel(
 
         def quantize_w1(a):
             rounded = round_block(
-                w1_raw[:, a].rearrange("p j (c i) -> p c j i", i=4),
-                lambda ap: ap.rearrange("p (c i j) -> p c j i", i=4, j=PACK),
+                w1_raw[:, a].rearrange("p j c -> p c j"),
+                lambda ap: ap.rearrange("p (c j) -> p c j", j=PACK),
             )
             nc.vector.quantize_mx(out=w1_w[:, a, :].bitcast(FP8X4), scales=w1_s[:, a, :], in_=rounded[:])
 
@@ -244,8 +244,8 @@ def tile_list_ocean_band_weave_kernel(
             if b == 1:
                 w4_rounded = [
                     round_block(
-                        w4_raw[:, :, g * BANK : (g + 1) * BANK].rearrange("p j (m t) -> p m j t", t=PACK),
-                        lambda ap: ap.rearrange("p (t m j) -> p m j t", t=PACK, j=PACK),
+                        w4_raw[:, :, g * BANK : (g + 1) * BANK].rearrange("p j (m t) -> p m t j", t=PACK),
+                        lambda ap: ap.rearrange("p (t m j) -> p m t j", t=PACK, j=PACK),
                     )
                     for g in range(N // BANK)
                 ]
@@ -307,7 +307,7 @@ def tile_list_ocean_band_weave_kernel(
             shape = [P, PACK, OUT_CHUNKS[c]]
             if OUT_CHUNKS[c] < BANK:
                 return rotating(shape, F32, "placed", 4)
-            return tenant(shape, F32, (("big0", "big1"), ("raw1", "raw4"))[OUT_CHUNKS[c] // BANK - 1][g])
+            return tenant(shape, F32, (("big0", "big1"), ("raw1", "raw4"), ("sine0", "sine1"))[c % 3][g])
 
         def fill_bank(y, g, slots, c, c0, width):
             acc = bank("prod")
@@ -332,24 +332,17 @@ def tile_list_ocean_band_weave_kernel(
         def make_y(c, g):
             c0, width = starts[c], OUT_CHUNKS[c]
             y = result_tile(c, g)
-            if width <= BANK:
-                share = BANK // width
-                for t0 in range(0, PACK, share):
-                    fill_bank(y, g, range(t0, t0 + share), c, c0, width)
-                store_y(y, g, c, 0, PACK)
-            else:
-                for at in range(c0, c0 + width, BANK):
-                    for t in range(PACK):
-                        fill_bank(y, g, [t], c, at, BANK)
-                        if at + BANK == c0 + width and t % 2 == 1:
-                            store_y(y, g, c, t - 1, t + 1)
+            share = BANK // width
+            for t0 in range(0, PACK, share):
+                fill_bank(y, g, range(t0, t0 + share), c, c0, width)
+            store_y(y, g, c, 0, PACK)
             return y
 
         def weave_y(y, at, width):
             woven = rotating([P, width * PACK], BF16, "rounded", 4)
             nc.vector.tensor_copy(
-                out=woven[:].rearrange("p (c i t) -> p c t i", i=4, t=PACK),
-                in_=y[:, :, at : at + width].rearrange("p t (c i) -> p c t i", i=4),
+                out=woven[:].rearrange("p (c t) -> p c t", t=PACK),
+                in_=y[:, :, at : at + width].rearrange("p t c -> p c t"),
             )
             return woven
 
@@ -383,11 +376,12 @@ def tile_list_ocean_band_weave_kernel(
             quantize_z(*pieces[i], woven_z)
             if i < chunks - 1:
                 ys.append([make_y(i, g) for g in groups])
-            if i < chunks:
-                make_planes(i - 1, ys[i - 1])
-        ys.append([make_y(chunks - 1, g) for g in groups])
-        for g in groups:
-            store_words(g, slice(0, starts[-1]))
+            else:
+                ys.append([make_y(chunks - 1, g) for g in groups])
+            make_planes(i - 1, ys[i - 1])
+            if starts[i] % BANK == 0:
+                for g in groups:
+                    store_words(g, slice(starts[i] - BANK, starts[i]))
         make_planes(chunks - 1, ys[-1])
         for g in groups:
             store_words(g, slice(starts[-1], T2))

@@ -23,7 +23,8 @@ K_PASS = P * PACK
 BANK = 512
 QUADS = 4
 H2_SLICE = 256
-OUT_CHUNKS = (256, 256, 512, 512, 512)
+OUT_CHUNKS = (256, 256, 512, 512, 256, 256)
+Z_ON_SCALAR = 1536
 PAGES = H // P
 
 
@@ -188,8 +189,8 @@ def tile_list_ocean_band_weave_kernel(
 
         def quantize_w1(a):
             rounded = round_block(
-                w1_raw[:, a].rearrange("p j c -> p c j"),
-                lambda ap: ap.rearrange("p (c j) -> p c j", j=PACK),
+                w1_raw[:, a].rearrange("p j (c i) -> p c j i", i=4),
+                lambda ap: ap.rearrange("p (c i j) -> p c j i", i=4, j=PACK),
             )
             nc.vector.quantize_mx(out=w1_w[:, a, :].bitcast(FP8X4), scales=w1_s[:, a, :], in_=rounded[:])
 
@@ -244,8 +245,8 @@ def tile_list_ocean_band_weave_kernel(
             if b == 1:
                 w4_rounded = [
                     round_block(
-                        w4_raw[:, :, g * BANK : (g + 1) * BANK].rearrange("p j (m t) -> p m t j", t=PACK),
-                        lambda ap: ap.rearrange("p (t m j) -> p m t j", t=PACK, j=PACK),
+                        w4_raw[:, :, g * BANK : (g + 1) * BANK].rearrange("p j (m t) -> p m j t", t=PACK),
+                        lambda ap: ap.rearrange("p (t m j) -> p m j t", t=PACK, j=PACK),
                     )
                     for g in range(N // BANK)
                 ]
@@ -293,7 +294,7 @@ def tile_list_ocean_band_weave_kernel(
                     at = (2 * ((c0 % BANK) // P + i0) + iu) * P
                     nc.tensor.transpose(back[:, iu * P : (iu + 1) * P], pairs[:, at : at + P], ident[:])
                 dst = woven[:].bitcast(F32)[:, 2 * i0 * P : 2 * (i0 + 2) * P]
-                nc.vector.tensor_copy(
+                (nc.scalar.copy if c0 >= Z_ON_SCALAR else nc.vector.tensor_copy)(
                     out=dst.rearrange("p (i c u) -> p i c u", i=2, u=2),
                     in_=back[:].rearrange("p (i u c) -> p i c u", i=2, u=2),
                 )
@@ -307,7 +308,7 @@ def tile_list_ocean_band_weave_kernel(
             shape = [P, PACK, OUT_CHUNKS[c]]
             if OUT_CHUNKS[c] < BANK:
                 return rotating(shape, F32, "placed", 4)
-            return tenant(shape, F32, (("big0", "big1"), ("raw1", "raw4"), ("sine0", "sine1"))[c % 3][g])
+            return tenant(shape, F32, (("big0", "big1"), ("raw1", "raw4"), ("sine0", "sine1"))[c % 2][g])
 
         def fill_bank(y, g, slots, c, c0, width):
             acc = bank("prod")
@@ -327,7 +328,7 @@ def tile_list_ocean_band_weave_kernel(
 
         def store_y(y, g, c, t0, t1):
             rows = out_0[g * K_PASS : (g + 1) * K_PASS, starts[c] : starts[c] + OUT_CHUNKS[c]]
-            nc.sync.dma_start(rows.rearrange("(p t) c -> p t c", t=PACK)[:, t0:t1, :], y[:, t0:t1, :])
+            nc.scalar.dma_start(rows.rearrange("(p t) c -> p t c", t=PACK)[:, t0:t1, :], y[:, t0:t1, :])
 
         def make_y(c, g):
             c0, width = starts[c], OUT_CHUNKS[c]
@@ -341,8 +342,8 @@ def tile_list_ocean_band_weave_kernel(
         def weave_y(y, at, width):
             woven = rotating([P, width * PACK], BF16, "rounded", 4)
             nc.vector.tensor_copy(
-                out=woven[:].rearrange("p (c t) -> p c t", t=PACK),
-                in_=y[:, :, at : at + width].rearrange("p t c -> p c t"),
+                out=woven[:].rearrange("p (c i t) -> p c t i", i=4, t=PACK),
+                in_=y[:, :, at : at + width].rearrange("p t (c i) -> p c t i", i=4),
             )
             return woven
 
@@ -384,7 +385,7 @@ def tile_list_ocean_band_weave_kernel(
                     store_words(g, slice(starts[i] - BANK, starts[i]))
         make_planes(chunks - 1, ys[-1])
         for g in groups:
-            store_words(g, slice(starts[-1], T2))
+            store_words(g, slice(T2 - BANK, T2))
         for q in range(QUADS):
             (nc.scalar, nc.sync)[q % 2].dma_start(
                 out_2.bitcast(I32)[:, 4 * q : 4 * q + 4, :], y_s[32 * q : 32 * q + 8, :].bitcast(I32)

@@ -23,8 +23,7 @@ K_PASS = P * PACK
 BANK = 512
 QUADS = 4
 H2_SLICE = 256
-OUT_CHUNKS = (256, 256, 512, 512, 256, 256)
-Z_ON_SCALAR = 1536
+OUT_CHUNKS = (256, 256, 512, 512, 512)
 PAGES = H // P
 
 
@@ -82,13 +81,13 @@ def tile_list_ocean_band_weave_kernel(
         list2 = load_list(offs2, "list2")
         tab2_s = load_plane(nc.sync, tab2_scales[0], "tab2_s")
         tab2_w = load_words(nc.sync, tab2_words[0], "big2")
+        w3_s = load_plane(nc.sync, w3_scales[0], "w3_s")
+        w3_w = load_words(nc.sync, w3_words[0], "w3_w")
         list1 = load_list(offs, "list1")
         tab_s = held([P, T], U8, "tab_s")
         nc.sync.dma_start(tab_s[0:32, :].bitcast(I32), tab_scales.bitcast(I32).rearrange("a q c -> (a q) c"))
         nc.vector.memset(tab_s[32:64, :].bitcast(I32), 0)
         nc.vector.memset(tab_s[64:P, :].bitcast(I32), 0)
-        w3_s = load_plane(nc.sync, w3_scales[0], "w3_s")
-        w3_w = load_words(nc.sync, w3_words[0], "w3_w")
         tab_w = [load_words(nc.sync, tab_words[a], "big%d" % a) for a in range(K // K_PASS)]
         gain_sb = held([P, PAGES], F32, "gain_sb")
         with nc.allow_non_contiguous_dma(reason="one gain value for each partition and page"):
@@ -125,10 +124,8 @@ def tile_list_ocean_band_weave_kernel(
         v2_s = held([P, S], U8, "v2_s")
         v2_w = held([P, S], U32, "v2_w")
         nc.vector.tensor_copy(v2_s[:], tab2_s[:].indirect(list2[:]))
-        for h in range(2):
-            nc.vector.tensor_copy(
-                v2_w[:, h * 512 : (h + 1) * 512], tab2_w[:].indirect(list2[:, h * 32 : (h + 1) * 32])
-            )
+        for j0, j1 in ((0, H2_SLICE), (H2_SLICE, S)):
+            nc.vector.tensor_copy(v2_w[:, j0:j1], tab2_w[:].indirect(list2[:, j0 // 16 : j1 // 16]))
         v_rows = held([P, S], U8, "v_rows")
         nc.vector.tensor_copy(v_rows[:], tab_s[:].indirect(list1[:]))
         for a in range(K // K_PASS):
@@ -194,17 +191,19 @@ def tile_list_ocean_band_weave_kernel(
             )
             nc.vector.quantize_mx(out=w1_w[:, a, :].bitcast(FP8X4), scales=w1_s[:, a, :], in_=rounded[:])
 
-        for s in range(S // H2_SLICE):
-            for jj in range(tiles_per_slice):
-                sines_of_tile(s, jj)
-                if s == 3 and jj == 0:
-                    place_slice(2)
-            if s == 1:
-                quantize_w1(0)
-                place_slice(1)
-                quantize_w1(1)
-            if s == 0:
-                place_slice(0)
+        sines_of_tile(0, 0)
+        sines_of_tile(0, 1)
+        place_slice(0)
+        sines_of_tile(1, 0)
+        sines_of_tile(1, 1)
+        sines_of_tile(2, 0)
+        place_slice(1)
+        sines_of_tile(2, 1)
+        for a in range(K // K_PASS):
+            quantize_w1(a)
+        place_slice(2)
+        sines_of_tile(3, 0)
+        sines_of_tile(3, 1)
 
         def first_product(words, scales, b, cols):
             acc = bank("prod")
@@ -218,38 +217,37 @@ def tile_list_ocean_band_weave_kernel(
 
         halves = [slice(h * BANK, (h + 1) * BANK) for h in range(S // BANK)]
         sines = [tenant([P, 2, S], F32, "sine%d" % i) for i in range(PAGES // 2)]
-        for b in range(PAGES):
-            for cols in halves:
-                phase = first_product(lambda a, b: w1_w[:, a, b * P : (b + 1) * P].bitcast(FP8X4), w1_s, b, cols)
-                nc.scalar.activation(out=sines[b // 2][:, b % 2, cols], in_=phase[:], func=ACT.Sin)
-            if b == 0:
-                place_slice(3)
-
         h1 = []
-        for b in range(PAGES):
-            if b < PAGES - 1:
-                h1.append(rotating([P, S], F32, "placed", 4))
-            else:
-                h1.append(tenant([P, S], F32, "last"))
-            for cols in halves:
-                level = first_product(
-                    lambda a, b: w2_w[:, a, 2 * b * P : 2 * (b + 1) * P].bitcast(FP4X4), w2_s, b, cols
-                )
-                nc.scalar.activation(out=h1[b][:, cols], in_=level[:], func=ACT.Exp)
-            nc.vector.scalar_tensor_tensor(
-                out=h1[b][:], in0=h1[b][:], scalar=gain_sb[:, b : b + 1],
-                in1=sines[b // 2][:, b % 2, :], op0=MULT, op1=MULT,
-            )
-            if b > 0:
-                nc.vector.tensor_tensor(pages[b - 1][:].indirect(list3[:]), h1[b - 1][:], wg1_sb[:], MULT)
-            if b == 1:
-                w4_rounded = [
-                    round_block(
-                        w4_raw[:, :, g * BANK : (g + 1) * BANK].rearrange("p j (m t) -> p m j t", t=PACK),
-                        lambda ap: ap.rearrange("p (t m j) -> p m j t", t=PACK, j=PACK),
+        for pair in range(PAGES // 2):
+            for b in (2 * pair, 2 * pair + 1):
+                for cols in halves:
+                    phase = first_product(lambda a, b: w1_w[:, a, b * P : (b + 1) * P].bitcast(FP8X4), w1_s, b, cols)
+                    nc.scalar.activation(out=sines[pair][:, b % 2, cols], in_=phase[:], func=ACT.Sin)
+                if b == 0:
+                    place_slice(3)
+            for b in (2 * pair, 2 * pair + 1):
+                if b < PAGES - 1:
+                    h1.append(rotating([P, S], F32, "placed", 4))
+                else:
+                    h1.append(tenant([P, S], F32, "last"))
+                for cols in halves:
+                    level = first_product(
+                        lambda a, b: w2_w[:, a, 2 * b * P : 2 * (b + 1) * P].bitcast(FP4X4), w2_s, b, cols
                     )
-                    for g in range(N // BANK)
-                ]
+                    nc.scalar.activation(out=h1[b][:, cols], in_=level[:], func=ACT.Exp)
+                nc.vector.scalar_tensor_tensor(
+                    out=h1[b][:], in0=h1[b][:], scalar=gain_sb[:, b : b + 1],
+                    in1=sines[pair][:, b % 2, :], op0=MULT, op1=MULT,
+                )
+                if b > 0:
+                    nc.vector.tensor_tensor(pages[b - 1][:].indirect(list3[:]), h1[b - 1][:], wg1_sb[:], MULT)
+        w4_rounded = [
+            round_block(
+                w4_raw[:, :, g * BANK : (g + 1) * BANK].rearrange("p j (m t) -> p m j t", t=PACK),
+                lambda ap: ap.rearrange("p (t m j) -> p m j t", t=PACK, j=PACK),
+            )
+            for g in range(N // BANK)
+        ]
         nc.vector.tensor_tensor(pages[PAGES - 1][:].indirect(list3[:]), h1[PAGES - 1][:], wg1_sb[:], MULT)
 
         w4_w = tenant([P, N], U32, "last")
@@ -294,7 +292,7 @@ def tile_list_ocean_band_weave_kernel(
                     at = (2 * ((c0 % BANK) // P + i0) + iu) * P
                     nc.tensor.transpose(back[:, iu * P : (iu + 1) * P], pairs[:, at : at + P], ident[:])
                 dst = woven[:].bitcast(F32)[:, 2 * i0 * P : 2 * (i0 + 2) * P]
-                (nc.scalar.copy if c0 >= Z_ON_SCALAR else nc.vector.tensor_copy)(
+                nc.vector.tensor_copy(
                     out=dst.rearrange("p (i c u) -> p i c u", i=2, u=2),
                     in_=back[:].rearrange("p (i u c) -> p i c u", i=2, u=2),
                 )
@@ -308,7 +306,7 @@ def tile_list_ocean_band_weave_kernel(
             shape = [P, PACK, OUT_CHUNKS[c]]
             if OUT_CHUNKS[c] < BANK:
                 return rotating(shape, F32, "placed", 4)
-            return tenant(shape, F32, (("big0", "big1"), ("raw1", "raw4"), ("sine0", "sine1"))[c % 2][g])
+            return tenant(shape, F32, (("big0", "big1"), ("raw1", "raw4"), ("sine0", "sine1"))[c % 3][g])
 
         def fill_bank(y, g, slots, c, c0, width):
             acc = bank("prod")
@@ -328,7 +326,7 @@ def tile_list_ocean_band_weave_kernel(
 
         def store_y(y, g, c, t0, t1):
             rows = out_0[g * K_PASS : (g + 1) * K_PASS, starts[c] : starts[c] + OUT_CHUNKS[c]]
-            nc.scalar.dma_start(rows.rearrange("(p t) c -> p t c", t=PACK)[:, t0:t1, :], y[:, t0:t1, :])
+            nc.sync.dma_start(rows.rearrange("(p t) c -> p t c", t=PACK)[:, t0:t1, :], y[:, t0:t1, :])
 
         def make_y(c, g):
             c0, width = starts[c], OUT_CHUNKS[c]
@@ -339,54 +337,55 @@ def tile_list_ocean_band_weave_kernel(
             store_y(y, g, c, 0, PACK)
             return y
 
-        def weave_y(y, at, width):
+        def weave_y(y, shared):
+            width = y.shape[2]
             woven = rotating([P, width * PACK], BF16, "rounded", 4)
-            nc.vector.tensor_copy(
-                out=woven[:].rearrange("p (c i t) -> p c t i", i=4, t=PACK),
-                in_=y[:, :, at : at + width].rearrange("p t (c i) -> p c t i", i=4),
-            )
+            dst = woven[:].rearrange("p (c i t) -> p c t i", i=4, t=PACK)
+            src = y[:].rearrange("p t (c i) -> p c t i", i=4)
+            cut = width // 8 if shared else width // 4
+            nc.vector.tensor_copy(out=dst[:, :cut], in_=src[:, :cut])
+            if shared:
+                nc.scalar.copy(out=dst[:, cut:], in_=src[:, cut:])
             return woven
 
         def make_planes(c, ys):
-            width = min(BANK, OUT_CHUNKS[c])
-            parts = [(g, c0) for g in groups for c0 in range(starts[c], starts[c] + OUT_CHUNKS[c], BANK)]
-            for pair in range(0, len(parts), 2):
-                woven = [weave_y(ys[g], c0 - starts[c], width) for g, c0 in parts[pair : pair + 2]]
-                for (g, c0), tile in zip(parts[pair : pair + 2], woven):
-                    cols = slice(c0, c0 + width)
-                    nc.vector.quantize_mx(
-                        out=y_w[:, g, cols].bitcast(FP8X4), scales=y_s[4 * g : P, cols], in_=tile[:]
-                    )
+            cols = slice(starts[c], starts[c] + OUT_CHUNKS[c])
+            woven = [weave_y(ys[g], (c, g) == (chunks - 1, 1)) for g in groups]
+            for g in groups:
+                nc.vector.quantize_mx(
+                    out=y_w[:, g, cols].bitcast(FP8X4), scales=y_s[4 * g : P, cols], in_=woven[g][:]
+                )
+            if cols.stop % BANK == 0:
+                store_words(slice(cols.stop - BANK, cols.stop))
 
-        def store_words(g, cols):
+        def store_words(cols):
             nc.sync.dma_start(
-                out_1[g, :, cols, :].rearrange("p m t -> p (m t)").bitcast(I32), y_w[:, g, cols].bitcast(I32)
+                out_1[:, :, cols, :].rearrange("g p m t -> p g (m t)").bitcast(I32), y_w[:, :, cols].bitcast(I32)
             )
+
+        def store_scales(queues, cols):
+            words = slice(cols.start // 4, cols.stop // 4)
+            for q in range(QUADS):
+                queues[q % len(queues)].dma_start(
+                    out_2.bitcast(I32)[:, 4 * q : 4 * q + 4, words],
+                    y_s[32 * q : 32 * q + 8, :].bitcast(I32)[:, words],
+                )
+
+        def make_z(c):
+            quantize_z(*pieces[c], weave_z(*pieces[c]))
 
         turn_page(PAGES - 1, *pieces[0])
         turn_page(PAGES - 1, *pieces[1])
-        quantize_z(*pieces[0], weave_z(*pieces[0]))
-        for piece in pieces[2:]:
-            turn_page(PAGES - 1, *piece)
+        make_z(0)
+        turn_page(PAGES - 1, *pieces[2])
         ys = [[make_y(0, g) for g in groups]]
-        ahead = weave_z(*pieces[1])
-        for i in range(1, len(pieces)):
-            woven_z = ahead
-            if i + 1 < len(pieces):
-                ahead = weave_z(*pieces[i + 1])
-            quantize_z(*pieces[i], woven_z)
-            if i < chunks - 1:
-                ys.append([make_y(i, g) for g in groups])
-            else:
-                ys.append([make_y(chunks - 1, g) for g in groups])
-            make_planes(i - 1, ys[i - 1])
-            if starts[i] % BANK == 0:
-                for g in groups:
-                    store_words(g, slice(starts[i] - BANK, starts[i]))
+        make_z(1)
+        for c in range(1, chunks):
+            if c + 1 < chunks:
+                make_z(c + 1)
+            if c + 2 < chunks:
+                turn_page(PAGES - 1, *pieces[c + 2])
+            ys.append([make_y(c, g) for g in groups])
+            make_planes(c - 1, ys[c - 1])
         make_planes(chunks - 1, ys[-1])
-        for g in groups:
-            store_words(g, slice(T2 - BANK, T2))
-        for q in range(QUADS):
-            (nc.scalar, nc.sync)[q % 2].dma_start(
-                out_2.bitcast(I32)[:, 4 * q : 4 * q + 4, :], y_s[32 * q : 32 * q + 8, :].bitcast(I32)
-            )
+        store_scales((nc.scalar, nc.sync), slice(0, T2))

@@ -23,7 +23,7 @@ K_PASS = P * PACK
 BANK = 512
 QUADS = 4
 H2_SLICE = 256
-OUT_CHUNKS = (256, 256, 512, 512, 512)
+Z_PIECES = (256, 256, 512, 512, 512)
 PAGES = H // P
 
 
@@ -95,15 +95,17 @@ def tile_list_ocean_band_weave_kernel(
         list4 = load_list(offs4, "list4")
         wg2_sb = held([P, S], F32, "wg2_sb")
         nc.sync.dma_start(wg2_sb[:], wg2)
-        w1_raw = tenant([P, K // K_PASS, PACK, H], F32, "raw1")
-        nc.sync.dma_start(w1_raw[:], w1.rearrange("(a p j) c -> p a j c", p=P, j=PACK))
+        w1_raw = [tenant([P, PACK, H], F32, "raw1_%d" % a) for a in range(K // K_PASS)]
+        for a in range(K // K_PASS):
+            nc.sync.dma_start(w1_raw[a][:], w1[a * K_PASS : (a + 1) * K_PASS].rearrange("(p j) c -> p j c", j=PACK))
         w2_w = held([P, K // K_PASS, 2 * H], U8, "w2_w")
         nc.sync.dma_start(w2_w[:].bitcast(I32), w2_words.bitcast(I32).rearrange("a p c -> p a c"))
         list3 = load_list(offs3, "list3")
         wg1_sb = held([P, S], F32, "wg1_sb")
         nc.sync.dma_start(wg1_sb[:], wg1)
-        w4_raw = tenant([P, PACK, N], F32, "raw4")
-        nc.sync.dma_start(w4_raw[:], w4.rearrange("(p j) c -> p j c", j=PACK))
+        w4_raw = [tenant([P, PACK, BANK], F32, "raw4_%d" % g) for g in range(N // BANK)]
+        for g in range(N // BANK):
+            nc.sync.dma_start(w4_raw[g][:], w4[:, g * BANK : (g + 1) * BANK].rearrange("(p j) c -> p j c", j=PACK))
         w2_s = held([P, K // K_PASS, H], U8, "w2_s")
         nc.vector.memset(w2_s[:].bitcast(I32), 0)
         for q in range(QUADS):
@@ -186,7 +188,7 @@ def tile_list_ocean_band_weave_kernel(
 
         def quantize_w1(a):
             rounded = round_block(
-                w1_raw[:, a].rearrange("p j (c i) -> p c j i", i=4),
+                w1_raw[a][:].rearrange("p j (c i) -> p c j i", i=4),
                 lambda ap: ap.rearrange("p (c i j) -> p c j i", i=4, j=PACK),
             )
             nc.vector.quantize_mx(out=w1_w[:, a, :].bitcast(FP8X4), scales=w1_s[:, a, :], in_=rounded[:])
@@ -243,7 +245,7 @@ def tile_list_ocean_band_weave_kernel(
                     nc.vector.tensor_tensor(pages[b - 1][:].indirect(list3[:]), h1[b - 1][:], wg1_sb[:], MULT)
         w4_rounded = [
             round_block(
-                w4_raw[:, :, g * BANK : (g + 1) * BANK].rearrange("p j (m t) -> p m j t", t=PACK),
+                w4_raw[g][:].rearrange("p j (m t) -> p m j t", t=PACK),
                 lambda ap: ap.rearrange("p (t m j) -> p m j t", t=PACK, j=PACK),
             )
             for g in range(N // BANK)
@@ -256,112 +258,121 @@ def tile_list_ocean_band_weave_kernel(
             cols = slice(g * BANK, (g + 1) * BANK)
             nc.vector.quantize_mx(out=w4_w[:, cols].bitcast(FP8X4), scales=w4_s[:, cols], in_=w4_rounded[g][:])
 
-        across = [rotating([P, BANK // P, 2, P, 2], BF16, "turned", 4) for c in range(T2 // BANK)]
+        pieces = [(sum(Z_PIECES[:i]), Z_PIECES[i]) for i in range(len(Z_PIECES))]
+        across = []
+        for i, (c0, width) in enumerate(pieces):
+            shape = [P, width // P, 2, P, 2]
+            if width < BANK:
+                across.append(held(shape, BF16, "across%d" % i))
+            else:
+                across.append(rotating(shape, BF16, "turned", 4))
 
-        def turn_page(b, c0, width):
-            turned = bank("turn")
-            tiles = width // P
-            first = (c0 % BANK) // P
-            for i in range(tiles):
-                nc.tensor.transpose(turned[:, i * P : (i + 1) * P], pages[b][:, c0 + i * P : c0 + (i + 1) * P], ident[:])
+        def turn_out(b, i, turned):
             nc.scalar.copy(
-                out=across[c0 // BANK][:, first : first + tiles, :, 32 * b : 32 * (b + 1), :],
-                in_=turned[:, 0:width].rearrange("c (i q u e) -> c i u q e", q=32, u=2, e=2),
+                out=across[i][:, :, :, 32 * b : 32 * (b + 1), :],
+                in_=turned.rearrange("c (i q u e) -> c i u q e", q=32, u=2, e=2),
             )
 
-        for b in range(PAGES - 1):
-            for c0 in range(0, T2, BANK):
-                turn_page(b, c0, BANK)
+        def turn_page(b, group):
+            turned = bank("turn")
+            c0 = pieces[group[0]][0]
+            for i in group:
+                at, width = pieces[i]
+                for col in range(at, at + width, P):
+                    nc.tensor.transpose(turned[:, col - c0 : col - c0 + P], pages[b][:, col : col + P], ident[:])
+            for i in group:
+                at, width = pieces[i]
+                turn_out(b, i, turned[:, at - c0 : at - c0 + width])
 
-        z_w = held([P, T2], U32, "z_w")
+        blocks = range(T2 // BANK)
+        in_block = [[i for i, (c0, width) in enumerate(pieces) if c0 // BANK == k] for k in blocks]
+        for b in range(PAGES - 1):
+            for k in blocks:
+                turn_page(b, in_block[k])
+
+        z_w = tenant([P, T2], U32, "big2")
         z_s = held([P, T2], U8, "z_s")
         y_s = held([P, T2], U8, "y_s")
         y_w = held([P, N // K_PASS, T2], U32, "y_w")
-        chunks = len(OUT_CHUNKS)
         groups = range(N // K_PASS)
-        starts = [sum(OUT_CHUNKS[:c]) for c in range(chunks)]
-        pieces = [(c0, min(BANK, starts[c] + OUT_CHUNKS[c] - c0)) for c in range(chunks)
-                  for c0 in range(starts[c], starts[c] + OUT_CHUNKS[c], BANK)]
 
-        def weave_z(c0, width):
-            pairs = across[c0 // BANK][:].rearrange("c i u p e -> c (i u p e)").bitcast(F32)
+        def make_z(i):
+            c0, width = pieces[i]
+            pairs = across[i][:].rearrange("c i u p e -> c (i u p e)").bitcast(F32)
             woven = rotating([P, width * PACK], BF16, "z_woven", 2)
-            for i0 in range(0, width // P, 2):
+            per = min(2, width // P)
+            for i0 in range(0, width // P, per):
                 back = bank("turn")
-                for iu in range(4):
-                    at = (2 * ((c0 % BANK) // P + i0) + iu) * P
+                for iu in range(2 * per):
+                    at = (2 * i0 + iu) * P
                     nc.tensor.transpose(back[:, iu * P : (iu + 1) * P], pairs[:, at : at + P], ident[:])
-                dst = woven[:].bitcast(F32)[:, 2 * i0 * P : 2 * (i0 + 2) * P]
+                dst = woven[:].bitcast(F32)[:, 2 * i0 * P : 2 * (i0 + per) * P]
                 nc.vector.tensor_copy(
-                    out=dst.rearrange("p (i c u) -> p i c u", i=2, u=2),
-                    in_=back[:].rearrange("p (i u c) -> p i c u", i=2, u=2),
+                    out=dst.rearrange("p (i c u) -> p i c u", i=per, u=2),
+                    in_=back[:, 0 : 2 * per * P].rearrange("p (i u c) -> p i c u", i=per, u=2),
                 )
-            return woven
-
-        def quantize_z(c0, width, woven):
             cols = slice(c0, c0 + width)
             nc.vector.quantize_mx(out=z_w[:, cols].bitcast(FP8X4), scales=z_s[:, cols], in_=woven[:])
 
-        def result_tile(c, g):
-            shape = [P, PACK, OUT_CHUNKS[c]]
-            if OUT_CHUNKS[c] < BANK:
-                return rotating(shape, F32, "placed", 4)
-            return tenant(shape, F32, (("big0", "big1"), ("raw1", "raw4"), ("sine0", "sine1"))[c % 3][g])
+        homes = (("big0", "big1"), ("raw1_0", "raw1_1"), ("raw4_0", "raw4_1"), ("sine0", "sine1"))
+        ys = {}
 
-        def fill_bank(y, g, slots, c, c0, width):
-            acc = bank("prod")
-            for i, t in enumerate(slots):
-                at = g * BANK + t * P
-                nc.tensor.matmul_mx(
-                    out=acc[:, i * width : (i + 1) * width],
-                    lhsT=w4_w[:, at : at + P].bitcast(FP8X4), lhsT_scale=w4_s[:, at : at + P],
-                    rhs=z_w[:, c0 : c0 + width].bitcast(FP8X4), rhs_scale=z_s[:, c0 : c0 + width],
-                    start=True, stop=True,
-                )
-            at = c0 - starts[c]
-            nc.scalar.copy(
-                out=y[:, slots[0] : slots[-1] + 1, at : at + width],
-                in_=acc[:].rearrange("p (t c) -> p t c", c=width),
-            )
+        def result_tile(k, g):
+            if (k, g) not in ys:
+                ys[k, g] = tenant([P, PACK, BANK], F32, homes[k][g])
+            return ys[k, g]
 
-        def store_y(y, g, c, t0, t1):
-            rows = out_0[g * K_PASS : (g + 1) * K_PASS, starts[c] : starts[c] + OUT_CHUNKS[c]]
-            nc.sync.dma_start(rows.rearrange("(p t) c -> p t c", t=PACK)[:, t0:t1, :], y[:, t0:t1, :])
-
-        def make_y(c, g):
-            c0, width = starts[c], OUT_CHUNKS[c]
-            y = result_tile(c, g)
+        def fill(g, c0, width, stores):
+            y = result_tile(c0 // BANK, g)
             share = BANK // width
             for t0 in range(0, PACK, share):
-                fill_bank(y, g, range(t0, t0 + share), c, c0, width)
-            store_y(y, g, c, 0, PACK)
-            return y
+                acc = bank("prod")
+                for i in range(share):
+                    at = g * BANK + (t0 + i) * P
+                    nc.tensor.matmul_mx(
+                        out=acc[:, i * width : (i + 1) * width],
+                        lhsT=w4_w[:, at : at + P].bitcast(FP8X4), lhsT_scale=w4_s[:, at : at + P],
+                        rhs=z_w[:, c0 : c0 + width].bitcast(FP8X4), rhs_scale=z_s[:, c0 : c0 + width],
+                        start=True, stop=True,
+                    )
+                at = c0 % BANK
+                nc.scalar.copy(
+                    out=y[:, t0 : t0 + share, at : at + width],
+                    in_=acc[:].rearrange("p (t c) -> p t c", c=width),
+                )
+                done = t0 + share
+                if done % (PACK // stores) == 0:
+                    store_y(g, c0, width, done - PACK // stores, done)
 
-        def weave_y(y, shared):
-            width = y.shape[2]
+        def store_y(g, c0, width, t0, t1):
+            rows = out_0[g * K_PASS : (g + 1) * K_PASS, c0 : c0 + width].rearrange("(p t) c -> p t c", t=PACK)
+            at = c0 % BANK
+            nc.sync.dma_start(rows[:, t0:t1, :], ys[c0 // BANK, g][:, t0:t1, at : at + width])
+
+        def weave_y(g, c0, width, by_scalar):
+            at = c0 % BANK
             woven = rotating([P, width * PACK], BF16, "rounded", 4)
             dst = woven[:].rearrange("p (c i t) -> p c t i", i=4, t=PACK)
-            src = y[:].rearrange("p t (c i) -> p c t i", i=4)
-            cut = width // 8 if shared else width // 4
-            nc.vector.tensor_copy(out=dst[:, :cut], in_=src[:, :cut])
-            if shared:
+            src = ys[c0 // BANK, g][:, :, at : at + width].rearrange("p t (c i) -> p c t i", i=4)
+            cut = (width - by_scalar) // 4
+            if cut > 0:
+                nc.vector.tensor_copy(out=dst[:, :cut], in_=src[:, :cut])
+            if by_scalar > 0:
                 nc.scalar.copy(out=dst[:, cut:], in_=src[:, cut:])
             return woven
 
-        def make_planes(c, ys):
-            cols = slice(starts[c], starts[c] + OUT_CHUNKS[c])
-            woven = [weave_y(ys[g], (c, g) == (chunks - 1, 1)) for g in groups]
+        def make_planes(c0, width, by_scalar=(0, 0)):
+            cols = slice(c0, c0 + width)
+            woven = [weave_y(g, c0, width, by_scalar[g]) for g in groups]
             for g in groups:
                 nc.vector.quantize_mx(
                     out=y_w[:, g, cols].bitcast(FP8X4), scales=y_s[4 * g : P, cols], in_=woven[g][:]
                 )
             if cols.stop % BANK == 0:
-                store_words(slice(cols.stop - BANK, cols.stop))
-
-        def store_words(cols):
-            nc.sync.dma_start(
-                out_1[:, :, cols, :].rearrange("g p m t -> p g (m t)").bitcast(I32), y_w[:, :, cols].bitcast(I32)
-            )
+                cols = slice(cols.stop - BANK, cols.stop)
+                nc.sync.dma_start(
+                    out_1[:, :, cols, :].rearrange("g p m t -> p g (m t)").bitcast(I32), y_w[:, :, cols].bitcast(I32)
+                )
 
         def store_scales(queues, cols):
             words = slice(cols.start // 4, cols.stop // 4)
@@ -371,21 +382,29 @@ def tile_list_ocean_band_weave_kernel(
                     y_s[32 * q : 32 * q + 8, :].bitcast(I32)[:, words],
                 )
 
-        def make_z(c):
-            quantize_z(*pieces[c], weave_z(*pieces[c]))
+        def make_y(c0, width, stores=(1, 1)):
+            for g in groups:
+                fill(g, c0, width, stores[g])
 
-        turn_page(PAGES - 1, *pieces[0])
-        turn_page(PAGES - 1, *pieces[1])
+        last = PAGES - 1
+        turn_page(last, [0])
+        turn_page(last, [1])
         make_z(0)
-        turn_page(PAGES - 1, *pieces[2])
-        ys = [[make_y(0, g) for g in groups]]
+        turn_page(last, [2])
         make_z(1)
-        for c in range(1, chunks):
-            if c + 1 < chunks:
-                make_z(c + 1)
-            if c + 2 < chunks:
-                turn_page(PAGES - 1, *pieces[c + 2])
-            ys.append([make_y(c, g) for g in groups])
-            make_planes(c - 1, ys[c - 1])
-        make_planes(chunks - 1, ys[-1])
+        turn_page(last, [3])
+        turn_page(last, [4])
+        make_y(*pieces[0], stores=(2, 1))
+        make_z(2)
+        make_y(*pieces[1])
+        make_planes(*pieces[0])
+        make_z(3)
+        make_y(*pieces[2], stores=(2, 2))
+        make_planes(*pieces[1])
+        make_z(4)
+        make_y(*pieces[3])
+        make_planes(*pieces[2])
+        make_y(*pieces[4])
+        make_planes(*pieces[3])
+        make_planes(*pieces[4], by_scalar=(0, BANK // 2))
         store_scales((nc.scalar, nc.sync), slice(0, T2))

@@ -23,7 +23,7 @@ K_PASS = P * PACK
 BANK = 512
 QUADS = 4
 H2_SLICE = 256
-Z_PIECES = (256, 256, 512, 512, 512)
+Z_PIECES = (128, 128, 256, 512, 512, 512)
 PAGES = H // P
 
 
@@ -267,14 +267,15 @@ def tile_list_ocean_band_weave_kernel(
             else:
                 across.append(rotating(shape, BF16, "turned", 4))
 
-        def turn_out(b, i, turned):
-            nc.scalar.copy(
+        def turn_out(b, i, turned, copy):
+            copy(
                 out=across[i][:, :, :, 32 * b : 32 * (b + 1), :],
                 in_=turned.rearrange("c (i q u e) -> c i u q e", q=32, u=2, e=2),
             )
 
-        def turn_page(b, group):
-            turned = bank("turn")
+        def turn_page(b, group, turned=None, copy=nc.scalar.copy):
+            if turned is None:
+                turned = bank("turn")
             c0 = pieces[group[0]][0]
             for i in group:
                 at, width = pieces[i]
@@ -282,13 +283,22 @@ def tile_list_ocean_band_weave_kernel(
                     nc.tensor.transpose(turned[:, col - c0 : col - c0 + P], pages[b][:, col : col + P], ident[:])
             for i in group:
                 at, width = pieces[i]
-                turn_out(b, i, turned[:, at - c0 : at - c0 + width])
+                turn_out(b, i, turned[:, at - c0 : at - c0 + width], copy)
+            return turned
+
+        def warm_up(acc, passes):
+            for i in range(passes):
+                nc.tensor.matmul_mx(
+                    out=acc[:], lhsT=v2_w[:, 0:P].bitcast(FP8X4), lhsT_scale=v2_s[:, 0:P],
+                    rhs=w3_w[:, 0:H].bitcast(FP8X4), rhs_scale=w3_s[:, 0:H], start=(i == 0), stop=(i == passes - 1),
+                )
 
         blocks = range(T2 // BANK)
         in_block = [[i for i, (c0, width) in enumerate(pieces) if c0 // BANK == k] for k in blocks]
         for b in range(PAGES - 1):
             for k in blocks:
-                turn_page(b, in_block[k])
+                turned = turn_page(b, in_block[k])
+        warm_up(bank("turn"), 8)
 
         z_w = tenant([P, T2], U32, "big2")
         z_s = held([P, T2], U8, "z_s")
@@ -341,7 +351,7 @@ def tile_list_ocean_band_weave_kernel(
                     in_=acc[:].rearrange("p (t c) -> p t c", c=width),
                 )
                 done = t0 + share
-                if done % (PACK // stores) == 0:
+                if stores and done % (PACK // stores) == 0:
                     store_y(g, c0, width, done - PACK // stores, done)
 
         def store_y(g, c0, width, t0, t1):
@@ -388,23 +398,27 @@ def tile_list_ocean_band_weave_kernel(
 
         last = PAGES - 1
         turn_page(last, [0])
-        turn_page(last, [1])
+        turn_page(last, [1, 2])
         make_z(0)
-        turn_page(last, [2])
-        make_z(1)
         turn_page(last, [3])
-        turn_page(last, [4])
-        make_y(*pieces[0], stores=(2, 1))
+        make_z(1)
         make_z(2)
-        make_y(*pieces[1])
-        make_planes(*pieces[0])
+        turn_page(last, [4])
+        make_y(*pieces[0])
         make_z(3)
-        make_y(*pieces[2], stores=(2, 2))
-        make_planes(*pieces[1])
+        for g in groups:
+            fill(g, *pieces[1], 0)
+            fill(g, *pieces[2], 0)
+            store_y(g, P, BANK - P, 0, PACK // 2)
+            store_y(g, P, BANK - P, PACK // 2, PACK)
+        turn_page(last, [5])
         make_z(4)
-        make_y(*pieces[3])
-        make_planes(*pieces[2])
+        make_y(*pieces[3], stores=(2, 2))
+        make_planes(0, BANK)
+        make_z(5)
         make_y(*pieces[4])
-        make_planes(*pieces[3])
-        make_planes(*pieces[4], by_scalar=(0, BANK // 2))
+        make_planes(BANK, BANK)
+        make_y(*pieces[5])
+        make_planes(2 * BANK, BANK)
+        make_planes(3 * BANK, BANK, by_scalar=(0, BANK // 2))
         store_scales((nc.scalar, nc.sync), slice(0, T2))

@@ -70,16 +70,18 @@ def tile_list_ocean_band_weave_kernel(
                 )
             return tile
 
-        def round_block(src, order):
+        def round_block(src, order, first=nc.scalar.copy):
             rounded = rotating([P, BANK * PACK], BF16, "rounded", 4)
             dst = order(rounded[:])
             half = src.shape[1] // 2
-            for m0 in (0, half):
-                nc.scalar.copy(out=dst[:, m0 : m0 + half], in_=src[:, m0 : m0 + half])
+            first(out=dst[:, :half], in_=src[:, :half])
+            nc.scalar.copy(out=dst[:, half:], in_=src[:, half:])
             return rounded
 
         list2 = load_list(offs2, "list2")
         tab2_s = load_plane(nc.sync, tab2_scales[0], "tab2_s")
+        wg1_sb = held([P, S], F32, "wg1_sb")
+        nc.sync.dma_start(wg1_sb[:], wg1)
         tab2_w = load_words(nc.sync, tab2_words[0], "big2")
         w3_s = load_plane(nc.sync, w3_scales[0], "w3_s")
         w3_w = load_words(nc.sync, w3_words[0], "w3_w")
@@ -101,8 +103,6 @@ def tile_list_ocean_band_weave_kernel(
         w2_w = held([P, K // K_PASS, 2 * H], U8, "w2_w")
         nc.sync.dma_start(w2_w[:].bitcast(I32), w2_words.bitcast(I32).rearrange("a p c -> p a c"))
         list3 = load_list(offs3, "list3")
-        wg1_sb = held([P, S], F32, "wg1_sb")
-        nc.sync.dma_start(wg1_sb[:], wg1)
         w4_raw = [tenant([P, PACK, BANK], F32, "raw4_%d" % g) for g in range(N // BANK)]
         for g in range(N // BANK):
             nc.sync.dma_start(w4_raw[g][:], w4[:, g * BANK : (g + 1) * BANK].rearrange("(p j) c -> p j c", j=PACK))
@@ -122,6 +122,20 @@ def tile_list_ocean_band_weave_kernel(
         gain_p2 = held([P, PAGES], F32, "gain_p2")
         nc.gpsimd.tensor_scalar(out=gain_m2[:], in0=gain_sb[:], scalar1=-2.0, scalar2=None, op0=MULT)
         nc.gpsimd.tensor_scalar(out=gain_p2[:], in0=gain_sb[:], scalar1=2.0, scalar2=None, op0=MULT)
+
+        gain_sign = held([P, PAGES], F32, "gain_sign")
+        gain_abs = held([P, PAGES], F32, "gain_abs")
+        nc.scalar.activation(out=gain_sign[:], in_=gain_sb[:], func=ACT.Sign)
+        nc.scalar.activation(out=gain_abs[:], in_=gain_sb[:], func=ACT.Abs)
+        ln_gain = held([P, PAGES], F32, "ln_gain")
+        nc.scalar.activation(out=ln_gain[:], in_=gain_abs[:], func=ACT.Ln, bias=2.0**-64)
+
+        ln_wg = held([P, S], F32, "ln_wg")
+        for c0 in range(0, S, BANK):
+            turned = bank("turn")
+            for at in range(0, BANK, P):
+                nc.tensor.transpose(turned[:, at : at + P], wg1_sb[:, c0 + at : c0 + at + P], ident[:])
+            nc.scalar.activation(out=ln_wg[:, c0 : c0 + BANK], in_=turned[:], func=ACT.Ln)
 
         v2_s = held([P, S], U8, "v2_s")
         v2_w = held([P, S], U32, "v2_w")
@@ -190,6 +204,7 @@ def tile_list_ocean_band_weave_kernel(
             rounded = round_block(
                 w1_raw[a][:].rearrange("p j (c i) -> p c j i", i=4),
                 lambda ap: ap.rearrange("p (c i j) -> p c j i", i=4, j=PACK),
+                nc.vector.tensor_copy if a == 0 else nc.scalar.copy,
             )
             nc.vector.quantize_mx(out=w1_w[:, a, :].bitcast(FP8X4), scales=w1_s[:, a, :], in_=rounded[:])
 
@@ -218,31 +233,63 @@ def tile_list_ocean_band_weave_kernel(
             return acc
 
         halves = [slice(h * BANK, (h + 1) * BANK) for h in range(S // BANK)]
+        tiles_per_half = BANK // P
         sines = [tenant([P, 2, S], F32, "sine%d" % i) for i in range(PAGES // 2)]
-        h1 = []
-        for pair in range(PAGES // 2):
-            for b in (2 * pair, 2 * pair + 1):
-                for cols in halves:
-                    phase = first_product(lambda a, b: w1_w[:, a, b * P : (b + 1) * P].bitcast(FP8X4), w1_s, b, cols)
-                    nc.scalar.activation(out=sines[pair][:, b % 2, cols], in_=phase[:], func=ACT.Sin)
-                if b == 0:
-                    place_slice(3)
-            for b in (2 * pair, 2 * pair + 1):
-                if b < PAGES - 1:
-                    h1.append(rotating([P, S], F32, "placed", 4))
-                else:
-                    h1.append(tenant([P, S], F32, "last"))
-                for cols in halves:
-                    level = first_product(
-                        lambda a, b: w2_w[:, a, 2 * b * P : 2 * (b + 1) * P].bitcast(FP4X4), w2_s, b, cols
+        levels = [tenant([P, tiles_per_half, H], F32, "raw1_%d" % h) for h in range(len(halves))]
+
+        def make_levels(h):
+            for i in range(tiles_per_half):
+                cols = slice(h * BANK + i * P, h * BANK + (i + 1) * P)
+                acc = bank("prod")
+                for a in range(K // K_PASS):
+                    nc.tensor.matmul_mx(
+                        out=acc[:], lhsT=v_w[a][:, cols].bitcast(FP8X4), lhsT_scale=v_s[:, a, cols],
+                        rhs=w2_w[:, a, :].bitcast(FP4X4), rhs_scale=w2_s[:, a, :],
+                        start=(a == 0), stop=(a == K // K_PASS - 1),
                     )
-                    nc.scalar.activation(out=h1[b][:, cols], in_=level[:], func=ACT.Exp)
-                nc.vector.scalar_tensor_tensor(
-                    out=h1[b][:], in0=h1[b][:], scalar=gain_sb[:, b : b + 1],
-                    in1=sines[pair][:, b % 2, :], op0=MULT, op1=MULT,
+                nc.scalar.copy(out=levels[h][:, i, :], in_=acc[:])
+
+        def make_sines(b):
+            for cols in halves:
+                phase = first_product(lambda a, b: w1_w[:, a, b * P : (b + 1) * P].bitcast(FP8X4), w1_s, b, cols)
+                nc.scalar.activation(
+                    out=sines[b // 2][:, b % 2, cols], in_=phase[:], func=ACT.Sin, scale=gain_sign[:, b : b + 1]
                 )
-                if b > 0:
-                    nc.vector.tensor_tensor(pages[b - 1][:].indirect(list3[:]), h1[b - 1][:], wg1_sb[:], MULT)
+
+        def make_amp(b, h):
+            total = bank("turn")
+            for i in range(tiles_per_half):
+                at = h * BANK + i * P
+                terms = (levels[h][:, i, b * P : (b + 1) * P], ln_wg[:, at : at + P])
+                for c, term in enumerate(terms):
+                    nc.tensor.matmul(
+                        total[:, i * P : (i + 1) * P], term, ident[:], is_transpose=True, start=(c == 0), stop=(c == 1)
+                    )
+            nc.scalar.activation(out=amps[b][:, halves[h]], in_=total[:], func=ACT.Exp, bias=ln_gain[:, b : b + 1])
+
+        def place(b, cols):
+            picks = list3[:, cols.start // 16 : cols.stop // 16]
+            nc.vector.tensor_tensor(pages[b][:].indirect(picks), sines[b // 2][:, b % 2, cols], amps[b][:, cols], MULT)
+
+        make_levels(0)
+        place_slice(3)
+        amps = [rotating([P, S], F32, "placed", 4) for b in range(PAGES - 1)] + [tenant([P, S], F32, "last")]
+        make_sines(0)
+        make_sines(1)
+        for b in (0, 1):
+            make_amp(b, 0)
+            place(b, halves[0])
+        make_levels(1)
+        for b in (0, 1):
+            make_amp(b, 1)
+            place(b, halves[1])
+        make_sines(2)
+        make_sines(3)
+        for b in (2, 3):
+            for h in range(len(halves)):
+                make_amp(b, h)
+            if b < PAGES - 1:
+                place(b, slice(0, S))
         w4_rounded = [
             round_block(
                 w4_raw[g][:].rearrange("p j (m t) -> p m j t", t=PACK),
@@ -250,7 +297,7 @@ def tile_list_ocean_band_weave_kernel(
             )
             for g in range(N // BANK)
         ]
-        nc.vector.tensor_tensor(pages[PAGES - 1][:].indirect(list3[:]), h1[PAGES - 1][:], wg1_sb[:], MULT)
+        place(PAGES - 1, slice(0, S))
 
         w4_w = tenant([P, N], U32, "last")
         w4_s = held([P, N], U8, "w4_s")
@@ -298,7 +345,6 @@ def tile_list_ocean_band_weave_kernel(
         for b in range(PAGES - 1):
             for k in blocks:
                 turned = turn_page(b, in_block[k])
-        warm_up(bank("turn"), 8)
 
         z_w = tenant([P, T2], U32, "big2")
         z_s = held([P, T2], U8, "z_s")

@@ -25,6 +25,7 @@ QUADS = 4
 H2_SLICE = 256
 Z_PIECES = (128, 128, 256, 512, 512, 512)
 PAGES = H // P
+EARLY = 256
 
 
 def tile_list_ocean_band_weave_kernel(
@@ -74,6 +75,10 @@ def tile_list_ocean_band_weave_kernel(
             rounded = rotating([P, BANK * PACK], BF16, "rounded", 4)
             dst = order(rounded[:])
             half = src.shape[1] // 2
+            if half == 1:
+                first(out=dst[:, 0], in_=src[:, 0])
+                nc.scalar.copy(out=dst[:, 1], in_=src[:, 1])
+                return rounded
             first(out=dst[:, :half], in_=src[:, :half])
             nc.scalar.copy(out=dst[:, half:], in_=src[:, half:])
             return rounded
@@ -83,7 +88,12 @@ def tile_list_ocean_band_weave_kernel(
         wg1_sb = held([P, S], F32, "wg1_sb")
         nc.sync.dma_start(wg1_sb[:], wg1)
         tab2_w = load_words(nc.sync, tab2_words[0], "big2")
-        w3_s = load_plane(nc.sync, w3_scales[0], "w3_s")
+        w3_s = held([P, 2 * H], U8, "w3_s")
+        nc.gpsimd.memset(w3_s[:].bitcast(I32), 0)
+        for q in range(QUADS):
+            nc.sync.dma_start(
+                w3_s[32 * q : 32 * q + 4, :].bitcast(I32), w3_scales[0].bitcast(I32)[4 * q : 4 * q + 4, :]
+            )
         w3_w = load_words(nc.sync, w3_words[0], "w3_w")
         list1 = load_list(offs, "list1")
         tab_s = held([P, T], U8, "tab_s")
@@ -97,9 +107,11 @@ def tile_list_ocean_band_weave_kernel(
         list4 = load_list(offs4, "list4")
         wg2_sb = held([P, S], F32, "wg2_sb")
         nc.sync.dma_start(wg2_sb[:], wg2)
-        w1_raw = [tenant([P, PACK, H], F32, "raw1_%d" % a) for a in range(K // K_PASS)]
-        for a in range(K // K_PASS):
-            nc.sync.dma_start(w1_raw[a][:], w1[a * K_PASS : (a + 1) * K_PASS].rearrange("(p j) c -> p j c", j=PACK))
+        w1_raw = [tenant([P, K // K_PASS, PACK, H // 2], F32, "raw1_%d" % u) for u in range(2)]
+        for u in range(2):
+            for a in range(K // K_PASS):
+                rows = w1[a * K_PASS : (a + 1) * K_PASS, u * H // 2 : (u + 1) * H // 2]
+                nc.sync.dma_start(w1_raw[u][:, a], rows.rearrange("(p j) c -> p j c", j=PACK))
         w2_w = held([P, K // K_PASS, 2 * H], U8, "w2_w")
         nc.sync.dma_start(w2_w[:].bitcast(I32), w2_words.bitcast(I32).rearrange("a p c -> p a c"))
         list3 = load_list(offs3, "list3")
@@ -157,8 +169,8 @@ def tile_list_ocean_band_weave_kernel(
 
         pages = [held([P, T2], F32, "page%d" % b) for b in range(PAGES)]
 
-        w1_w = held([P, K // K_PASS, H], U32, "w1_w")
-        w1_s = held([P, K // K_PASS, H], U8, "w1_s")
+        w1_w = held([P, 2, H], U32, "w1_w")
+        w1_s = held([P, 2, H], U8, "w1_s")
         per_bank = BANK // H2_SLICE
         tiles_per_slice = H2_SLICE // P
         sums = {}
@@ -202,9 +214,8 @@ def tile_list_ocean_band_weave_kernel(
 
         def quantize_w1(a):
             rounded = round_block(
-                w1_raw[a][:].rearrange("p j (c i) -> p c j i", i=4),
-                lambda ap: ap.rearrange("p (c i j) -> p c j i", i=4, j=PACK),
-                nc.vector.tensor_copy if a == 0 else nc.scalar.copy,
+                w1_raw[a][:].rearrange("p a j (c i) -> p a c j i", i=4),
+                lambda ap: ap.rearrange("p (a c i j) -> p a c j i", a=2, i=4, j=PACK),
             )
             nc.vector.quantize_mx(out=w1_w[:, a, :].bitcast(FP8X4), scales=w1_s[:, a, :], in_=rounded[:])
 
@@ -216,9 +227,8 @@ def tile_list_ocean_band_weave_kernel(
         sines_of_tile(2, 0)
         place_slice(1)
         sines_of_tile(2, 1)
-        for a in range(K // K_PASS):
-            quantize_w1(a)
         place_slice(2)
+        quantize_w1(0)
         sines_of_tile(3, 0)
         sines_of_tile(3, 1)
 
@@ -226,7 +236,7 @@ def tile_list_ocean_band_weave_kernel(
             acc = bank("prod")
             for a in range(K // K_PASS):
                 nc.tensor.matmul_mx(
-                    out=acc[:], lhsT=words(a, b), lhsT_scale=scales[:, a, b * P : (b + 1) * P],
+                    out=acc[:], lhsT=words(a, b), lhsT_scale=scales(a, b),
                     rhs=v_w[a][:, cols].bitcast(FP8X4), rhs_scale=v_s[:, a, cols],
                     start=(a == 0), stop=(a == K // K_PASS - 1),
                 )
@@ -249,9 +259,16 @@ def tile_list_ocean_band_weave_kernel(
                     )
                 nc.scalar.copy(out=levels[h][:, i, :], in_=acc[:])
 
+        def w1_cols(a, b):
+            at = a * (H // 2) + (b % 2) * P
+            return slice(at, at + P)
+
         def make_sines(b):
             for cols in halves:
-                phase = first_product(lambda a, b: w1_w[:, a, b * P : (b + 1) * P].bitcast(FP8X4), w1_s, b, cols)
+                phase = first_product(
+                    lambda a, b: w1_w[:, b // 2, w1_cols(a, b)].bitcast(FP8X4),
+                    lambda a, b: w1_s[:, b // 2, w1_cols(a, b)], b, cols,
+                )
                 nc.scalar.activation(
                     out=sines[b // 2][:, b % 2, cols], in_=phase[:], func=ACT.Sin, scale=gain_sign[:, b : b + 1]
                 )
@@ -279,17 +296,19 @@ def tile_list_ocean_band_weave_kernel(
         for b in (0, 1):
             make_amp(b, 0)
             place(b, halves[0])
+        quantize_w1(1)
         make_levels(1)
         for b in (0, 1):
             make_amp(b, 1)
             place(b, halves[1])
         make_sines(2)
         make_sines(3)
-        for b in (2, 3):
-            for h in range(len(halves)):
-                make_amp(b, h)
-            if b < PAGES - 1:
-                place(b, slice(0, S))
+        make_amp(3, 0)
+        place(3, slice(0, EARLY))
+        make_amp(2, 0)
+        make_amp(2, 1)
+        place(2, slice(0, S))
+        make_amp(3, 1)
         w4_rounded = [
             round_block(
                 w4_raw[g][:].rearrange("p j (m t) -> p m j t", t=PACK),
@@ -297,7 +316,7 @@ def tile_list_ocean_band_weave_kernel(
             )
             for g in range(N // BANK)
         ]
-        place(PAGES - 1, slice(0, S))
+        place(PAGES - 1, slice(EARLY, S))
 
         w4_w = tenant([P, N], U32, "last")
         w4_s = held([P, N], U8, "w4_s")
@@ -342,9 +361,14 @@ def tile_list_ocean_band_weave_kernel(
 
         blocks = range(T2 // BANK)
         in_block = [[i for i, (c0, width) in enumerate(pieces) if c0 // BANK == k] for k in blocks]
-        for b in range(PAGES - 1):
+        for b in range(PAGES - 2):
             for k in blocks:
-                turned = turn_page(b, in_block[k])
+                turn_page(b, in_block[k])
+        emptied = []
+        for k in blocks:
+            emptied.append(turn_page(PAGES - 2, in_block[k]))
+            if k > 0:
+                warm_up(emptied[k - 1], 2)
 
         z_w = tenant([P, T2], U32, "big2")
         z_s = held([P, T2], U8, "z_s")
@@ -424,7 +448,11 @@ def tile_list_ocean_band_weave_kernel(
                 nc.vector.quantize_mx(
                     out=y_w[:, g, cols].bitcast(FP8X4), scales=y_s[4 * g : P, cols], in_=woven[g][:]
                 )
-            if cols.stop % BANK == 0:
+                if cols.stop == T2:
+                    nc.sync.dma_start(
+                        out_1[g, :, cols, :].rearrange("p m t -> p (m t)").bitcast(I32), y_w[:, g, cols].bitcast(I32)
+                    )
+            if cols.stop < T2:
                 cols = slice(cols.stop - BANK, cols.stop)
                 nc.sync.dma_start(
                     out_1[:, :, cols, :].rearrange("g p m t -> p g (m t)").bitcast(I32), y_w[:, :, cols].bitcast(I32)
@@ -444,6 +472,7 @@ def tile_list_ocean_band_weave_kernel(
 
         last = PAGES - 1
         turn_page(last, [0])
+        warm_up(emptied[-1], 2)
         turn_page(last, [1, 2])
         make_z(0)
         turn_page(last, [3])

@@ -61,14 +61,11 @@ def tile_list_ocean_band_weave_kernel(
             return tile
 
         def load_plane(queue, rows, name):
-            width = rows.shape[1]
-            tile = held([P, width], U8, name)
+            tile = held([P, rows.shape[1]], U8, name)
+            nc.gpsimd.memset(tile[:].bitcast(I32), 0)
             words = rows.bitcast(I32)
             for q in range(QUADS):
-                queue.dma_start(
-                    tile[32 * q : 32 * q + 32, :].bitcast(I32),
-                    words[4 * q : 4 * q + 4, :].unsqueeze(0).to_broadcast([8, 4, width // 4]),
-                )
+                queue.dma_start(tile[32 * q : 32 * q + 4, :].bitcast(I32), words[4 * q : 4 * q + 4, :])
             return tile
 
         def round_block(src, order, first=nc.scalar.copy):
@@ -83,27 +80,22 @@ def tile_list_ocean_band_weave_kernel(
             nc.scalar.copy(out=dst[:, half:], in_=src[:, half:])
             return rounded
 
-        list2 = load_list(offs2, "list2")
-        tab2_s = load_plane(nc.sync, tab2_scales[0], "tab2_s")
-        wg1_sb = held([P, S], F32, "wg1_sb")
-        nc.sync.dma_start(wg1_sb[:], wg1)
-        tab2_w = load_words(nc.sync, tab2_words[0], "big2")
-        w3_s = held([P, 2 * H], U8, "w3_s")
-        nc.gpsimd.memset(w3_s[:].bitcast(I32), 0)
-        for q in range(QUADS):
-            nc.sync.dma_start(
-                w3_s[32 * q : 32 * q + 4, :].bitcast(I32), w3_scales[0].bitcast(I32)[4 * q : 4 * q + 4, :]
-            )
-        w3_w = load_words(nc.sync, w3_words[0], "w3_w")
         list1 = load_list(offs, "list1")
         tab_s = held([P, T], U8, "tab_s")
         nc.sync.dma_start(tab_s[0:32, :].bitcast(I32), tab_scales.bitcast(I32).rearrange("a q c -> (a q) c"))
         nc.vector.memset(tab_s[32:64, :].bitcast(I32), 0)
         nc.vector.memset(tab_s[64:P, :].bitcast(I32), 0)
+        wg1_sb = held([P, S], F32, "wg1_sb")
+        nc.sync.dma_start(wg1_sb[:], wg1)
+        gain_rows = held([P, P], F32, "gain_rows")
+        nc.gpsimd.memset(gain_rows[:], 0.0)
+        nc.sync.dma_start(gain_rows[0:PAGES, :], gain.rearrange("(b p) -> b p", p=P))
+        list2 = load_list(offs2, "list2")
+        tab2_s = load_plane(nc.sync, tab2_scales[0], "tab2_s")
+        tab2_w = load_words(nc.sync, tab2_words[0], "big2")
+        w3_s = load_plane(nc.sync, w3_scales[0], "w3_s")
+        w3_w = load_words(nc.sync, w3_words[0], "w3_w")
         tab_w = [load_words(nc.sync, tab_words[a], "big%d" % a) for a in range(K // K_PASS)]
-        gain_sb = held([P, PAGES], F32, "gain_sb")
-        with nc.allow_non_contiguous_dma(reason="one gain value for each partition and page"):
-            nc.scalar.dma_start(gain_sb[:], gain.rearrange("(b p) -> p b", p=P))
         list4 = load_list(offs4, "list4")
         wg2_sb = held([P, S], F32, "wg2_sb")
         nc.sync.dma_start(wg2_sb[:], wg2)
@@ -125,20 +117,20 @@ def tile_list_ocean_band_weave_kernel(
                 w2_s[32 * q : 32 * q + 4, :, :].bitcast(I32),
                 w2_scales.bitcast(I32)[:, 4 * q : 4 * q + 4, :].rearrange("a r c -> r a c"),
             )
-        v_s = held([P, K // K_PASS, S], U8, "v_s")
-        nc.vector.memset(v_s[:].bitcast(I32), 0)
 
         ident = held([P, P], F32, "ident")
         make_identity(nc, ident[:])
+        gain_turned = bank("prod")
+        nc.tensor.transpose(gain_turned[:, 0:P], gain_rows[:], ident[:])
+        gain_at = gain_turned[:, 0:PAGES]
         gain_m2 = held([P, PAGES], F32, "gain_m2")
         gain_p2 = held([P, PAGES], F32, "gain_p2")
-        nc.gpsimd.tensor_scalar(out=gain_m2[:], in0=gain_sb[:], scalar1=-2.0, scalar2=None, op0=MULT)
-        nc.gpsimd.tensor_scalar(out=gain_p2[:], in0=gain_sb[:], scalar1=2.0, scalar2=None, op0=MULT)
-
         gain_sign = held([P, PAGES], F32, "gain_sign")
         gain_abs = held([P, PAGES], F32, "gain_abs")
-        nc.scalar.activation(out=gain_sign[:], in_=gain_sb[:], func=ACT.Sign)
-        nc.scalar.activation(out=gain_abs[:], in_=gain_sb[:], func=ACT.Abs)
+        nc.scalar.activation(out=gain_abs[:], in_=gain_at, func=ACT.Abs)
+        nc.scalar.activation(out=gain_sign[:], in_=gain_at, func=ACT.Sign)
+        nc.scalar.activation(out=gain_m2[:], in_=gain_at, func=ACT.Copy, scale=-2.0)
+        nc.scalar.activation(out=gain_p2[:], in_=gain_at, func=ACT.Copy, scale=2.0)
         ln_gain = held([P, PAGES], F32, "ln_gain")
         nc.scalar.activation(out=ln_gain[:], in_=gain_abs[:], func=ACT.Ln, bias=2.0**-64)
 
@@ -151,11 +143,13 @@ def tile_list_ocean_band_weave_kernel(
 
         v2_s = held([P, S], U8, "v2_s")
         v2_w = held([P, S], U32, "v2_w")
+        v_rows = held([P, S], U8, "v_rows")
+        nc.vector.tensor_copy(v_rows[:], tab_s[:].indirect(list1[:]))
         nc.vector.tensor_copy(v2_s[:], tab2_s[:].indirect(list2[:]))
         for j0, j1 in ((0, H2_SLICE), (H2_SLICE, S)):
             nc.vector.tensor_copy(v2_w[:, j0:j1], tab2_w[:].indirect(list2[:, j0 // 16 : j1 // 16]))
-        v_rows = held([P, S], U8, "v_rows")
-        nc.vector.tensor_copy(v_rows[:], tab_s[:].indirect(list1[:]))
+        v_s = tenant([P, K // K_PASS, S], U8, "big2")
+        nc.vector.memset(v_s[:].bitcast(I32), 0)
         for a in range(K // K_PASS):
             for q in range(QUADS):
                 nc.sync.dma_start(
@@ -216,6 +210,7 @@ def tile_list_ocean_band_weave_kernel(
             rounded = round_block(
                 w1_raw[a][:].rearrange("p a j (c i) -> p a c j i", i=4),
                 lambda ap: ap.rearrange("p (a c i j) -> p a c j i", a=2, i=4, j=PACK),
+                nc.vector.tensor_copy if a == 0 else nc.scalar.copy,
             )
             nc.vector.quantize_mx(out=w1_w[:, a, :].bitcast(FP8X4), scales=w1_s[:, a, :], in_=rounded[:])
 

@@ -22,10 +22,16 @@ PACK = 4
 K_PASS = P * PACK
 BANK = 512
 QUADS = 4
+PER_COLUMN = 16
+PAGES = H // P
+PASSES = K // K_PASS
+GROUPS = N // K_PASS
+RING = 4
 H2_SLICE = 256
 Z_PIECES = (128, 128, 256, 512, 512, 512)
-PAGES = H // P
 EARLY = 256
+ROWS_AT = P - 32
+WARM_PASSES = 2
 
 
 def tile_list_ocean_band_weave_kernel(
@@ -44,74 +50,69 @@ def tile_list_ocean_band_weave_kernel(
         def rotating(shape, dtype, tag, bufs):
             return ring.tile(shape, dtype, name=tag, tag=tag, bufs=bufs, align_bytes=64)
 
-        def bank(tag):
-            return psum.tile([P, BANK], F32, name=tag, tag=tag, bufs=4)
-
-        def load_list(src, name):
-            tile = keep.tile([P, S // 16], U16, name=name)
-            nc.sync.dma_start(tile[:], src)
-            return tile
-
         def tenant(shape, dtype, tag):
             return ring.tile(shape, dtype, name=tag, tag=tag, bufs=1, align_bytes=64)
 
-        def load_words(queue, src, tag):
-            tile = tenant([P, src.shape[1]], U32, tag)
-            queue.dma_start(tile[:].bitcast(I32), src.rearrange("p c i -> p (c i)").bitcast(I32))
+        def bank(tag):
+            return psum.tile([P, BANK], F32, name=tag, tag=tag, bufs=RING)
+
+        def entries(tile, start, stop):
+            return tile[:, start // PER_COLUMN : stop // PER_COLUMN]
+
+        def load_list(src, name):
+            tile = keep.tile([P, S // PER_COLUMN], U16, name=name)
+            nc.sync.dma_start(tile[:], src)
             return tile
 
-        def load_plane(queue, rows, name):
-            tile = held([P, rows.shape[1]], U8, name)
+        def load_words(src, tag):
+            tile = tenant([P, src.shape[1]], U32, tag)
+            nc.sync.dma_start(tile[:].bitcast(I32), src.rearrange("p c i -> p (c i)").bitcast(I32))
+            return tile
+
+        def load_plane(rows, tag):
+            tile = tenant([P, rows.shape[1]], U8, tag)
             nc.gpsimd.memset(tile[:].bitcast(I32), 0)
-            words = rows.bitcast(I32)
             for q in range(QUADS):
-                queue.dma_start(tile[32 * q : 32 * q + 4, :].bitcast(I32), words[4 * q : 4 * q + 4, :])
+                nc.sync.dma_start(tile[32 * q : 32 * q + 4, :].bitcast(I32), rows.bitcast(I32)[4 * q : 4 * q + 4, :])
             return tile
 
         def round_block(src, order, first=nc.scalar.copy):
-            rounded = rotating([P, BANK * PACK], BF16, "rounded", 4)
+            rounded = rotating([P, BANK * PACK], BF16, "rounded", RING)
             dst = order(rounded[:])
-            half = src.shape[1] // 2
-            if half == 1:
-                first(out=dst[:, 0], in_=src[:, 0])
-                nc.scalar.copy(out=dst[:, 1], in_=src[:, 1])
-                return rounded
-            first(out=dst[:, :half], in_=src[:, :half])
-            nc.scalar.copy(out=dst[:, half:], in_=src[:, half:])
+            first(out=dst[:, 0], in_=src[:, 0])
+            nc.scalar.copy(out=dst[:, 1], in_=src[:, 1])
             return rounded
 
         list1 = load_list(offs, "list1")
         tab_s = held([P, T], U8, "tab_s")
-        nc.sync.dma_start(tab_s[0:32, :].bitcast(I32), tab_scales.bitcast(I32).rearrange("a q c -> (a q) c"))
-        nc.vector.memset(tab_s[32:64, :].bitcast(I32), 0)
-        nc.vector.memset(tab_s[64:P, :].bitcast(I32), 0)
+        nc.sync.dma_start(tab_s[ROWS_AT:P, :].bitcast(I32), tab_scales.bitcast(I32).rearrange("a q c -> (a q) c"))
+        nc.vector.memset(tab_s[0:ROWS_AT, :].bitcast(I32), 0)
         wg1_sb = held([P, S], F32, "wg1_sb")
         nc.sync.dma_start(wg1_sb[:], wg1)
         gain_rows = held([P, P], F32, "gain_rows")
         nc.gpsimd.memset(gain_rows[:], 0.0)
         nc.sync.dma_start(gain_rows[0:PAGES, :], gain.rearrange("(b p) -> b p", p=P))
         list2 = load_list(offs2, "list2")
-        tab2_s = load_plane(nc.sync, tab2_scales[0], "tab2_s")
-        tab2_w = load_words(nc.sync, tab2_words[0], "big2")
-        w3_s = load_plane(nc.sync, w3_scales[0], "w3_s")
-        w3_w = load_words(nc.sync, w3_words[0], "w3_w")
-        tab_w = [load_words(nc.sync, tab_words[a], "big%d" % a) for a in range(K // K_PASS)]
+        tab2_s = load_plane(tab2_scales[0], "tab2_s")
+        tab2_w = load_words(tab2_words[0], "big2")
+        w3_s = load_plane(w3_scales[0], "w3_s")
+        w3_w = load_words(w3_words[0], "w3_w")
+        tab_w = [load_words(tab_words[a], "big%d" % a) for a in range(PASSES)]
         list4 = load_list(offs4, "list4")
         wg2_sb = held([P, S], F32, "wg2_sb")
         nc.sync.dma_start(wg2_sb[:], wg2)
-        w1_raw = [tenant([P, K // K_PASS, PACK, H // 2], F32, "raw1_%d" % u) for u in range(2)]
+        w1_raw = [tenant([P, PASSES, PACK, H // 2], F32, "raw1_%d" % u) for u in range(2)]
         for u in range(2):
-            for a in range(K // K_PASS):
+            for a in range(PASSES):
                 rows = w1[a * K_PASS : (a + 1) * K_PASS, u * H // 2 : (u + 1) * H // 2]
                 nc.sync.dma_start(w1_raw[u][:, a], rows.rearrange("(p j) c -> p j c", j=PACK))
-        w2_w = held([P, K // K_PASS, 2 * H], U8, "w2_w")
+        w2_w = held([P, PASSES, 2 * H], U8, "w2_w")
         nc.sync.dma_start(w2_w[:].bitcast(I32), w2_words.bitcast(I32).rearrange("a p c -> p a c"))
         list3 = load_list(offs3, "list3")
-        w4_raw = [tenant([P, PACK, BANK], F32, "raw4_%d" % g) for g in range(N // BANK)]
-        for g in range(N // BANK):
+        w4_raw = [tenant([P, PACK, BANK], F32, "raw4_%d" % g) for g in range(GROUPS)]
+        for g in range(GROUPS):
             nc.sync.dma_start(w4_raw[g][:], w4[:, g * BANK : (g + 1) * BANK].rearrange("(p j) c -> p j c", j=PACK))
-        w2_s = held([P, K // K_PASS, H], U8, "w2_s")
-        nc.vector.memset(w2_s[:].bitcast(I32), 0)
+        w2_s = tenant([P, PASSES, H], U8, "tab2_s")
         for q in range(QUADS):
             nc.sync.dma_start(
                 w2_s[32 * q : 32 * q + 4, :, :].bitcast(I32),
@@ -147,17 +148,14 @@ def tile_list_ocean_band_weave_kernel(
         nc.vector.tensor_copy(v_rows[:], tab_s[:].indirect(list1[:]))
         nc.vector.tensor_copy(v2_s[:], tab2_s[:].indirect(list2[:]))
         for j0, j1 in ((0, H2_SLICE), (H2_SLICE, S)):
-            nc.vector.tensor_copy(v2_w[:, j0:j1], tab2_w[:].indirect(list2[:, j0 // 16 : j1 // 16]))
-        v_s = tenant([P, K // K_PASS, S], U8, "big2")
-        nc.vector.memset(v_s[:].bitcast(I32), 0)
-        for a in range(K // K_PASS):
+            nc.vector.tensor_copy(v2_w[:, j0:j1], tab2_w[:].indirect(entries(list2, j0, j1)))
+        v_s = tenant([P, PASSES, S], U8, "big2")
+        for a in range(PASSES):
             for q in range(QUADS):
-                nc.sync.dma_start(
-                    v_s[32 * q : 32 * q + 4, a, :].bitcast(I32),
-                    v_rows[16 * a + 4 * q : 16 * a + 4 * q + 4, :].bitcast(I32),
-                )
+                row = ROWS_AT + 16 * a + 4 * q
+                nc.sync.dma_start(v_s[32 * q : 32 * q + 4, a, :].bitcast(I32), v_rows[row : row + 4, :].bitcast(I32))
         v_w = []
-        for a in range(K // K_PASS):
+        for a in range(PASSES):
             v_w.append(held([P, S], U32, "v_w%d" % a))
             nc.vector.tensor_copy(v_w[a][:], tab_w[a][:].indirect(list1[:]))
 
@@ -170,8 +168,8 @@ def tile_list_ocean_band_weave_kernel(
         sums = {}
 
         def sines_of_tile(s, jj):
-            cols = slice(s * H2_SLICE + jj * P, s * H2_SLICE + (jj + 1) * P)
-            half_sin = rotating([P, 2 * H], F32, "turned", 4)
+            cols = slice((s * tiles_per_slice + jj) * P, (s * tiles_per_slice + jj + 1) * P)
+            half_sin = rotating([P, 2 * H], F32, "turned", RING)
             for c in range(2):
                 arg = bank("prod")
                 nc.tensor.matmul_mx(
@@ -193,26 +191,26 @@ def tile_list_ocean_band_weave_kernel(
                     )
 
         def place_slice(s):
-            h2 = rotating([P, PAGES, H2_SLICE], F32, "placed", 4)
+            h2 = rotating([P, PAGES, H2_SLICE], F32, "placed", RING)
             for b in range(PAGES):
                 at = (b % per_bank) * H2_SLICE
                 nc.scalar.activation(
                     out=h2[:, b, :], in_=sums[s][b // per_bank][:, at : at + H2_SLICE], func=ACT.Identity,
                     scale=gain_m2[:, b : b + 1], bias=gain_p2[:, b : b + 1],
                 )
-            picks = list4[:, s * H2_SLICE // 16 : (s + 1) * H2_SLICE // 16]
+            j0, j1 = s * H2_SLICE, (s + 1) * H2_SLICE
             for b in range(PAGES):
                 nc.vector.tensor_tensor(
-                    pages[b][:].indirect(picks), h2[:, b, :], wg2_sb[:, s * H2_SLICE : (s + 1) * H2_SLICE], MULT
+                    pages[b][:].indirect(entries(list4, j0, j1)), h2[:, b, :], wg2_sb[:, j0:j1], MULT
                 )
 
-        def quantize_w1(a):
+        def quantize_w1(u, first):
             rounded = round_block(
-                w1_raw[a][:].rearrange("p a j (c i) -> p a c j i", i=4),
-                lambda ap: ap.rearrange("p (a c i j) -> p a c j i", a=2, i=4, j=PACK),
-                nc.vector.tensor_copy if a == 0 else nc.scalar.copy,
+                w1_raw[u][:].rearrange("p a j (c i) -> p a c j i", i=4),
+                lambda ap: ap.rearrange("p (a c i j) -> p a c j i", a=PASSES, i=4, j=PACK),
+                first,
             )
-            nc.vector.quantize_mx(out=w1_w[:, a, :].bitcast(FP8X4), scales=w1_s[:, a, :], in_=rounded[:])
+            nc.vector.quantize_mx(out=w1_w[:, u, :].bitcast(FP8X4), scales=w1_s[:, u, :], in_=rounded[:])
 
         sines_of_tile(0, 0)
         sines_of_tile(0, 1)
@@ -223,19 +221,9 @@ def tile_list_ocean_band_weave_kernel(
         place_slice(1)
         sines_of_tile(2, 1)
         place_slice(2)
-        quantize_w1(0)
+        quantize_w1(0, nc.vector.tensor_copy)
         sines_of_tile(3, 0)
         sines_of_tile(3, 1)
-
-        def first_product(words, scales, b, cols):
-            acc = bank("prod")
-            for a in range(K // K_PASS):
-                nc.tensor.matmul_mx(
-                    out=acc[:], lhsT=words(a, b), lhsT_scale=scales(a, b),
-                    rhs=v_w[a][:, cols].bitcast(FP8X4), rhs_scale=v_s[:, a, cols],
-                    start=(a == 0), stop=(a == K // K_PASS - 1),
-                )
-            return acc
 
         halves = [slice(h * BANK, (h + 1) * BANK) for h in range(S // BANK)]
         tiles_per_half = BANK // P
@@ -246,24 +234,25 @@ def tile_list_ocean_band_weave_kernel(
             for i in range(tiles_per_half):
                 cols = slice(h * BANK + i * P, h * BANK + (i + 1) * P)
                 acc = bank("prod")
-                for a in range(K // K_PASS):
+                for a in range(PASSES):
                     nc.tensor.matmul_mx(
                         out=acc[:], lhsT=v_w[a][:, cols].bitcast(FP8X4), lhsT_scale=v_s[:, a, cols],
                         rhs=w2_w[:, a, :].bitcast(FP4X4), rhs_scale=w2_s[:, a, :],
-                        start=(a == 0), stop=(a == K // K_PASS - 1),
+                        start=(a == 0), stop=(a == PASSES - 1),
                     )
                 nc.scalar.copy(out=levels[h][:, i, :], in_=acc[:])
 
-        def w1_cols(a, b):
-            at = a * (H // 2) + (b % 2) * P
-            return slice(at, at + P)
-
         def make_sines(b):
             for cols in halves:
-                phase = first_product(
-                    lambda a, b: w1_w[:, b // 2, w1_cols(a, b)].bitcast(FP8X4),
-                    lambda a, b: w1_s[:, b // 2, w1_cols(a, b)], b, cols,
-                )
+                phase = bank("prod")
+                for a in range(PASSES):
+                    at = a * (H // 2) + (b % 2) * P
+                    nc.tensor.matmul_mx(
+                        out=phase[:],
+                        lhsT=w1_w[:, b // 2, at : at + P].bitcast(FP8X4), lhsT_scale=w1_s[:, b // 2, at : at + P],
+                        rhs=v_w[a][:, cols].bitcast(FP8X4), rhs_scale=v_s[:, a, cols],
+                        start=(a == 0), stop=(a == PASSES - 1),
+                    )
                 nc.scalar.activation(
                     out=sines[b // 2][:, b % 2, cols], in_=phase[:], func=ACT.Sin, scale=gain_sign[:, b : b + 1]
                 )
@@ -280,42 +269,43 @@ def tile_list_ocean_band_weave_kernel(
             nc.scalar.activation(out=amps[b][:, halves[h]], in_=total[:], func=ACT.Exp, bias=ln_gain[:, b : b + 1])
 
         def place(b, cols):
-            picks = list3[:, cols.start // 16 : cols.stop // 16]
+            picks = entries(list3, cols.start, cols.stop)
             nc.vector.tensor_tensor(pages[b][:].indirect(picks), sines[b // 2][:, b % 2, cols], amps[b][:, cols], MULT)
 
+        last = PAGES - 1
         make_levels(0)
         place_slice(3)
-        amps = [rotating([P, S], F32, "placed", 4) for b in range(PAGES - 1)] + [tenant([P, S], F32, "last")]
+        amps = [rotating([P, S], F32, "placed", RING) for b in range(last)] + [tenant([P, S], F32, "last")]
         make_sines(0)
         make_sines(1)
         for b in (0, 1):
             make_amp(b, 0)
             place(b, halves[0])
-        quantize_w1(1)
+        quantize_w1(1, nc.scalar.copy)
         make_levels(1)
         for b in (0, 1):
             make_amp(b, 1)
             place(b, halves[1])
-        make_sines(2)
-        make_sines(3)
-        make_amp(3, 0)
-        place(3, slice(0, EARLY))
-        make_amp(2, 0)
-        make_amp(2, 1)
-        place(2, slice(0, S))
-        make_amp(3, 1)
+        make_sines(last - 1)
+        make_sines(last)
+        make_amp(last, 0)
+        place(last, slice(0, EARLY))
+        make_amp(last - 1, 0)
+        make_amp(last - 1, 1)
+        place(last - 1, slice(0, S))
+        make_amp(last, 1)
         w4_rounded = [
             round_block(
-                w4_raw[g][:].rearrange("p j (m t) -> p m j t", t=PACK),
-                lambda ap: ap.rearrange("p (t m j) -> p m j t", t=PACK, j=PACK),
+                w4_raw[g][:].rearrange("p j (h m t) -> p h m j t", h=2, t=PACK),
+                lambda ap: ap.rearrange("p (t h m j) -> p h m j t", t=PACK, h=2, j=PACK),
             )
-            for g in range(N // BANK)
+            for g in range(GROUPS)
         ]
-        place(PAGES - 1, slice(EARLY, S))
+        place(last, slice(EARLY, S))
 
         w4_w = tenant([P, N], U32, "last")
         w4_s = held([P, N], U8, "w4_s")
-        for g in range(N // BANK):
+        for g in range(GROUPS):
             cols = slice(g * BANK, (g + 1) * BANK)
             nc.vector.quantize_mx(out=w4_w[:, cols].bitcast(FP8X4), scales=w4_s[:, cols], in_=w4_rounded[g][:])
 
@@ -326,50 +316,46 @@ def tile_list_ocean_band_weave_kernel(
             if width < BANK:
                 across.append(held(shape, BF16, "across%d" % i))
             else:
-                across.append(rotating(shape, BF16, "turned", 4))
+                across.append(rotating(shape, BF16, "turned", RING))
 
-        def turn_out(b, i, turned, copy):
-            copy(
-                out=across[i][:, :, :, 32 * b : 32 * (b + 1), :],
-                in_=turned.rearrange("c (i q u e) -> c i u q e", q=32, u=2, e=2),
-            )
-
-        def turn_page(b, group, turned=None, copy=nc.scalar.copy):
-            if turned is None:
-                turned = bank("turn")
-            c0 = pieces[group[0]][0]
-            for i in group:
+        def turn_page(b, chosen):
+            turned = bank("turn")
+            c0 = pieces[chosen[0]][0]
+            for i in chosen:
                 at, width = pieces[i]
                 for col in range(at, at + width, P):
                     nc.tensor.transpose(turned[:, col - c0 : col - c0 + P], pages[b][:, col : col + P], ident[:])
-            for i in group:
+            for i in chosen:
                 at, width = pieces[i]
-                turn_out(b, i, turned[:, at - c0 : at - c0 + width], copy)
+                nc.scalar.copy(
+                    out=across[i][:, :, :, 32 * b : 32 * (b + 1), :],
+                    in_=turned[:, at - c0 : at - c0 + width].rearrange("c (i q u e) -> c i u q e", q=32, u=2, e=2),
+                )
             return turned
 
-        def warm_up(acc, passes):
-            for i in range(passes):
+        def warm_up(emptied):
+            for i in range(WARM_PASSES):
                 nc.tensor.matmul_mx(
-                    out=acc[:], lhsT=v2_w[:, 0:P].bitcast(FP8X4), lhsT_scale=v2_s[:, 0:P],
-                    rhs=w3_w[:, 0:H].bitcast(FP8X4), rhs_scale=w3_s[:, 0:H], start=(i == 0), stop=(i == passes - 1),
+                    out=emptied[:], lhsT=v2_w[:, 0:P].bitcast(FP8X4), lhsT_scale=v2_s[:, 0:P],
+                    rhs=w3_w[:, 0:H].bitcast(FP8X4), rhs_scale=w3_s[:, 0:H],
+                    start=(i == 0), stop=(i == WARM_PASSES - 1),
                 )
 
         blocks = range(T2 // BANK)
         in_block = [[i for i, (c0, width) in enumerate(pieces) if c0 // BANK == k] for k in blocks]
-        for b in range(PAGES - 2):
+        for b in range(last - 1):
             for k in blocks:
                 turn_page(b, in_block[k])
-        emptied = []
+        turns = []
         for k in blocks:
-            emptied.append(turn_page(PAGES - 2, in_block[k]))
+            turns.append(turn_page(last - 1, in_block[k]))
             if k > 0:
-                warm_up(emptied[k - 1], 2)
+                warm_up(turns[k - 1])
 
         z_w = tenant([P, T2], U32, "big2")
         z_s = held([P, T2], U8, "z_s")
         y_s = held([P, T2], U8, "y_s")
-        y_w = held([P, N // K_PASS, T2], U32, "y_w")
-        groups = range(N // K_PASS)
+        y_w = held([P, GROUPS, T2], U32, "y_w")
 
         def make_z(i):
             c0, width = pieces[i]
@@ -392,103 +378,80 @@ def tile_list_ocean_band_weave_kernel(
         homes = (("big0", "big1"), ("raw1_0", "raw1_1"), ("raw4_0", "raw4_1"), ("sine0", "sine1"))
         ys = {}
 
-        def result_tile(k, g):
-            if (k, g) not in ys:
-                ys[k, g] = tenant([P, PACK, BANK], F32, homes[k][g])
-            return ys[k, g]
-
-        def fill(g, c0, width, stores):
-            y = result_tile(c0 // BANK, g)
+        def make_y(i, stores=1):
+            c0, width = pieces[i]
+            k, at = divmod(c0, BANK)
             share = BANK // width
-            for t0 in range(0, PACK, share):
-                acc = bank("prod")
-                for i in range(share):
-                    at = g * BANK + (t0 + i) * P
-                    nc.tensor.matmul_mx(
-                        out=acc[:, i * width : (i + 1) * width],
-                        lhsT=w4_w[:, at : at + P].bitcast(FP8X4), lhsT_scale=w4_s[:, at : at + P],
-                        rhs=z_w[:, c0 : c0 + width].bitcast(FP8X4), rhs_scale=z_s[:, c0 : c0 + width],
-                        start=True, stop=True,
-                    )
-                at = c0 % BANK
-                nc.scalar.copy(
-                    out=y[:, t0 : t0 + share, at : at + width],
-                    in_=acc[:].rearrange("p (t c) -> p t c", c=width),
-                )
-                done = t0 + share
-                if stores and done % (PACK // stores) == 0:
-                    store_y(g, c0, width, done - PACK // stores, done)
+            for g in range(GROUPS):
+                if at == 0:
+                    ys[k, g] = tenant([P, PACK, BANK], F32, homes[k][g])
+                y = ys[k, g][:, :, at : at + width]
+                rows = out_0[g * K_PASS : (g + 1) * K_PASS, c0 : c0 + width].rearrange("(p t) c -> p t c", t=PACK)
+                for t0 in range(0, PACK, share):
+                    acc = bank("prod")
+                    for t in range(t0, t0 + share):
+                        w4_cols = slice(g * BANK + t * P, g * BANK + (t + 1) * P)
+                        nc.tensor.matmul_mx(
+                            out=acc[:, (t - t0) * width : (t - t0 + 1) * width],
+                            lhsT=w4_w[:, w4_cols].bitcast(FP8X4), lhsT_scale=w4_s[:, w4_cols],
+                            rhs=z_w[:, c0 : c0 + width].bitcast(FP8X4), rhs_scale=z_s[:, c0 : c0 + width],
+                            start=True, stop=True,
+                        )
+                    done = t0 + share
+                    nc.scalar.copy(out=y[:, t0:done, :], in_=acc[:].rearrange("p (t c) -> p t c", c=width))
+                    part = PACK // stores
+                    if done % part == 0:
+                        nc.sync.dma_start(rows[:, done - part : done, :], y[:, done - part : done, :])
 
-        def store_y(g, c0, width, t0, t1):
-            rows = out_0[g * K_PASS : (g + 1) * K_PASS, c0 : c0 + width].rearrange("(p t) c -> p t c", t=PACK)
-            at = c0 % BANK
-            nc.sync.dma_start(rows[:, t0:t1, :], ys[c0 // BANK, g][:, t0:t1, at : at + width])
-
-        def weave_y(g, c0, width, by_scalar):
-            at = c0 % BANK
-            woven = rotating([P, width * PACK], BF16, "rounded", 4)
+        def weave_y(k, g, by_scalar):
+            woven = rotating([P, BANK * PACK], BF16, "rounded", RING)
             dst = woven[:].rearrange("p (c i t) -> p c t i", i=4, t=PACK)
-            src = ys[c0 // BANK, g][:, :, at : at + width].rearrange("p t (c i) -> p c t i", i=4)
-            cut = (width - by_scalar) // 4
-            if cut > 0:
-                nc.vector.tensor_copy(out=dst[:, :cut], in_=src[:, :cut])
+            src = ys[k, g][:].rearrange("p t (c i) -> p c t i", i=4)
+            cut = (BANK - by_scalar) // 4
+            nc.vector.tensor_copy(out=dst[:, :cut], in_=src[:, :cut])
             if by_scalar > 0:
                 nc.scalar.copy(out=dst[:, cut:], in_=src[:, cut:])
             return woven
 
-        def make_planes(c0, width, by_scalar=(0, 0)):
-            cols = slice(c0, c0 + width)
-            woven = [weave_y(g, c0, width, by_scalar[g]) for g in groups]
-            for g in groups:
+        def make_planes(k):
+            cols = slice(k * BANK, (k + 1) * BANK)
+            final = k == blocks[-1]
+            woven = [weave_y(k, g, BANK // 2 if final and g == GROUPS - 1 else 0) for g in range(GROUPS)]
+            for g in range(GROUPS):
                 nc.vector.quantize_mx(
                     out=y_w[:, g, cols].bitcast(FP8X4), scales=y_s[4 * g : P, cols], in_=woven[g][:]
                 )
-                if cols.stop == T2:
+                if final:
                     nc.sync.dma_start(
                         out_1[g, :, cols, :].rearrange("p m t -> p (m t)").bitcast(I32), y_w[:, g, cols].bitcast(I32)
                     )
-            if cols.stop < T2:
-                cols = slice(cols.stop - BANK, cols.stop)
+            if not final:
                 nc.sync.dma_start(
                     out_1[:, :, cols, :].rearrange("g p m t -> p g (m t)").bitcast(I32), y_w[:, :, cols].bitcast(I32)
                 )
 
-        def store_scales(queues, cols):
-            words = slice(cols.start // 4, cols.stop // 4)
-            for q in range(QUADS):
-                queues[q % len(queues)].dma_start(
-                    out_2.bitcast(I32)[:, 4 * q : 4 * q + 4, words],
-                    y_s[32 * q : 32 * q + 8, :].bitcast(I32)[:, words],
-                )
-
-        def make_y(c0, width, stores=(1, 1)):
-            for g in groups:
-                fill(g, c0, width, stores[g])
-
-        last = PAGES - 1
         turn_page(last, [0])
-        warm_up(emptied[-1], 2)
+        warm_up(turns[-1])
         turn_page(last, [1, 2])
         make_z(0)
         turn_page(last, [3])
         make_z(1)
         make_z(2)
         turn_page(last, [4])
-        make_y(*pieces[0])
+        make_y(0)
         make_z(3)
-        for g in groups:
-            fill(g, *pieces[1], 0)
-            fill(g, *pieces[2], 0)
-            store_y(g, P, BANK - P, 0, PACK // 2)
-            store_y(g, P, BANK - P, PACK // 2, PACK)
+        make_y(1)
+        make_y(2)
         turn_page(last, [5])
         make_z(4)
-        make_y(*pieces[3], stores=(2, 2))
-        make_planes(0, BANK)
+        make_y(3, stores=2)
+        make_planes(0)
         make_z(5)
-        make_y(*pieces[4])
-        make_planes(BANK, BANK)
-        make_y(*pieces[5])
-        make_planes(2 * BANK, BANK)
-        make_planes(3 * BANK, BANK, by_scalar=(0, BANK // 2))
-        store_scales((nc.scalar, nc.sync), slice(0, T2))
+        make_y(4)
+        make_planes(1)
+        make_y(5)
+        make_planes(2)
+        make_planes(3)
+        for q in range(QUADS):
+            queue = nc.scalar if q % 2 == 0 else nc.sync
+            queue.dma_start(out_2.bitcast(I32)[:, 4 * q : 4 * q + 4, :], y_s[32 * q : 32 * q + 8, :].bitcast(I32))

@@ -31,6 +31,7 @@ H2_SLICE = 256
 Z_PIECES = (128, 128, 256, 512, 512, 512)
 EARLY = 256
 ROWS_AT = P - 32
+SLOT = PACK * BANK * 4
 WARM_PASSES = 2
 
 
@@ -42,6 +43,7 @@ def tile_list_ocean_band_weave_kernel(
     with ExitStack() as ctx:
         keep = ctx.enter_context(tc.tile_pool(name="keep", bufs=1))
         ring = ctx.enter_context(tc.tile_pool(name="ring", bufs=1))
+        arena = ctx.enter_context(tc.tile_pool(name="arena", bufs=1))
         psum = ctx.enter_context(tc.psum_pool(name="psum", bufs=1))
 
         def held(shape, dtype, name):
@@ -52,6 +54,9 @@ def tile_list_ocean_band_weave_kernel(
 
         def tenant(shape, dtype, tag):
             return ring.tile(shape, dtype, name=tag, tag=tag, bufs=1, align_bytes=64)
+
+        def placed_at(shape, dtype, name, slot):
+            return arena.tile(shape, dtype, name=name, offset=slot * SLOT, align_bytes=64)
 
         def bank(tag):
             return psum.tile([P, BANK], F32, name=tag, tag=tag, bufs=RING)
@@ -101,7 +106,7 @@ def tile_list_ocean_band_weave_kernel(
         list4 = load_list(offs4, "list4")
         wg2_sb = held([P, S], F32, "wg2_sb")
         nc.sync.dma_start(wg2_sb[:], wg2)
-        w1_raw = [tenant([P, PASSES, PACK, H // 2], F32, "raw1_%d" % u) for u in range(2)]
+        w1_raw = [placed_at([P, PASSES, PACK, H // 2], F32, "w1_raw%d" % u, u) for u in range(2)]
         for u in range(2):
             for a in range(PASSES):
                 rows = w1[a * K_PASS : (a + 1) * K_PASS, u * H // 2 : (u + 1) * H // 2]
@@ -109,7 +114,7 @@ def tile_list_ocean_band_weave_kernel(
         w2_w = held([P, PASSES, 2 * H], U8, "w2_w")
         nc.sync.dma_start(w2_w[:].bitcast(I32), w2_words.bitcast(I32).rearrange("a p c -> p a c"))
         list3 = load_list(offs3, "list3")
-        w4_raw = [tenant([P, PACK, BANK], F32, "raw4_%d" % g) for g in range(GROUPS)]
+        w4_raw = [placed_at([P, PACK, BANK], F32, "w4_raw%d" % g, 2 + g) for g in range(GROUPS)]
         for g in range(GROUPS):
             nc.sync.dma_start(w4_raw[g][:], w4[:, g * BANK : (g + 1) * BANK].rearrange("(p j) c -> p j c", j=PACK))
         w2_s = tenant([P, PASSES, H], U8, "tab2_s")
@@ -227,8 +232,8 @@ def tile_list_ocean_band_weave_kernel(
 
         halves = [slice(h * BANK, (h + 1) * BANK) for h in range(S // BANK)]
         tiles_per_half = BANK // P
-        sines = [tenant([P, 2, S], F32, "sine%d" % i) for i in range(PAGES // 2)]
-        levels = [tenant([P, tiles_per_half, H], F32, "raw1_%d" % h) for h in range(len(halves))]
+        sines = [placed_at([P, 2, S], F32, "sines%d" % i, 4 + i) for i in range(PAGES // 2)]
+        levels = [placed_at([P, tiles_per_half, H], F32, "levels%d" % h, h) for h in range(len(halves))]
 
         def make_levels(h):
             for i in range(tiles_per_half):
@@ -375,60 +380,73 @@ def tile_list_ocean_band_weave_kernel(
             cols = slice(c0, c0 + width)
             nc.vector.quantize_mx(out=z_w[:, cols].bitcast(FP8X4), scales=z_s[:, cols], in_=woven[:])
 
-        homes = (("big0", "big1"), ("raw1_0", "raw1_1"), ("raw4_0", "raw4_1"), ("sine0", "sine1"))
-        ys = {}
+        spans = [(0, 0, 1), (1, 0, 1), (0, 1, 2), (1, 1, 4), (0, 2, 4)]
+        ys = [tenant([P, PACK, BANK], F32, "big%d" % g) for g in range(GROUPS)]
+        for slot, (g, k0, k1) in zip((0, 1, 4), spans[GROUPS:]):
+            ys.append(placed_at([P, PACK, (k1 - k0) * BANK], F32, "y%d" % slot, slot))
 
-        def make_y(i, stores=1):
+        def rows_of(g, c0, c1):
+            return out_0[g * K_PASS : (g + 1) * K_PASS, c0:c1].rearrange("(p t) c -> p t c", t=PACK)
+
+        def product(out, g, t, c0, c1):
+            w4_cols = slice(g * BANK + t * P, g * BANK + (t + 1) * P)
+            nc.tensor.matmul_mx(
+                out=out, lhsT=w4_w[:, w4_cols].bitcast(FP8X4), lhsT_scale=w4_s[:, w4_cols],
+                rhs=z_w[:, c0:c1].bitcast(FP8X4), rhs_scale=z_s[:, c0:c1], start=True, stop=True,
+            )
+
+        def make_piece(i):
             c0, width = pieces[i]
-            k, at = divmod(c0, BANK)
             share = BANK // width
             for g in range(GROUPS):
-                if at == 0:
-                    ys[k, g] = tenant([P, PACK, BANK], F32, homes[k][g])
-                y = ys[k, g][:, :, at : at + width]
-                rows = out_0[g * K_PASS : (g + 1) * K_PASS, c0 : c0 + width].rearrange("(p t) c -> p t c", t=PACK)
+                y = ys[g][:, :, c0 : c0 + width]
                 for t0 in range(0, PACK, share):
                     acc = bank("prod")
                     for t in range(t0, t0 + share):
-                        w4_cols = slice(g * BANK + t * P, g * BANK + (t + 1) * P)
-                        nc.tensor.matmul_mx(
-                            out=acc[:, (t - t0) * width : (t - t0 + 1) * width],
-                            lhsT=w4_w[:, w4_cols].bitcast(FP8X4), lhsT_scale=w4_s[:, w4_cols],
-                            rhs=z_w[:, c0 : c0 + width].bitcast(FP8X4), rhs_scale=z_s[:, c0 : c0 + width],
-                            start=True, stop=True,
-                        )
-                    done = t0 + share
-                    nc.scalar.copy(out=y[:, t0:done, :], in_=acc[:].rearrange("p (t c) -> p t c", c=width))
-                    part = PACK // stores
-                    if done % part == 0:
-                        nc.sync.dma_start(rows[:, done - part : done, :], y[:, done - part : done, :])
+                        product(acc[:, (t - t0) * width : (t - t0 + 1) * width], g, t, c0, c0 + width)
+                    nc.scalar.copy(out=y[:, t0 : t0 + share, :], in_=acc[:].rearrange("p (t c) -> p t c", c=width))
+                nc.sync.dma_start(rows_of(g, c0, c0 + width), y)
 
-        def weave_y(k, g, by_scalar):
+        def make_span(n, order, rows_a_store=1):
+            g, k0, k1 = spans[n]
+            rows = rows_of(g, k0 * BANK, k1 * BANK)
+            for t, k in order:
+                acc = bank("prod")
+                product(acc[:], g, t, k * BANK, (k + 1) * BANK)
+                nc.scalar.copy(out=ys[n][:, t, (k - k0) * BANK : (k - k0 + 1) * BANK], in_=acc[:])
+                if k == k1 - 1 and (t + 1) % rows_a_store == 0:
+                    part = slice(t + 1 - rows_a_store, t + 1)
+                    nc.sync.dma_start(rows[:, part, :], ys[n][:, part, :])
+
+        def by_rows(n):
+            return [(t, k) for t in range(PACK) for k in range(spans[n][1], spans[n][2])]
+
+        def by_blocks(n):
+            return [(t, k) for k in range(spans[n][1], spans[n][2]) for t in range(PACK)]
+
+        def weave_y(n, k, by_scalar):
+            at = (k - spans[n][1]) * BANK
             woven = rotating([P, BANK * PACK], BF16, "rounded", RING)
             dst = woven[:].rearrange("p (c i t) -> p c t i", i=4, t=PACK)
-            src = ys[k, g][:].rearrange("p t (c i) -> p c t i", i=4)
+            src = ys[n][:, :, at : at + BANK].rearrange("p t (c i) -> p c t i", i=4)
             cut = (BANK - by_scalar) // 4
             nc.vector.tensor_copy(out=dst[:, :cut], in_=src[:, :cut])
             if by_scalar > 0:
                 nc.scalar.copy(out=dst[:, cut:], in_=src[:, cut:])
             return woven
 
-        def make_planes(k):
-            cols = slice(k * BANK, (k + 1) * BANK)
-            final = k == blocks[-1]
-            woven = [weave_y(k, g, BANK // 2 if final and g == GROUPS - 1 else 0) for g in range(GROUPS)]
-            for g in range(GROUPS):
-                nc.vector.quantize_mx(
-                    out=y_w[:, g, cols].bitcast(FP8X4), scales=y_s[4 * g : P, cols], in_=woven[g][:]
-                )
-                if final:
-                    nc.sync.dma_start(
-                        out_1[g, :, cols, :].rearrange("p m t -> p (m t)").bitcast(I32), y_w[:, g, cols].bitcast(I32)
-                    )
-            if not final:
-                nc.sync.dma_start(
-                    out_1[:, :, cols, :].rearrange("g p m t -> p g (m t)").bitcast(I32), y_w[:, :, cols].bitcast(I32)
-                )
+        def make_planes(chosen, by_scalar=0):
+            woven = [weave_y(n, k, by_scalar) for n, k in chosen]
+            for i, (n, k) in enumerate(chosen):
+                g = spans[n][0]
+                cols = slice(k * BANK, (k + 1) * BANK)
+                nc.vector.quantize_mx(out=y_w[:, g, cols].bitcast(FP8X4), scales=y_s[4 * g : P, cols], in_=woven[i][:])
+
+        def store_words(g, k0, k1):
+            cols = slice(k0 * BANK, k1 * BANK)
+            nc.sync.dma_start(
+                out_1[g, :, cols, :].rearrange("p m t -> p (m t)").bitcast(I32), y_w[:, g, cols].bitcast(I32)
+            )
 
         turn_page(last, [0])
         warm_up(turns[-1])
@@ -438,20 +456,25 @@ def tile_list_ocean_band_weave_kernel(
         make_z(1)
         make_z(2)
         turn_page(last, [4])
-        make_y(0)
+        make_piece(0)
         make_z(3)
-        make_y(1)
-        make_y(2)
         turn_page(last, [5])
+        make_piece(1)
         make_z(4)
-        make_y(3, stores=2)
-        make_planes(0)
+        make_piece(2)
         make_z(5)
-        make_y(4)
-        make_planes(1)
-        make_y(5)
-        make_planes(2)
-        make_planes(3)
+        make_span(2, by_rows(2), 2)
+        make_planes([(0, 0), (1, 0)])
+        store_words(1, 0, 1)
+        make_span(3, by_rows(3))
+        make_planes([(2, 1)])
+        store_words(0, 0, 2)
+        make_span(4, by_blocks(4), 2)
+        make_planes([(3, 1), (3, 2)])
+        make_planes([(3, 3), (4, 2)])
+        store_words(1, 1, 4)
+        make_planes([(4, 3)], BANK // 2)
+        store_words(0, 2, 4)
         for q in range(QUADS):
             queue = nc.scalar if q % 2 == 0 else nc.sync
             queue.dma_start(out_2.bitcast(I32)[:, 4 * q : 4 * q + 4, :], y_s[32 * q : 32 * q + 8, :].bitcast(I32))

@@ -32,6 +32,7 @@ Z_PIECES = (128, 128, 256, 512, 512, 512)
 EARLY = 256
 ROWS_AT = P - 32
 SLOT = PACK * BANK * 4
+SHARE = 32
 WARM_PASSES = 2
 
 
@@ -380,9 +381,9 @@ def tile_list_ocean_band_weave_kernel(
             cols = slice(c0, c0 + width)
             nc.vector.quantize_mx(out=z_w[:, cols].bitcast(FP8X4), scales=z_s[:, cols], in_=woven[:])
 
-        spans = [(0, 0, 1), (1, 0, 1), (0, 1, 2), (1, 1, 4), (0, 2, 4)]
+        spans = [(0, 0, 1), (1, 0, 1), (0, 1, 2), (1, 1, 3), (0, 2, 4), (1, 3, 4)]
         ys = [tenant([P, PACK, BANK], F32, "big%d" % g) for g in range(GROUPS)]
-        for slot, (g, k0, k1) in zip((0, 1, 4), spans[GROUPS:]):
+        for slot, (g, k0, k1) in zip((0, 1, 3, 5), spans[GROUPS:]):
             ys.append(placed_at([P, PACK, (k1 - k0) * BANK], F32, "y%d" % slot, slot))
 
         def rows_of(g, c0, c1):
@@ -407,45 +408,43 @@ def tile_list_ocean_band_weave_kernel(
                     nc.scalar.copy(out=y[:, t0 : t0 + share, :], in_=acc[:].rearrange("p (t c) -> p t c", c=width))
                 nc.sync.dma_start(rows_of(g, c0, c0 + width), y)
 
-        def make_span(n, order, rows_a_store=1):
+        def make_rows(n, t0, t1):
             g, k0, k1 = spans[n]
-            rows = rows_of(g, k0 * BANK, k1 * BANK)
-            for t, k in order:
-                acc = bank("prod")
-                product(acc[:], g, t, k * BANK, (k + 1) * BANK)
-                nc.scalar.copy(out=ys[n][:, t, (k - k0) * BANK : (k - k0 + 1) * BANK], in_=acc[:])
-                if k == k1 - 1 and (t + 1) % rows_a_store == 0:
-                    part = slice(t + 1 - rows_a_store, t + 1)
-                    nc.sync.dma_start(rows[:, part, :], ys[n][:, part, :])
+            for t in range(t0, t1):
+                for k in range(k0, k1):
+                    acc = bank("prod")
+                    product(acc[:], g, t, k * BANK, (k + 1) * BANK)
+                    nc.scalar.copy(out=ys[n][:, t, (k - k0) * BANK : (k - k0 + 1) * BANK], in_=acc[:])
+            nc.sync.dma_start(rows_of(g, k0 * BANK, k1 * BANK)[:, t0:t1, :], ys[n][:, t0:t1, :])
 
-        def by_rows(n):
-            return [(t, k) for t in range(PACK) for k in range(spans[n][1], spans[n][2])]
+        woven = {}
 
-        def by_blocks(n):
-            return [(t, k) for k in range(spans[n][1], spans[n][2]) for t in range(PACK)]
-
-        def weave_y(n, k, by_scalar):
+        def weave_y(n, k, c0, c1, copy):
+            if (n, k) not in woven:
+                woven[n, k] = rotating([P, BANK * PACK], BF16, "rounded", RING)
             at = (k - spans[n][1]) * BANK
-            woven = rotating([P, BANK * PACK], BF16, "rounded", RING)
-            dst = woven[:].rearrange("p (c i t) -> p c t i", i=4, t=PACK)
-            src = ys[n][:, :, at : at + BANK].rearrange("p t (c i) -> p c t i", i=4)
-            cut = (BANK - by_scalar) // 4
-            nc.vector.tensor_copy(out=dst[:, :cut], in_=src[:, :cut])
-            if by_scalar > 0:
-                nc.scalar.copy(out=dst[:, cut:], in_=src[:, cut:])
-            return woven
+            copy(
+                out=woven[n, k][:, c0 * PACK : c1 * PACK].rearrange("p (c i t) -> p c t i", i=4, t=PACK),
+                in_=ys[n][:, :, at + c0 : at + c1].rearrange("p t (c i) -> p c t i", i=4),
+            )
 
-        def make_planes(chosen, by_scalar=0):
-            woven = [weave_y(n, k, by_scalar) for n, k in chosen]
-            for i, (n, k) in enumerate(chosen):
+        def make_planes(chosen, by_scalar):
+            for n, k in chosen[:-1]:
+                weave_y(n, k, 0, BANK, nc.vector.tensor_copy)
+            n, k = chosen[-1]
+            weave_y(n, k, 0, BANK - by_scalar, nc.vector.tensor_copy)
+            weave_y(n, k, BANK - by_scalar, BANK, nc.scalar.copy)
+            for n, k in chosen:
                 g = spans[n][0]
                 cols = slice(k * BANK, (k + 1) * BANK)
-                nc.vector.quantize_mx(out=y_w[:, g, cols].bitcast(FP8X4), scales=y_s[4 * g : P, cols], in_=woven[i][:])
+                nc.vector.quantize_mx(
+                    out=y_w[:, g, cols].bitcast(FP8X4), scales=y_s[4 * g : P, cols], in_=woven[n, k][:]
+                )
 
-        def store_words(g, k0, k1):
+        def store_words(g0, g1, k0, k1):
             cols = slice(k0 * BANK, k1 * BANK)
             nc.sync.dma_start(
-                out_1[g, :, cols, :].rearrange("p m t -> p (m t)").bitcast(I32), y_w[:, g, cols].bitcast(I32)
+                out_1[g0:g1, :, cols, :].rearrange("g p m t -> p g (m t)").bitcast(I32), y_w[:, g0:g1, cols].bitcast(I32)
             )
 
         turn_page(last, [0])
@@ -463,18 +462,24 @@ def tile_list_ocean_band_weave_kernel(
         make_z(4)
         make_piece(2)
         make_z(5)
-        make_span(2, by_rows(2), 2)
-        make_planes([(0, 0), (1, 0)])
-        store_words(1, 0, 1)
-        make_span(3, by_rows(3))
-        make_planes([(2, 1)])
-        store_words(0, 0, 2)
-        make_span(4, by_blocks(4), 2)
-        make_planes([(3, 1), (3, 2)])
-        make_planes([(3, 3), (4, 2)])
-        store_words(1, 1, 4)
-        make_planes([(4, 3)], BANK // 2)
-        store_words(0, 2, 4)
+        make_rows(2, 0, 2)
+        make_rows(2, 2, 4)
+        for t in range(3):
+            make_rows(3, t, t + 1)
+        make_planes([(0, 0), (1, 0)], SHARE)
+        store_words(0, 2, 0, 1)
+        make_rows(3, 3, 4)
+        make_planes([(2, 1)], SHARE)
+        store_words(0, 1, 1, 2)
+        make_rows(4, 0, 2)
+        make_planes([(3, 1), (3, 2)], SHARE)
+        store_words(1, 2, 1, 3)
+        make_rows(4, 2, 4)
+        make_rows(5, 0, 4)
+        make_planes([(4, 2), (4, 3)], SHARE)
+        store_words(0, 1, 2, 4)
+        make_planes([(5, 3)], BANK // 2)
+        store_words(1, 2, 3, 4)
         for q in range(QUADS):
             queue = nc.scalar if q % 2 == 0 else nc.sync
             queue.dma_start(out_2.bitcast(I32)[:, 4 * q : 4 * q + 4, :], y_s[32 * q : 32 * q + 8, :].bitcast(I32))

@@ -432,7 +432,8 @@ def tile_list_ocean_band_weave_kernel(
             for n, k in chosen[:-1]:
                 weave_y(n, k, 0, BANK, nc.vector.tensor_copy)
             n, k = chosen[-1]
-            weave_y(n, k, 0, BANK - by_scalar, nc.vector.tensor_copy)
+            if by_scalar < BANK:
+                weave_y(n, k, 0, BANK - by_scalar, nc.vector.tensor_copy)
             weave_y(n, k, BANK - by_scalar, BANK, nc.scalar.copy)
             for n, k in chosen:
                 g = spans[n][0]
@@ -476,9 +477,9 @@ def tile_list_ocean_band_weave_kernel(
         store_words(1, 2, 1, 3)
         make_rows(4, 2, 4)
         make_rows(5, 0, 4)
-        make_planes([(4, 2), (4, 3)], SHARE)
+        make_planes([(4, 2), (4, 3)], BANK // 2)
         store_words(0, 1, 2, 4)
-        make_planes([(5, 3)], BANK // 2)
+        make_planes([(5, 3)], BANK)
         store_words(1, 2, 3, 4)
         for q in range(QUADS):
             queue = nc.scalar if q % 2 == 0 else nc.sync

@@ -57,7 +57,7 @@ def tile_list_ocean_band_weave_kernel(
             return ring.tile(shape, dtype, name=tag, tag=tag, bufs=1, align_bytes=64)
 
         def placed_at(shape, dtype, name, slot):
-            return arena.tile(shape, dtype, name=name, offset=slot * SLOT, align_bytes=64)
+            return arena.tile(shape, dtype, name=name, offset=int(slot * SLOT), align_bytes=64)
 
         def bank(tag):
             return psum.tile([P, BANK], F32, name=tag, tag=tag, bufs=RING)
@@ -82,10 +82,9 @@ def tile_list_ocean_band_weave_kernel(
                 nc.sync.dma_start(tile[32 * q : 32 * q + 4, :].bitcast(I32), rows.bitcast(I32)[4 * q : 4 * q + 4, :])
             return tile
 
-        def round_block(src, order, first=nc.scalar.copy):
-            rounded = rotating([P, BANK * PACK], BF16, "rounded", RING)
+        def round_block(rounded, src, order):
             dst = order(rounded[:])
-            first(out=dst[:, 0], in_=src[:, 0])
+            nc.scalar.copy(out=dst[:, 0], in_=src[:, 0])
             nc.scalar.copy(out=dst[:, 1], in_=src[:, 1])
             return rounded
 
@@ -196,6 +195,41 @@ def tile_list_ocean_band_weave_kernel(
                         is_transpose=True, start=(c == 0), stop=(c == 1),
                     )
 
+        def first_slice():
+            h2 = rotating([P, PAGES, H2_SLICE], F32, "placed", RING)
+            width = per_bank * P
+            for u in range(PAGES // per_bank):
+                total = bank("turn")
+                for jj in range(tiles_per_slice):
+                    cols = slice(jj * P, (jj + 1) * P)
+                    half_sin = rotating([P, 2 * width], F32, "turned", RING)
+                    arg = bank("prod")
+                    for c in range(2):
+                        w3_cols = slice(c * H + u * width, c * H + (u + 1) * width)
+                        nc.tensor.matmul_mx(
+                            out=arg[:, c * width : (c + 1) * width],
+                            lhsT=v2_w[:, cols].bitcast(FP8X4), lhsT_scale=v2_s[:, cols],
+                            rhs=w3_w[:, w3_cols].bitcast(FP8X4), rhs_scale=w3_s[:, w3_cols], start=True, stop=True,
+                        )
+                    nc.scalar.activation(out=half_sin[:], in_=arg[:], func=ACT.Sin, scale=0.5)
+                    nc.scalar.activation(out=half_sin[:], in_=half_sin[:], func=ACT.Square)
+                    for i in range(per_bank):
+                        at = i * H2_SLICE + jj * P
+                        for c in range(2):
+                            nc.tensor.matmul(
+                                total[:, at : at + P], half_sin[:, c * width + i * P : c * width + (i + 1) * P], ident[:],
+                                is_transpose=True, start=(c == 0), stop=(c == 1),
+                            )
+                for i in range(per_bank):
+                    b = u * per_bank + i
+                    nc.scalar.activation(
+                        out=h2[:, b, :], in_=total[:, i * H2_SLICE : (i + 1) * H2_SLICE], func=ACT.Identity,
+                        scale=gain_m2[:, b : b + 1], bias=gain_p2[:, b : b + 1],
+                    )
+                    nc.vector.tensor_tensor(
+                        pages[b][:].indirect(entries(list4, 0, H2_SLICE)), h2[:, b, :], wg2_sb[:, 0:H2_SLICE], MULT
+                    )
+
         def place_slice(s):
             h2 = rotating([P, PAGES, H2_SLICE], F32, "placed", RING)
             for b in range(PAGES):
@@ -210,43 +244,46 @@ def tile_list_ocean_band_weave_kernel(
                     pages[b][:].indirect(entries(list4, j0, j1)), h2[:, b, :], wg2_sb[:, j0:j1], MULT
                 )
 
-        def quantize_w1(u, first):
+        def quantize_w1(u, room):
             rounded = round_block(
+                room,
                 w1_raw[u][:].rearrange("p a j (c i) -> p a c j i", i=4),
                 lambda ap: ap.rearrange("p (a c i j) -> p a c j i", a=PASSES, i=4, j=PACK),
-                first,
             )
             nc.vector.quantize_mx(out=w1_w[:, u, :].bitcast(FP8X4), scales=w1_s[:, u, :], in_=rounded[:])
 
-        sines_of_tile(0, 0)
-        sines_of_tile(0, 1)
-        place_slice(0)
+        first_slice()
         sines_of_tile(1, 0)
         sines_of_tile(1, 1)
-        sines_of_tile(2, 0)
         place_slice(1)
+        sines_of_tile(2, 0)
         sines_of_tile(2, 1)
         place_slice(2)
-        quantize_w1(0, nc.vector.tensor_copy)
+        quantize_w1(0, rotating([P, BANK * PACK], BF16, "rounded", RING))
         sines_of_tile(3, 0)
         sines_of_tile(3, 1)
 
         halves = [slice(h * BANK, (h + 1) * BANK) for h in range(S // BANK)]
         tiles_per_half = BANK // P
         sines = [placed_at([P, 2, S], F32, "sines%d" % i, 4 + i) for i in range(PAGES // 2)]
-        levels = [placed_at([P, tiles_per_half, H], F32, "levels%d" % h, h) for h in range(len(halves))]
+        levels = {}
 
-        def make_levels(h):
-            for i in range(tiles_per_half):
-                cols = slice(h * BANK + i * P, h * BANK + (i + 1) * P)
+        def make_levels(u, h):
+            width = H // 2
+            levels[u, h] = placed_at([P, tiles_per_half, width], F32, "levels%d%d" % (u, h), ((0.25, 0), (1, 1.5))[u][h])
+            for i0 in range(0, tiles_per_half, 2):
                 acc = bank("prod")
-                for a in range(PASSES):
-                    nc.tensor.matmul_mx(
-                        out=acc[:], lhsT=v_w[a][:, cols].bitcast(FP8X4), lhsT_scale=v_s[:, a, cols],
-                        rhs=w2_w[:, a, :].bitcast(FP4X4), rhs_scale=w2_s[:, a, :],
-                        start=(a == 0), stop=(a == PASSES - 1),
-                    )
-                nc.scalar.copy(out=levels[h][:, i, :], in_=acc[:])
+                for i in range(2):
+                    cols = slice(h * BANK + (i0 + i) * P, h * BANK + (i0 + i + 1) * P)
+                    for a in range(PASSES):
+                        nc.tensor.matmul_mx(
+                            out=acc[:, i * width : (i + 1) * width],
+                            lhsT=v_w[a][:, cols].bitcast(FP8X4), lhsT_scale=v_s[:, a, cols],
+                            rhs=w2_w[:, a, 2 * u * width : 2 * (u + 1) * width].bitcast(FP4X4),
+                            rhs_scale=w2_s[:, a, u * width : (u + 1) * width],
+                            start=(a == 0), stop=(a == PASSES - 1),
+                        )
+                nc.scalar.copy(out=levels[u, h][:, i0 : i0 + 2, :], in_=acc[:].rearrange("p (i r) -> p i r", i=2))
 
         def make_sines(b):
             for cols in halves:
@@ -267,7 +304,7 @@ def tile_list_ocean_band_weave_kernel(
             total = bank("turn")
             for i in range(tiles_per_half):
                 at = h * BANK + i * P
-                terms = (levels[h][:, i, b * P : (b + 1) * P], ln_wg[:, at : at + P])
+                terms = (levels[b // 2, h][:, i, (b % 2) * P : (b % 2 + 1) * P], ln_wg[:, at : at + P])
                 for c, term in enumerate(terms):
                     nc.tensor.matmul(
                         total[:, i * P : (i + 1) * P], term, ident[:], is_transpose=True, start=(c == 0), stop=(c == 1)
@@ -279,29 +316,32 @@ def tile_list_ocean_band_weave_kernel(
             nc.vector.tensor_tensor(pages[b][:].indirect(picks), sines[b // 2][:, b % 2, cols], amps[b][:, cols], MULT)
 
         last = PAGES - 1
-        make_levels(0)
         place_slice(3)
+        make_levels(0, 0)
         amps = [rotating([P, S], F32, "placed", RING) for b in range(last)] + [tenant([P, S], F32, "last")]
         make_sines(0)
         make_sines(1)
         for b in (0, 1):
             make_amp(b, 0)
             place(b, halves[0])
-        quantize_w1(1, nc.scalar.copy)
-        make_levels(1)
+        make_levels(0, 1)
+        quantize_w1(1, rotating([P, BANK * PACK], BF16, "rounded", RING))
         for b in (0, 1):
             make_amp(b, 1)
             place(b, halves[1])
+        make_levels(1, 0)
         make_sines(last - 1)
         make_sines(last)
         make_amp(last, 0)
         place(last, slice(0, EARLY))
         make_amp(last - 1, 0)
+        make_levels(1, 1)
         make_amp(last - 1, 1)
         place(last - 1, slice(0, S))
         make_amp(last, 1)
         w4_rounded = [
             round_block(
+                placed_at([P, BANK * PACK], BF16, "w4_rounded%d" % g, g),
                 w4_raw[g][:].rearrange("p j (h m t) -> p h m j t", h=2, t=PACK),
                 lambda ap: ap.rearrange("p (t h m j) -> p h m j t", t=PACK, h=2, j=PACK),
             )

@@ -27,7 +27,8 @@ PAGES = H // P
 PASSES = K // K_PASS
 GROUPS = N // K_PASS
 RING = 4
-H2_SLICE = 256
+PAIR = 2 * P
+H2_CUTS = (0, 256, 640, S)
 Z_PIECES = (128, 128, 256, 512, 512, 512)
 EARLY = 256
 ROWS_AT = P - 32
@@ -101,15 +102,19 @@ def tile_list_ocean_band_weave_kernel(
         tab2_s = load_plane(tab2_scales[0], "tab2_s")
         tab2_w = load_words(tab2_words[0], "big2")
         w3_s = load_plane(w3_scales[0], "w3_s")
-        w3_w = load_words(w3_words[0], "w3_w")
+        w3_w = held([P, 2 * H], U32, "w3_w")
+        w3_src = w3_words[0].rearrange("p c i -> p (c i)").bitcast(I32).rearrange("p (c u r) -> p u c r", c=2, u=2)
+        w3_dst = w3_w[:].bitcast(I32).rearrange("p (c u r) -> p u c r", c=2, u=2)
+        nc.sync.dma_start(w3_dst[:, 0], w3_src[:, 0])
         tab_w = [load_words(tab_words[a], "big%d" % a) for a in range(PASSES)]
         list4 = load_list(offs4, "list4")
         wg2_sb = held([P, S], F32, "wg2_sb")
         nc.sync.dma_start(wg2_sb[:], wg2)
-        w1_raw = [placed_at([P, PASSES, PACK, H // 2], F32, "w1_raw%d" % u, u) for u in range(2)]
+        nc.sync.dma_start(w3_dst[:, 1], w3_src[:, 1])
+        w1_raw = [placed_at([P, PASSES, PACK, PAIR], F32, "w1_raw%d" % u, u) for u in range(2)]
         for u in range(2):
             for a in range(PASSES):
-                rows = w1[a * K_PASS : (a + 1) * K_PASS, u * H // 2 : (u + 1) * H // 2]
+                rows = w1[a * K_PASS : (a + 1) * K_PASS, u * PAIR : (u + 1) * PAIR]
                 nc.sync.dma_start(w1_raw[u][:, a], rows.rearrange("(p j) c -> p j c", j=PACK))
         w2_w = held([P, PASSES, 2 * H], U8, "w2_w")
         nc.sync.dma_start(w2_w[:].bitcast(I32), w2_words.bitcast(I32).rearrange("a p c -> p a c"))
@@ -152,7 +157,7 @@ def tile_list_ocean_band_weave_kernel(
         v_rows = held([P, S], U8, "v_rows")
         nc.vector.tensor_copy(v_rows[:], tab_s[:].indirect(list1[:]))
         nc.vector.tensor_copy(v2_s[:], tab2_s[:].indirect(list2[:]))
-        for j0, j1 in ((0, H2_SLICE), (H2_SLICE, S)):
+        for j0, j1 in ((0, H2_CUTS[1]), (H2_CUTS[1], S)):
             nc.vector.tensor_copy(v2_w[:, j0:j1], tab2_w[:].indirect(entries(list2, j0, j1)))
         v_s = tenant([P, PASSES, S], U8, "big2")
         for a in range(PASSES):
@@ -168,119 +173,75 @@ def tile_list_ocean_band_weave_kernel(
 
         w1_w = held([P, 2, H], U32, "w1_w")
         w1_s = held([P, 2, H], U8, "w1_s")
-        per_bank = BANK // H2_SLICE
-        tiles_per_slice = H2_SLICE // P
-        sums = {}
 
-        def sines_of_tile(s, jj):
-            cols = slice((s * tiles_per_slice + jj) * P, (s * tiles_per_slice + jj + 1) * P)
-            half_sin = rotating([P, 2 * H], F32, "turned", RING)
-            for c in range(2):
-                arg = bank("prod")
-                nc.tensor.matmul_mx(
-                    out=arg[:], lhsT=v2_w[:, cols].bitcast(FP8X4), lhsT_scale=v2_s[:, cols],
-                    rhs=w3_w[:, c * H : (c + 1) * H].bitcast(FP8X4), rhs_scale=w3_s[:, c * H : (c + 1) * H],
-                    start=True, stop=True,
-                )
-                nc.scalar.activation(out=half_sin[:, c * H : (c + 1) * H], in_=arg[:], func=ACT.Sin, scale=0.5)
-            nc.scalar.activation(out=half_sin[:], in_=half_sin[:], func=ACT.Square)
-            if jj == 0:
-                sums[s] = [bank("turn") for b in range(PAGES // per_bank)]
-            for b in range(PAGES):
-                at = (b % per_bank) * H2_SLICE + jj * P
-                for c in range(2):
-                    nc.tensor.matmul(
-                        sums[s][b // per_bank][:, at : at + P],
-                        half_sin[:, c * H + b * P : c * H + (b + 1) * P], ident[:],
-                        is_transpose=True, start=(c == 0), stop=(c == 1),
-                    )
-
-        def first_slice():
-            h2 = rotating([P, PAGES, H2_SLICE], F32, "placed", RING)
-            width = per_bank * P
-            for u in range(PAGES // per_bank):
-                total = bank("turn")
-                for jj in range(tiles_per_slice):
-                    cols = slice(jj * P, (jj + 1) * P)
-                    half_sin = rotating([P, 2 * width], F32, "turned", RING)
+        def second_stream(u, j0, j1):
+            totals = [bank("turn") for i in range(2)]
+            for first in range(j0, j1, 2 * P):
+                starts = range(first, min(first + 2 * P, j1), P)
+                half_sin = rotating([P, len(starts), 2 * PAIR], F32, "turned", RING)
+                for n, j in enumerate(starts):
                     arg = bank("prod")
                     for c in range(2):
-                        w3_cols = slice(c * H + u * width, c * H + (u + 1) * width)
+                        w3_cols = slice(c * H + u * PAIR, c * H + (u + 1) * PAIR)
                         nc.tensor.matmul_mx(
-                            out=arg[:, c * width : (c + 1) * width],
-                            lhsT=v2_w[:, cols].bitcast(FP8X4), lhsT_scale=v2_s[:, cols],
+                            out=arg[:, c * PAIR : (c + 1) * PAIR],
+                            lhsT=v2_w[:, j : j + P].bitcast(FP8X4), lhsT_scale=v2_s[:, j : j + P],
                             rhs=w3_w[:, w3_cols].bitcast(FP8X4), rhs_scale=w3_s[:, w3_cols], start=True, stop=True,
                         )
-                    nc.scalar.activation(out=half_sin[:], in_=arg[:], func=ACT.Sin, scale=0.5)
-                    nc.scalar.activation(out=half_sin[:], in_=half_sin[:], func=ACT.Square)
-                    for i in range(per_bank):
-                        at = i * H2_SLICE + jj * P
+                    nc.scalar.activation(out=half_sin[:, n, :], in_=arg[:], func=ACT.Sin, scale=0.5)
+                nc.scalar.activation(out=half_sin[:], in_=half_sin[:], func=ACT.Square)
+                for i in range(2):
+                    for n, j in enumerate(starts):
                         for c in range(2):
                             nc.tensor.matmul(
-                                total[:, at : at + P], half_sin[:, c * width + i * P : c * width + (i + 1) * P], ident[:],
+                                totals[i][:, j - j0 : j - j0 + P],
+                                half_sin[:, n, c * PAIR + i * P : c * PAIR + (i + 1) * P], ident[:],
                                 is_transpose=True, start=(c == 0), stop=(c == 1),
                             )
-                for i in range(per_bank):
-                    b = u * per_bank + i
-                    nc.scalar.activation(
-                        out=h2[:, b, :], in_=total[:, i * H2_SLICE : (i + 1) * H2_SLICE], func=ACT.Identity,
-                        scale=gain_m2[:, b : b + 1], bias=gain_p2[:, b : b + 1],
-                    )
-                    nc.vector.tensor_tensor(
-                        pages[b][:].indirect(entries(list4, 0, H2_SLICE)), h2[:, b, :], wg2_sb[:, 0:H2_SLICE], MULT
-                    )
-
-        def place_slice(s):
-            h2 = rotating([P, PAGES, H2_SLICE], F32, "placed", RING)
-            for b in range(PAGES):
-                at = (b % per_bank) * H2_SLICE
+            h2 = rotating([P, 2, j1 - j0], F32, "placed", RING)
+            for i in range(2):
+                b = 2 * u + i
                 nc.scalar.activation(
-                    out=h2[:, b, :], in_=sums[s][b // per_bank][:, at : at + H2_SLICE], func=ACT.Identity,
+                    out=h2[:, i, :], in_=totals[i][:, 0 : j1 - j0], func=ACT.Identity,
                     scale=gain_m2[:, b : b + 1], bias=gain_p2[:, b : b + 1],
                 )
-            j0, j1 = s * H2_SLICE, (s + 1) * H2_SLICE
-            for b in range(PAGES):
                 nc.vector.tensor_tensor(
-                    pages[b][:].indirect(entries(list4, j0, j1)), h2[:, b, :], wg2_sb[:, j0:j1], MULT
+                    pages[b][:].indirect(entries(list4, j0, j1)), h2[:, i, :], wg2_sb[:, j0:j1], MULT
                 )
 
-        def quantize_w1(u, room):
+        def quantize_w1(u):
             rounded = round_block(
-                room,
+                rotating([P, BANK * PACK], BF16, "rounded", RING),
                 w1_raw[u][:].rearrange("p a j (c i) -> p a c j i", i=4),
                 lambda ap: ap.rearrange("p (a c i j) -> p a c j i", a=PASSES, i=4, j=PACK),
             )
             nc.vector.quantize_mx(out=w1_w[:, u, :].bitcast(FP8X4), scales=w1_s[:, u, :], in_=rounded[:])
 
-        first_slice()
-        sines_of_tile(1, 0)
-        sines_of_tile(1, 1)
-        place_slice(1)
-        sines_of_tile(2, 0)
-        sines_of_tile(2, 1)
-        place_slice(2)
-        quantize_w1(0, rotating([P, BANK * PACK], BF16, "rounded", RING))
-        sines_of_tile(3, 0)
-        sines_of_tile(3, 1)
+        slices = list(zip(H2_CUTS[:-1], H2_CUTS[1:]))
+        for u in range(PAGES // 2):
+            for j0, j1 in slices[:-1]:
+                second_stream(u, j0, j1)
+        quantize_w1(0)
+        for u in range(PAGES // 2):
+            second_stream(u, *slices[-1])
 
         halves = [slice(h * BANK, (h + 1) * BANK) for h in range(S // BANK)]
         tiles_per_half = BANK // P
         sines = [placed_at([P, 2, S], F32, "sines%d" % i, 4 + i) for i in range(PAGES // 2)]
         levels = {}
 
-        def make_levels(u, h):
-            width = H // 2
-            levels[u, h] = placed_at([P, tiles_per_half, width], F32, "levels%d%d" % (u, h), ((0.25, 0), (1, 1.5))[u][h])
+        def make_levels(u, h, slot):
+            levels[u, h] = placed_at([P, tiles_per_half, PAIR], F32, "levels%d%d" % (u, h), slot)
             for i0 in range(0, tiles_per_half, 2):
                 acc = bank("prod")
                 for i in range(2):
                     cols = slice(h * BANK + (i0 + i) * P, h * BANK + (i0 + i + 1) * P)
                     for a in range(PASSES):
                         nc.tensor.matmul_mx(
-                            out=acc[:, i * width : (i + 1) * width],
+                            out=acc[:, i * PAIR : (i + 1) * PAIR],
                             lhsT=v_w[a][:, cols].bitcast(FP8X4), lhsT_scale=v_s[:, a, cols],
-                            rhs=w2_w[:, a, 2 * u * width : 2 * (u + 1) * width].bitcast(FP4X4),
-                            rhs_scale=w2_s[:, a, u * width : (u + 1) * width],
+                            rhs=w2_w[:, a, 2 * u * PAIR : 2 * (u + 1) * PAIR].bitcast(FP4X4),
+                            rhs_scale=w2_s[:, a, u * PAIR : (u + 1) * PAIR],
                             start=(a == 0), stop=(a == PASSES - 1),
                         )
                 nc.scalar.copy(out=levels[u, h][:, i0 : i0 + 2, :], in_=acc[:].rearrange("p (i r) -> p i r", i=2))
@@ -289,7 +250,7 @@ def tile_list_ocean_band_weave_kernel(
             for cols in halves:
                 phase = bank("prod")
                 for a in range(PASSES):
-                    at = a * (H // 2) + (b % 2) * P
+                    at = a * PAIR + (b % 2) * P
                     nc.tensor.matmul_mx(
                         out=phase[:],
                         lhsT=w1_w[:, b // 2, at : at + P].bitcast(FP8X4), lhsT_scale=w1_s[:, b // 2, at : at + P],
@@ -316,26 +277,25 @@ def tile_list_ocean_band_weave_kernel(
             nc.vector.tensor_tensor(pages[b][:].indirect(picks), sines[b // 2][:, b % 2, cols], amps[b][:, cols], MULT)
 
         last = PAGES - 1
-        place_slice(3)
-        make_levels(0, 0)
+        make_levels(0, 0, 0.25)
         amps = [rotating([P, S], F32, "placed", RING) for b in range(last)] + [tenant([P, S], F32, "last")]
         make_sines(0)
         make_sines(1)
         for b in (0, 1):
             make_amp(b, 0)
             place(b, halves[0])
-        make_levels(0, 1)
-        quantize_w1(1, rotating([P, BANK * PACK], BF16, "rounded", RING))
+        make_levels(0, 1, 0)
+        quantize_w1(1)
         for b in (0, 1):
             make_amp(b, 1)
             place(b, halves[1])
-        make_levels(1, 0)
+        make_levels(1, 0, 1)
         make_sines(last - 1)
         make_sines(last)
         make_amp(last, 0)
         place(last, slice(0, EARLY))
         make_amp(last - 1, 0)
-        make_levels(1, 1)
+        make_levels(1, 1, 1.5)
         make_amp(last - 1, 1)
         place(last - 1, slice(0, S))
         make_amp(last, 1)
@@ -423,8 +383,10 @@ def tile_list_ocean_band_weave_kernel(
 
         spans = [(0, 0, 1), (1, 0, 1), (0, 1, 2), (1, 1, 3), (0, 2, 4), (1, 3, 4)]
         ys = [tenant([P, PACK, BANK], F32, "big%d" % g) for g in range(GROUPS)]
-        for slot, (g, k0, k1) in zip((0, 1, 3, 5), spans[GROUPS:]):
+        slot = 0
+        for g, k0, k1 in spans[GROUPS:]:
             ys.append(placed_at([P, PACK, (k1 - k0) * BANK], F32, "y%d" % slot, slot))
+            slot = slot + k1 - k0
 
         def rows_of(g, c0, c1):
             return out_0[g * K_PASS : (g + 1) * K_PASS, c0:c1].rearrange("(p t) c -> p t c", t=PACK)

from contextlib import ExitStack

import concourse.mybir as mybir
from concourse.masks import make_identity

K, K2, H, N, T, S, T2 = 1024, 512, 512, 1024, 2048, 1024, 2048
FLOPS = 2 * (2 * K * H * S + K2 * 2 * H * S + H * N * T2)

F32 = mybir.dt.float32
BF16 = mybir.dt.bfloat16
I32 = mybir.dt.int32
U32 = mybir.dt.uint32
U16 = mybir.dt.uint16
U8 = mybir.dt.uint8
FP8X4 = mybir.dt.float8_e4m3fn_x4
FP4X4 = mybir.dt.float4_e2m1fn_x4
ACT = mybir.ActivationFunctionType
MULT = mybir.AluOpType.mult

P = 128
PACK = 4
K_PASS = P * PACK
BANK = 512
QUADS = 4
PER_COLUMN = 16
PAGES = H // P
PASSES = K // K_PASS
GROUPS = N // K_PASS
RING = 4
PAIR = 2 * P
H2_CUTS = (0, 256, 640, S)
Z_PIECES = (128, 128, 256, 512, 512, 512)
EARLY = 256
ROWS_AT = P - 32
SLOT = PACK * BANK * 4
SHARE = 32
WARM_PASSES = 2


def tile_list_ocean_band_weave_kernel(
    tc, tab_words, tab_scales, tab2_words, tab2_scales, w1, w2_words, w2_scales, w3_words, w3_scales,
    w4, gain, wg1, wg2, offs, offs2, offs3, offs4, out_0, out_1, out_2,
):
    nc = tc.nc
    with ExitStack() as ctx:
        keep = ctx.enter_context(tc.tile_pool(name="keep", bufs=1))
        ring = ctx.enter_context(tc.tile_pool(name="ring", bufs=1))
        arena = ctx.enter_context(tc.tile_pool(name="arena", bufs=1))
        psum = ctx.enter_context(tc.psum_pool(name="psum", bufs=1))

        def held(shape, dtype, name):
            return keep.tile(shape, dtype, name=name, align_bytes=64)

        def rotating(shape, dtype, tag, bufs):
            return ring.tile(shape, dtype, name=tag, tag=tag, bufs=bufs, align_bytes=64)

        def tenant(shape, dtype, tag):
            return ring.tile(shape, dtype, name=tag, tag=tag, bufs=1, align_bytes=64)

        def placed_at(shape, dtype, name, slot):
            return arena.tile(shape, dtype, name=name, offset=int(slot * SLOT), align_bytes=64)

        def bank(tag):
            return psum.tile([P, BANK], F32, name=tag, tag=tag, bufs=RING)

        def entries(tile, start, stop):
            return tile[:, start // PER_COLUMN : stop // PER_COLUMN]

        def load_list(src, name):
            tile = keep.tile([P, S // PER_COLUMN], U16, name=name)
            nc.sync.dma_start(tile[:], src)
            return tile

        def load_words(src, tag):
            tile = tenant([P, src.shape[1]], U32, tag)
            nc.sync.dma_start(tile[:].bitcast(I32), src.rearrange("p c i -> p (c i)").bitcast(I32))
            return tile

        def load_plane(rows, tag):
            tile = tenant([P, rows.shape[1]], U8, tag)
            nc.gpsimd.memset(tile[:].bitcast(I32), 0)
            for q in range(QUADS):
                nc.sync.dma_start(tile[32 * q : 32 * q + 4, :].bitcast(I32), rows.bitcast(I32)[4 * q : 4 * q + 4, :])
            return tile

        def round_block(rounded, src, order):
            dst = order(rounded[:])
            nc.scalar.copy(out=dst[:, 0], in_=src[:, 0])
            nc.scalar.copy(out=dst[:, 1], in_=src[:, 1])
            return rounded

        list1 = load_list(offs, "list1")
        tab_s = held([P, T], U8, "tab_s")
        nc.sync.dma_start(tab_s[ROWS_AT:P, :].bitcast(I32), tab_scales.bitcast(I32).rearrange("a q c -> (a q) c"))
        nc.vector.memset(tab_s[0:ROWS_AT, :].bitcast(I32), 0)
        wg1_sb = held([P, S], F32, "wg1_sb")
        nc.sync.dma_start(wg1_sb[:], wg1)
        gain_rows = held([P, P], F32, "gain_rows")
        nc.gpsimd.memset(gain_rows[:], 0.0)
        nc.sync.dma_start(gain_rows[0:PAGES, :], gain.rearrange("(b p) -> b p", p=P))
        list2 = load_list(offs2, "list2")
        tab2_s = load_plane(tab2_scales[0], "tab2_s")
        tab2_w = load_words(tab2_words[0], "big2")
        w3_s = load_plane(w3_scales[0], "w3_s")
        w3_w = held([P, 2 * H], U32, "w3_w")
        w3_src = w3_words[0].rearrange("p c i -> p (c i)").bitcast(I32).rearrange("p (c u r) -> p u c r", c=2, u=2)
        w3_dst = w3_w[:].bitcast(I32).rearrange("p (c u r) -> p u c r", c=2, u=2)
        nc.sync.dma_start(w3_dst[:, 0], w3_src[:, 0])
        tab_w = [load_words(tab_words[a], "big%d" % a) for a in range(PASSES)]
        list4 = load_list(offs4, "list4")
        wg2_sb = held([P, S], F32, "wg2_sb")
        nc.sync.dma_start(wg2_sb[:], wg2)
        nc.sync.dma_start(w3_dst[:, 1], w3_src[:, 1])
        w1_raw = [placed_at([P, PASSES, PACK, PAIR], F32, "w1_raw%d" % u, u) for u in range(2)]
        for u in range(2):
            for a in range(PASSES):
                rows = w1[a * K_PASS : (a + 1) * K_PASS, u * PAIR : (u + 1) * PAIR]
                nc.sync.dma_start(w1_raw[u][:, a], rows.rearrange("(p j) c -> p j c", j=PACK))
        w2_w = held([P, PASSES, 2 * H], U8, "w2_w")
        nc.sync.dma_start(w2_w[:].bitcast(I32), w2_words.bitcast(I32).rearrange("a p c -> p a c"))
        list3 = load_list(offs3, "list3")
        w4_raw = [placed_at([P, PACK, BANK], F32, "w4_raw%d" % g, 2 + g) for g in range(GROUPS)]
        for g in range(GROUPS):
            nc.sync.dma_start(w4_raw[g][:], w4[:, g * BANK : (g + 1) * BANK].rearrange("(p j) c -> p j c", j=PACK))
        w2_s = tenant([P, PASSES, H], U8, "tab2_s")
        for q in range(QUADS):
            nc.sync.dma_start(
                w2_s[32 * q : 32 * q + 4, :, :].bitcast(I32),
                w2_scales.bitcast(I32)[:, 4 * q : 4 * q + 4, :].rearrange("a r c -> r a c"),
            )

        ident = held([P, P], F32, "ident")
        make_identity(nc, ident[:])
        gain_turned = bank("prod")
        nc.tensor.transpose(gain_turned[:, 0:P], gain_rows[:], ident[:])
        gain_at = gain_turned[:, 0:PAGES]
        gain_m2 = held([P, PAGES], F32, "gain_m2")
        gain_p2 = held([P, PAGES], F32, "gain_p2")
        gain_sign = held([P, PAGES], F32, "gain_sign")
        gain_abs = held([P, PAGES], F32, "gain_abs")
        nc.scalar.activation(out=gain_abs[:], in_=gain_at, func=ACT.Abs)
        nc.scalar.activation(out=gain_sign[:], in_=gain_at, func=ACT.Sign)
        nc.scalar.activation(out=gain_m2[:], in_=gain_at, func=ACT.Copy, scale=-2.0)
        nc.scalar.activation(out=gain_p2[:], in_=gain_at, func=ACT.Copy, scale=2.0)
        ln_gain = held([P, PAGES], F32, "ln_gain")
        nc.scalar.activation(out=ln_gain[:], in_=gain_abs[:], func=ACT.Ln, bias=2.0**-64)

        ln_wg = held([P, S], F32, "ln_wg")
        for c0 in range(0, S, BANK):
            turned = bank("turn")
            for at in range(0, BANK, P):
                nc.tensor.transpose(turned[:, at : at + P], wg1_sb[:, c0 + at : c0 + at + P], ident[:])
            nc.scalar.activation(out=ln_wg[:, c0 : c0 + BANK], in_=turned[:], func=ACT.Ln)

        v2_s = held([P, S], U8, "v2_s")
        v2_w = held([P, S], U32, "v2_w")
        v_rows = held([P, S], U8, "v_rows")
        nc.vector.tensor_copy(v_rows[:], tab_s[:].indirect(list1[:]))
        nc.vector.tensor_copy(v2_s[:], tab2_s[:].indirect(list2[:]))
        for j0, j1 in ((0, H2_CUTS[1]), (H2_CUTS[1], S)):
            nc.vector.tensor_copy(v2_w[:, j0:j1], tab2_w[:].indirect(entries(list2, j0, j1)))
        v_s = tenant([P, PASSES, S], U8, "big2")
        for a in range(PASSES):
            for q in range(QUADS):
                row = ROWS_AT + 16 * a + 4 * q
                nc.sync.dma_start(v_s[32 * q : 32 * q + 4, a, :].bitcast(I32), v_rows[row : row + 4, :].bitcast(I32))
        v_w = []
        for a in range(PASSES):
            v_w.append(held([P, S], U32, "v_w%d" % a))
            nc.vector.tensor_copy(v_w[a][:], tab_w[a][:].indirect(list1[:]))

        pages = [held([P, T2], F32, "page%d" % b) for b in range(PAGES)]

        w1_w = held([P, 2, H], U32, "w1_w")
        w1_s = held([P, 2, H], U8, "w1_s")

        def second_stream(u, j0, j1):
            totals = [bank("turn") for i in range(2)]
            for first in range(j0, j1, 2 * P):
                starts = range(first, min(first + 2 * P, j1), P)
                half_sin = rotating([P, len(starts), 2 * PAIR], F32, "turned", RING)
                for n, j in enumerate(starts):
                    arg = bank("prod")
                    for c in range(2):
                        w3_cols = slice(c * H + u * PAIR, c * H + (u + 1) * PAIR)
                        nc.tensor.matmul_mx(
                            out=arg[:, c * PAIR : (c + 1) * PAIR],
                            lhsT=v2_w[:, j : j + P].bitcast(FP8X4), lhsT_scale=v2_s[:, j : j + P],
                            rhs=w3_w[:, w3_cols].bitcast(FP8X4), rhs_scale=w3_s[:, w3_cols], start=True, stop=True,
                        )
                    nc.scalar.activation(out=half_sin[:, n, :], in_=arg[:], func=ACT.Sin, scale=0.5)
                nc.scalar.activation(out=half_sin[:], in_=half_sin[:], func=ACT.Square)
                for i in range(2):
                    for n, j in enumerate(starts):
                        for c in range(2):
                            nc.tensor.matmul(
                                totals[i][:, j - j0 : j - j0 + P],
                                half_sin[:, n, c * PAIR + i * P : c * PAIR + (i + 1) * P], ident[:],
                                is_transpose=True, start=(c == 0), stop=(c == 1),
                            )
            h2 = rotating([P, 2, j1 - j0], F32, "placed", RING)
            for i in range(2):
                b = 2 * u + i
                nc.scalar.activation(
                    out=h2[:, i, :], in_=totals[i][:, 0 : j1 - j0], func=ACT.Identity,
                    scale=gain_m2[:, b : b + 1], bias=gain_p2[:, b : b + 1],
                )
                nc.vector.tensor_tensor(
                    pages[b][:].indirect(entries(list4, j0, j1)), h2[:, i, :], wg2_sb[:, j0:j1], MULT
                )

        def quantize_w1(u):
            rounded = round_block(
                rotating([P, BANK * PACK], BF16, "rounded", RING),
                w1_raw[u][:].rearrange("p a j (c i) -> p a c j i", i=4),
                lambda ap: ap.rearrange("p (a c i j) -> p a c j i", a=PASSES, i=4, j=PACK),
            )
            nc.vector.quantize_mx(out=w1_w[:, u, :].bitcast(FP8X4), scales=w1_s[:, u, :], in_=rounded[:])

        slices = list(zip(H2_CUTS[:-1], H2_CUTS[1:]))
        for u in range(PAGES // 2):
            for j0, j1 in slices[:-1]:
                second_stream(u, j0, j1)
        quantize_w1(0)
        for u in range(PAGES // 2):
            second_stream(u, *slices[-1])

        halves = [slice(h * BANK, (h + 1) * BANK) for h in range(S // BANK)]
        tiles_per_half = BANK // P
        sines = [placed_at([P, 2, S], F32, "sines%d" % i, 4 + i) for i in range(PAGES // 2)]
        levels = {}

        def make_levels(u, h, slot):
            levels[u, h] = placed_at([P, tiles_per_half, PAIR], F32, "levels%d%d" % (u, h), slot)
            for i0 in range(0, tiles_per_half, 2):
                acc = bank("prod")
                for i in range(2):
                    cols = slice(h * BANK + (i0 + i) * P, h * BANK + (i0 + i + 1) * P)
                    for a in range(PASSES):
                        nc.tensor.matmul_mx(
                            out=acc[:, i * PAIR : (i + 1) * PAIR],
                            lhsT=v_w[a][:, cols].bitcast(FP8X4), lhsT_scale=v_s[:, a, cols],
                            rhs=w2_w[:, a, 2 * u * PAIR : 2 * (u + 1) * PAIR].bitcast(FP4X4),
                            rhs_scale=w2_s[:, a, u * PAIR : (u + 1) * PAIR],
                            start=(a == 0), stop=(a == PASSES - 1),
                        )
                nc.scalar.copy(out=levels[u, h][:, i0 : i0 + 2, :], in_=acc[:].rearrange("p (i r) -> p i r", i=2))

        def make_sines(b):
            for cols in halves:
                phase = bank("prod")
                for a in range(PASSES):
                    at = a * PAIR + (b % 2) * P
                    nc.tensor.matmul_mx(
                        out=phase[:],
                        lhsT=w1_w[:, b // 2, at : at + P].bitcast(FP8X4), lhsT_scale=w1_s[:, b // 2, at : at + P],
                        rhs=v_w[a][:, cols].bitcast(FP8X4), rhs_scale=v_s[:, a, cols],
                        start=(a == 0), stop=(a == PASSES - 1),
                    )
                nc.scalar.activation(
                    out=sines[b // 2][:, b % 2, cols], in_=phase[:], func=ACT.Sin, scale=gain_sign[:, b : b + 1]
                )

        def make_amp(b, h):
            total = bank("turn")
            for i in range(tiles_per_half):
                at = h * BANK + i * P
                terms = (levels[b // 2, h][:, i, (b % 2) * P : (b % 2 + 1) * P], ln_wg[:, at : at + P])
                for c, term in enumerate(terms):
                    nc.tensor.matmul(
                        total[:, i * P : (i + 1) * P], term, ident[:], is_transpose=True, start=(c == 0), stop=(c == 1)
                    )
            nc.scalar.activation(out=amps[b][:, halves[h]], in_=total[:], func=ACT.Exp, bias=ln_gain[:, b : b + 1])

        def place(b, cols):
            picks = entries(list3, cols.start, cols.stop)
            nc.vector.tensor_tensor(pages[b][:].indirect(picks), sines[b // 2][:, b % 2, cols], amps[b][:, cols], MULT)

        last = PAGES - 1
        make_levels(0, 0, 0.25)
        amps = [rotating([P, S], F32, "placed", RING) for b in range(last)] + [tenant([P, S], F32, "last")]
        make_sines(0)
        make_sines(1)
        for b in (0, 1):
            make_amp(b, 0)
            place(b, halves[0])
        make_levels(0, 1, 0)
        quantize_w1(1)
        for b in (0, 1):
            make_amp(b, 1)
            place(b, halves[1])
        make_levels(1, 0, 1)
        make_sines(last - 1)
        make_sines(last)
        make_amp(last, 0)
        place(last, slice(0, EARLY))
        make_amp(last - 1, 0)
        make_levels(1, 1, 1.5)
        make_amp(last - 1, 1)
        place(last - 1, slice(0, S))
        make_amp(last, 1)
        w4_rounded = [
            round_block(
                placed_at([P, BANK * PACK], BF16, "w4_rounded%d" % g, g),
                w4_raw[g][:].rearrange("p j (h m t) -> p h m j t", h=2, t=PACK),
                lambda ap: ap.rearrange("p (t h m j) -> p h m j t", t=PACK, h=2, j=PACK),
            )
            for g in range(GROUPS)
        ]
        place(last, slice(EARLY, S))

        w4_w = tenant([P, N], U32, "last")
        w4_s = held([P, N], U8, "w4_s")
        for g in range(GROUPS):
            cols = slice(g * BANK, (g + 1) * BANK)
            nc.vector.quantize_mx(out=w4_w[:, cols].bitcast(FP8X4), scales=w4_s[:, cols], in_=w4_rounded[g][:])

        pieces = [(sum(Z_PIECES[:i]), Z_PIECES[i]) for i in range(len(Z_PIECES))]
        across = []
        for i, (c0, width) in enumerate(pieces):
            shape = [P, width // P, 2, P, 2]
            if width < BANK:
                across.append(held(shape, BF16, "across%d" % i))
            else:
                across.append(rotating(shape, BF16, "turned", RING))

        def turn_page(b, chosen):
            turned = bank("turn")
            c0 = pieces[chosen[0]][0]
            for i in chosen:
                at, width = pieces[i]
                for col in range(at, at + width, P):
                    nc.tensor.transpose(turned[:, col - c0 : col - c0 + P], pages[b][:, col : col + P], ident[:])
            for i in chosen:
                at, width = pieces[i]
                nc.scalar.copy(
                    out=across[i][:, :, :, 32 * b : 32 * (b + 1), :],
                    in_=turned[:, at - c0 : at - c0 + width].rearrange("c (i q u e) -> c i u q e", q=32, u=2, e=2),
                )
            return turned

        def warm_up(emptied):
            for i in range(WARM_PASSES):
                nc.tensor.matmul_mx(
                    out=emptied[:], lhsT=v2_w[:, 0:P].bitcast(FP8X4), lhsT_scale=v2_s[:, 0:P],
                    rhs=w3_w[:, 0:H].bitcast(FP8X4), rhs_scale=w3_s[:, 0:H],
                    start=(i == 0), stop=(i == WARM_PASSES - 1),
                )

        blocks = range(T2 // BANK)
        in_block = [[i for i, (c0, width) in enumerate(pieces) if c0 // BANK == k] for k in blocks]
        for b in range(last - 1):
            for k in blocks:
                turn_page(b, in_block[k])
        turns = []
        for k in blocks:
            turns.append(turn_page(last - 1, in_block[k]))
            if k > 0:
                warm_up(turns[k - 1])

        z_w = tenant([P, T2], U32, "big2")
        z_s = held([P, T2], U8, "z_s")
        y_s = held([P, T2], U8, "y_s")
        y_w = held([P, GROUPS, T2], U32, "y_w")

        def make_z(i):
            c0, width = pieces[i]
            pairs = across[i][:].rearrange("c i u p e -> c (i u p e)").bitcast(F32)
            woven = rotating([P, width * PACK], BF16, "z_woven", 2)
            per = min(2, width // P)
            for i0 in range(0, width // P, per):
                back = bank("turn")
                for iu in range(2 * per):
                    at = (2 * i0 + iu) * P
                    nc.tensor.transpose(back[:, iu * P : (iu + 1) * P], pairs[:, at : at + P], ident[:])
                dst = woven[:].bitcast(F32)[:, 2 * i0 * P : 2 * (i0 + per) * P]
                nc.vector.tensor_copy(
                    out=dst.rearrange("p (i c u) -> p i c u", i=per, u=2),
                    in_=back[:, 0 : 2 * per * P].rearrange("p (i u c) -> p i c u", i=per, u=2),
                )
            cols = slice(c0, c0 + width)
            nc.vector.quantize_mx(out=z_w[:, cols].bitcast(FP8X4), scales=z_s[:, cols], in_=woven[:])

        spans = [(0, 0, 1), (1, 0, 1), (0, 1, 2), (1, 1, 3), (0, 2, 4), (1, 3, 4)]
        ys = [tenant([P, PACK, BANK], F32, "big%d" % g) for g in range(GROUPS)]
        slot = 0
        for g, k0, k1 in spans[GROUPS:]:
            ys.append(placed_at([P, PACK, (k1 - k0) * BANK], F32, "y%d" % slot, slot))
            slot = slot + k1 - k0

        def rows_of(g, c0, c1):
            return out_0[g * K_PASS : (g + 1) * K_PASS, c0:c1].rearrange("(p t) c -> p t c", t=PACK)

        def product(out, g, t, c0, c1):
            w4_cols = slice(g * BANK + t * P, g * BANK + (t + 1) * P)
            nc.tensor.matmul_mx(
                out=out, lhsT=w4_w[:, w4_cols].bitcast(FP8X4), lhsT_scale=w4_s[:, w4_cols],
                rhs=z_w[:, c0:c1].bitcast(FP8X4), rhs_scale=z_s[:, c0:c1], start=True, stop=True,
            )

        def make_piece(i):
            c0, width = pieces[i]
            share = BANK // width
            for g in range(GROUPS):
                y = ys[g][:, :, c0 : c0 + width]
                for t0 in range(0, PACK, share):
                    acc = bank("prod")
                    for t in range(t0, t0 + share):
                        product(acc[:, (t - t0) * width : (t - t0 + 1) * width], g, t, c0, c0 + width)
                    nc.scalar.copy(out=y[:, t0 : t0 + share, :], in_=acc[:].rearrange("p (t c) -> p t c", c=width))
                nc.sync.dma_start(rows_of(g, c0, c0 + width), y)

        def make_rows(n, t0, t1):
            g, k0, k1 = spans[n]
            for t in range(t0, t1):
                for k in range(k0, k1):
                    acc = bank("prod")
                    product(acc[:], g, t, k * BANK, (k + 1) * BANK)
                    nc.scalar.copy(out=ys[n][:, t, (k - k0) * BANK : (k - k0 + 1) * BANK], in_=acc[:])
            nc.sync.dma_start(rows_of(g, k0 * BANK, k1 * BANK)[:, t0:t1, :], ys[n][:, t0:t1, :])

        woven = {}

        def weave_y(n, k, c0, c1, copy):
            if (n, k) not in woven:
                woven[n, k] = rotating([P, BANK * PACK], BF16, "rounded", RING)
            at = (k - spans[n][1]) * BANK
            copy(
                out=woven[n, k][:, c0 * PACK : c1 * PACK].rearrange("p (c i t) -> p c t i", i=4, t=PACK),
                in_=ys[n][:, :, at + c0 : at + c1].rearrange("p t (c i) -> p c t i", i=4),
            )

        def make_planes(chosen, by_scalar):
            for n, k in chosen[:-1]:
                weave_y(n, k, 0, BANK, nc.vector.tensor_copy)
            n, k = chosen[-1]
            if by_scalar < BANK:
                weave_y(n, k, 0, BANK - by_scalar, nc.vector.tensor_copy)
            weave_y(n, k, BANK - by_scalar, BANK, nc.scalar.copy)
            for n, k in chosen:
                g = spans[n][0]
                cols = slice(k * BANK, (k + 1) * BANK)
                nc.vector.quantize_mx(
                    out=y_w[:, g, cols].bitcast(FP8X4), scales=y_s[4 * g : P, cols], in_=woven[n, k][:]
                )

        def store_words(g0, g1, k0, k1):
            cols = slice(k0 * BANK, k1 * BANK)
            nc.sync.dma_start(
                out_1[g0:g1, :, cols, :].rearrange("g p m t -> p g (m t)").bitcast(I32), y_w[:, g0:g1, cols].bitcast(I32)
            )

        turn_page(last, [0])
        warm_up(turns[-1])
        turn_page(last, [1, 2])
        make_z(0)
        turn_page(last, [3])
        make_z(1)
        make_z(2)
        turn_page(last, [4])
        make_piece(0)
        make_z(3)
        turn_page(last, [5])
        make_piece(1)
        make_z(4)
        make_piece(2)
        make_z(5)
        make_rows(2, 0, 2)
        make_rows(2, 2, 4)
        for t in range(3):
            make_rows(3, t, t + 1)
        make_planes([(0, 0), (1, 0)], SHARE)
        store_words(0, 2, 0, 1)
        make_rows(3, 3, 4)
        make_planes([(2, 1)], SHARE)
        store_words(0, 1, 1, 2)
        make_rows(4, 0, 2)
        make_planes([(3, 1), (3, 2)], SHARE)
        store_words(1, 2, 1, 3)
        make_rows(4, 2, 4)
        make_rows(5, 0, 4)
        make_planes([(4, 2), (4, 3)], BANK // 2)
        store_words(0, 1, 2, 4)
        make_planes([(5, 3)], BANK)
        store_words(1, 2, 3, 4)
        for q in range(QUADS):
            queue = nc.scalar if q % 2 == 0 else nc.sync
            queue.dma_start(out_2.bitcast(I32)[:, 4 * q : 4 * q + 4, :], y_s[32 * q : 32 * q + 8, :].bitcast(I32))
